import numpy as np, ml_dtypes
CORES = [40,41,42,43,44,45,46,47]
N = 8
import mx_ref
BF = ml_dtypes.bfloat16
def gcols(t, e):
    v = np.concatenate([t.reshape(8, 16, -1, 4), np.zeros((8, 16, 1, 4), BF)], axis=2)
    return np.ascontiguousarray(np.stack([v[g][:, e[g]] for g in range(8)])).reshape(128, -1)
def tile(rs):
    return np.stack(rs, axis=2).reshape(128, -1).astype(BF)
def pick(q, e):
    c = np.concatenate([q[0].reshape(128, -1, 4), np.zeros((128, 1, 4), np.uint8)], axis=1); s = np.concatenate([q[1], np.ones((16, 1), np.uint8)], axis=1)
    return (np.ascontiguousarray(c[:, e].reshape(128, -1)), np.ascontiguousarray(s[:, e]))
def join(*qs):
    return (np.concatenate([q[0] for q in qs], axis=1), np.concatenate([q[1] for q in qs], axis=1))
def put(q, e, v):
    c, s = q[0].reshape(128, -1, 4).copy(), q[1].copy(); c[:, e] = v[0].reshape(128, -1, 4); s[:, e] = v[1]
    return (c.reshape(128, -1), s)
def pk(c, s):
    return (np.ascontiguousarray(c), mx_ref.live(s))
def emit(q):
    return q[0], q[1]
def packed(v, rng):
    q = [mx_ref.quantize(np.ascontiguousarray(v[r])) for r in range(N)]
    return np.stack([a for a, b in q]), np.stack([mx_ref.plane(b, rng) for a, b in q])
def values_of_codes():
    e, c = np.zeros((128, 128, 4), np.float32), np.zeros((128, 2, 4), np.uint8)
    e[np.arange(128), np.arange(128), 0] = 1
    c[:127, :, 0] = np.arange(256).reshape(2, 128).T[:127]
    return mx_ref.matmul(mx_ref.quantize(e.reshape(128, 512).astype(BF)), (c.reshape(128, 8), np.full((16, 2), 127, np.uint8))).T.reshape(-1).astype(np.float64)
CODE_VALUE, SCALE_VALUE = values_of_codes(), 2.0 ** (np.arange(256) - 127.0)
def decode(q):
    return (CODE_VALUE[q[0]].reshape(16, 8, -1, 4) * SCALE_VALUE[q[1]][:, None, :, None] + 0.0).reshape(128, -1).astype(np.float32)
def f(rng, *shape):
    return mx_ref.flush((rng.standard_normal(shape, dtype=np.float32) * np.exp2(rng.integers(-2, 3, shape[:-1] + (1,)))).astype(BF))
def wide(rng, *shape, cols=0):
    v = rng.standard_normal(shape, dtype=np.float32) * np.exp2(rng.integers(-12, 13, shape)).astype(np.float32)
    if cols: v *= np.repeat(np.exp2(rng.integers(-cols, cols + 1, shape[:-2] + (1, shape[-1] // 4))) * (rng.random(shape[:-2] + (1, shape[-1] // 4)) > 0.0625), 4, axis=-1).astype(np.float32)
    return mx_ref.flush(v.astype(BF))
C, A, B, S = 512, 256, 128, 16
def top(s, k):
    return np.sort(np.argsort(-s, axis=-1, kind="stable")[..., :k], axis=-1)
def layer(w, q):
    return tile([np.maximum(mx_ref.matmul(pick(w, np.arange(128 * b, 128 * b + 128)), q), np.float32(0.0)) * np.float32(0.03125) for b in range(4)])
def gadd(t, e, v):
    a, c = t.astype(np.float32).reshape(8, 16, -1, 4), v.astype(np.float32).reshape(8, 16, -1, 4)
    for g in range(8): a[g][:, e[g]] = a[g][:, e[g]] + c[g]
    return a.reshape(128, -1).astype(BF)
def big(v, k):
    v = v.astype(np.float32) * np.float32(k)
    v[np.abs(v) < np.float32(2.0 ** -16)] = 0
    return v.astype(BF)
def numbers_of(rng):
    return {"x": big(f(rng, N, 128, 4 * C), 1), "u1": np.array(f(rng, N, 128, 512)), "u2": np.array(f(rng, N, 128, 512)), "v": np.array(f(rng, N, 128, 512))}
def weights(rng, w, z):
    a, b = packed(w, rng)
    c, e = packed(z, rng)
    return {"wc": a, "ws": b, "zc": c, "zs": e}
def unit(k):
    w = np.zeros((N, 128, 4, 128, 4), np.float32)
    i = np.arange(128)
    for b in range(4): w[:, i, b, i, b] = k
    return w.reshape(N, 128, 2048).astype(BF)
def signs(rng):
    return np.stack([rng.permutation(8) % 2 * 2.0 - 1.0 for r in range(N)])
def steps(n):
    return np.minimum((np.arange(n) + 1) // 2, n // 2 - 1)
def planted(rng, p1, p2, k):
    d = numbers_of(rng)
    s1, t, s2 = np.zeros((N, 8, C), int), np.zeros((N, 8, A), int), np.zeros((N, 8, C), int)
    np.put_along_axis(s1, p1, np.broadcast_to(steps(C), p1.shape), axis=2)
    np.put_along_axis(t, p2, np.broadcast_to(steps(A), p2.shape), axis=2)
    first = top(s1, A)
    np.put_along_axis(s2, first, t, axis=2)
    x = d["x"].astype(np.float32).reshape(N, 8, 16, C, 4)
    x[:, :, 0] = 0
    x[:, :, 0, :, 0] = 1
    np.put_along_axis(x[:, :, 0, :, 1], p1[..., -1:], np.float32(2.0 ** 13), axis=2)
    np.put_along_axis(x[:, :, 0, :, 1], p1[..., :1], np.float32(-2.0 ** 30), axis=2)
    np.put_along_axis(x[:, :, 0, :, 2], np.take_along_axis(first, p2[..., -1:], axis=2), np.float32(2.0 ** 13), axis=2)
    for s, at in ((s1, 8), (s2, 10)):
        g = ((s[..., None] >> np.arange(8)) & 1) * np.exp2(np.arange(8) - 23.0)
        x[:, :, at] = g[..., :4]
        x[:, :, at + 1] = g[..., 4:]
    x[:, :, 12] = 0
    x[:, :, 12, :, 0] = 2.0 ** -10
    x[:, :, 13:] = rng.integers(4, 8, (N, 8, 3, C, 4)) * rng.choice([-1.0, 1.0], (N, 8, 3, C, 4)) * 2.0 ** -20
    d["x"] = x.reshape(N, 128, 4 * C).astype(BF)
    for n, at, far in (("u1", 8, 1), ("u2", 10, 2)):
        u = d[n].reshape(N, 128, 128, 4)
        u[:, :, ::16] = 0
        g = (signs(rng) * k).astype(BF)
        for i in range(8):
            u[:, 16 * i, 16 * i, 0] = g[:, i]
            u[:, 16 * i, 16 * i, far] = 2.0 ** 13 * k
            u[:, 16 * i + at:16 * i + at + 2, 16 * i] = k
            u[:, 16 * i + 12, 16 * i, 0] = g[:, i]
        d[n] = u.reshape(N, 128, 512)
    return {**d, **weights(rng, unit(32), f(rng, N, 128, 2048))}
def setup_inputs(rng):
    return {**numbers_of(rng), **weights(rng, f(rng, N, 128, 2048), f(rng, N, 128, 2048))}
def setup_inputs_ties(rng):
    d = numbers_of(rng)
    e = rng.permutation(N)
    x = d["x"].reshape(N, 8, 16, C, 4)
    for r in range(N):
        k = np.zeros(C, int) if r == e[0] else rng.permutation(C) % 3
        a = x[r][:, :8, :3].copy()
        a[:, :, 2] = 0
        x[r][:, :8] = a[:, :, k]
    d["x"] = x.reshape(N, 128, 4 * C)
    w = np.array(f(rng, N, 128, 2048)).reshape(N, 8, 16, 4, 8, 16, 4)
    w[:, :, 8:, :, :, :8] = 0
    for g in range(8): w[:, np.arange(8) != g, :, :, g, :8] = 0
    for n in ("u1", "u2"):
        u = d[n].reshape(N, 8, 16, 128, 4)
        u[:, :, 8:, ::16] = 0
        for g in range(8): u[:, np.arange(8) != g, :, 16 * g] = 0
        d[n] = u.reshape(N, 128, 512)
    return {**d, **weights(rng, w.reshape(N, 128, 2048), f(rng, N, 128, 2048))}
def setup_inputs_near(rng):
    p = []
    for n, k in ((C, A), (A, B)):
        a = rng.permuted(np.tile(np.arange(n), (N, 8, 1)), axis=2)
        a[:, :, n - k - 3:n - k + 1] = np.sort(a[:, :, n - k - 3:n - k + 1], axis=2)
        p.append(a)
    return planted(rng, p[0], p[1], 1.0)
def setup_inputs_runs(rng):
    a, b = signs(rng)[:, :, None] > 0, signs(rng)[:, :, None] > 0
    return planted(rng, np.where(a, np.arange(C), np.arange(C)[::-1]), np.where(b, np.arange(A), np.arange(A)[::-1]), 2.0 ** -30)
def setup_inputs_huge(rng):
    d = numbers_of(rng)
    c = np.stack([rng.permutation(C) % 2 * 2.0 - 1.0 for r in range(N)])
    c[rng.permutation(N) < N // 2] = -1
    x = 2.0 ** 30 * (0.6 + 0.3 * rng.random((N, 128, C, 4))) * c[:, None, :, None]
    d["x"] = x.astype(np.float32).reshape(N, 128, 4 * C).astype(BF)
    for n in ("u1", "u2"):
        u = d[n].reshape(N, 128, 128, 4)
        a = 2.0 ** 30 * (1 - 0.25 * rng.random((N, 128, 8, 4))) * signs(rng)[:, None, :, None]
        u[:, :, ::16] = a.astype(np.float32).astype(BF)
        d[n] = u.reshape(N, 128, 512)
    return {**d, **weights(rng, unit(-32), big(f(rng, N, 128, 2048), 2.0 ** -6))}
def setup_inputs_spread(rng):
    d = setup_inputs(rng)
    d["x"] = big(wide(rng, N, 128, 4 * C, cols=6), 1)
    return d
def check_inputs(d):
    b = []
    for k in ("x", "u1", "u2", "v"):
        a = np.abs(d[k].astype(np.float32))
        if not (np.isfinite(a).all() and ((a == 0) | (a >= 2.0 ** -30) & (a <= 2.0 ** 30)).all()): b.append("a value of " + k)
    return b
def reference(x, u1, u2, v, wc, ws, zc, zs):
    one, two, h, down = [], [], [], []
    for r in range(N):
        p = mx_ref.matmul(mx_ref.quantize(u1[r]), mx_ref.quantize(x[r]))
        one.append(top(p[::16] + np.float32(0.0), A))
        h.append(layer(pk(wc[r], ws[r]), mx_ref.quantize(gcols(x[r], one[r]))))
        p = mx_ref.matmul(mx_ref.quantize(u2[r]), mx_ref.quantize(h[r]))
        two.append(top(p[::16] + np.float32(0.0), B))
        down.append(mx_ref.quantize(gcols(h[r], two[r])))
    done = []
    for d in range(N):
        q = join(*[pick(down[r], S * d + np.arange(S)) for r in range(N)])
        done.append(mx_ref.quantize(layer(pk(zc[d], zs[d]), q)))
    y, ol = np.zeros((N, 128, C), np.float32), np.zeros((N, 8, B), np.float32)
    oc, osc = np.zeros((N, 128, 4 * C), np.uint8), np.zeros((N, 16, C), np.uint8)
    for r in range(N):
        came = decode(join(*[pick(done[d], S * r + np.arange(S)) for d in range(N)]))
        q = mx_ref.quantize(gadd(x[r], one[r], gadd(h[r], two[r], came)))
        y[r] = mx_ref.matmul(mx_ref.quantize(v[r]), q)
        ol[r] = np.take_along_axis(one[r], two[r], axis=1)
        oc[r], osc[r] = emit(q)
    return {"y": y, "ol": ol, "oc": oc, "osc": osc}

@@ -1,0 +1,564 @@
+from concourse.bass import DstId, RemoteDMATransfer
+from concourse.mybir import dt, AluOpType as A, AxisListType, ActivationFunctionType as AF
+
+F8, U8, BF, F32, I32, U16 = "float8_e4m3fn_x4", "uint8", "bfloat16", "float32", "int32", "uint16"
+SCRATCH = {}
+for _d, _l in (
+    (BF, "tu1 512 tu2 512 tv 512 tx 2048 xf 2048 tf 1024 th 1024 txh 1024 tg 512 tt 512 thn 512 txg 512 txn 512 ones 512 te 2048 "
+         "tot 528 ps 1056 val1 512 val2 256 sj 512 sk 512 sjv 512 R1 1056 R2 544 Tr1 512 Tr2 256 Tr3 1024 gap3 528"),
+    (F32, "br 296 wt 296 iw 296 nt1 296 tbr 128 tbt 128 tb 24 seq 24 ft 16 ir 512 kr1 32 kr2 16 tr1 32 tr2 16 zero 32 c 64 gj 64 l64 128 "
+          "sc8 8 si8 8 sm 64 srow 512 ch1 32 ch2 16 gt 32 eq 32 lt 32 ges 72 es2 32 ngt 32 trn 32 y1 32 me 32 dd 32 mm 32 vi 32 "
+          "L1r 256 olr 128 ysb 512"),
+    (I32, "ip 8 ipick 8 itb 4 irep 33"),
+    (U16, "opick 8 otb 8 orep 34 off 2 offb 2 offn 2 offq 2 og 2 osc1 32 osc2 16 o1 80 o2 80 o3 32 sel1 2 sel2 2 sel3 2")):
+    _l = _l.split()
+    for _i in range(0, len(_l), 2):
+        SCRATCH[_l[_i]] = ("sbuf", [128, int(_l[_i + 1])], _d)
+for _n, _w in (("W", 512), ("Z", 512), ("x", 512), ("N", 512), ("E", 512), ("F", 256), ("H", 256), ("u1", 128), ("u2", 128), ("r1", 128), ("r2", 128), ("v", 128),
+               ("G", 128), ("L", 128), ("T", 128), ("U", 128)):
+    SCRATCH["q" + _n] = ("sbuf", [128, _w], F8)
+    SCRATCH["s" + _n] = ("sbuf", [128, _w], U8)
+for _i in range(8):
+    SCRATCH["p%d" % _i] = ("psum", [128, 512], F32)
+SEMAPHORES = ["qv", "qa", "qt", "qg", "down", "up", "sent"] + ["d%d" % i for i in range(44)]
+
+
+def rank_program(g, core, T, topo):
+    rank = T.rank_of(core)
+    if rank is None:
+        return
+    N = len(T.cores)
+    V, S, P = g.vector, g.scalar, g.tensor
+    ENG = {"v": V, "a": S, "t": P, "g": g, "s": g.sync}
+    clock = {q: {} for q in ENG}
+    total, seen, wr, rd, nd = {}, {}, {}, {}, [0]
+
+    def learn(q, deps):
+        want = {}
+        for _, s, n, _c in deps:
+            want[s] = max(want.get(s, 0), n)
+        for s in sorted(want):
+            n = want[s]
+            if clock[q].get(s, 0) >= n:
+                continue
+            if any(d[1] != s and want[d[1]] == d[2] and d[3].get(s, 0) >= n for d in deps if clock[q].get(d[1], 0) < d[2]):
+                continue
+            ENG[q].wait_ge(T.sem[s], n)
+            seen[s] = max(seen.get(s, 0), n)
+        for d in deps:
+            for s, n in list(d[3].items()) + [(d[1], d[2])]:
+                clock[q][s] = max(clock[q].get(s, 0), n)
+
+    def deps_of(r, w):
+        deps = []
+        for t in r:
+            deps += wr.get(t, [])
+        for t in w:
+            deps += wr.get(t, []) + rd.get(t, [])
+        return deps
+
+    def note(q, s, n, r, w, base):
+        e = (q, s, n, dict(base))
+        for t in w:
+            wr[t], rd[t] = [e], []
+        for t in r:
+            if t not in w:
+                rd.setdefault(t, []).append(e)
+
+    def do(q, fn, *a, r=(), w=(), **k):
+        learn(q, deps_of(r, w))
+        s = "q" + q
+        total[s] = total.get(s, 0) + 1
+        fn(*a, **k).then_inc(T.sem[s], 1)
+        note(q, s, total[s], r, w, clock[q])
+
+    def dma(q, out, in_, r=(), w=(), **k):
+        learn(q, deps_of(r, w))
+        s = "d%d" % nd[0]
+        nd[0] += 1
+        total[s] = 16
+        ENG[q].dma_start(out, in_, **k).then_inc(T.sem[s], 16)
+        note(q, s, 16, r, w, clock[q])
+
+    def mm(p, n, a, ac, b, bc, r):
+        do("t", P.matmul_mx, T[p][:, 0:n], T["q" + a][:, ac:ac + 128], T["s" + a][:, ac:ac + 128], T["q" + b][:, bc:bc + n], T["s" + b][:, bc:bc + n], True, True, r=r, w=[p])
+
+    def quant(q, c, n, t, r, w, tc=None):
+        tc = 4 * c if tc is None else tc
+        do("v", V.quantize_mx, T["q" + q][:, c:c + n], T["s" + q][:, c:c + n], t[:, tc:tc + 4 * n], r=r, w=[w])
+
+    def ts(out, in0, s1, op0, r, w, s2=None, op1=None):
+        do("v", V.tensor_scalar, out, in0, s1, s2, op0, *([] if op1 is None else [op1]), r=r, w=[w])
+
+    def tt(out, a, b, op, r, w):
+        do("v", V.tensor_tensor, out, a, b, op, r=r, w=[w])
+
+    def red(out, in_, op, r, w):
+        do("v", V.tensor_reduce, out, in_, AxisListType.X, op, r=r, w=[w])
+
+    def scan(out, a, z, r, w):
+        do("v", V.tensor_tensor_scan, out, a, z, 0.0, A.add, A.add, r=r, w=[w])
+
+    def turn(out, in_, r, w):
+        do("v", V.transpose, out, in_, r=r, w=[w])
+
+    def fill(ap, x, w):
+        do("v", V.memset, ap, x, w=[w])
+
+    def cp(out, in_, r, w):
+        do("v", V.tensor_copy, out, in_, r=r, w=[w])
+
+    def act(out, in_, f, r, w, **k):
+        do("a", S.activation, out, in_, f, r=r, w=w, **k)
+
+    def codes(v):
+        return v.bitcast(dt.uint8)
+
+    def words(v):
+        return v.bitcast(dt.uint32)
+
+    def cc(j):
+        return T.c[:, j:j + 1]
+
+    def sm(j):
+        return T.sm[:, j:j + 1]
+
+    dma("s", T.tu1[:, :], T.u1[:, :], w=["tu1"])
+    for j in range(4):
+        dma("a" if j % 2 == 0 else "s", T.tx[:, 512 * j:512 * j + 512], T.x[:, 512 * j:512 * j + 512], w=["tx%d" % j])
+    X = ["tx%d" % j for j in range(4)]
+
+    def iota(n, pattern, base, cm=0):
+        k = 1
+        for _s, m in pattern:
+            k *= m
+        f = {} if SCRATCH[n][2] == I32 else {"allow_small_or_imprecise_dtypes": True}
+        do("g", g.iota, T[n][:, 0:k], pattern, base, cm, w=[n], **f)
+
+    def select(out, src, pattern, op, base, cm, r, w):
+        do("g", g.affine_select, out, src, pattern, op, 0.0, base, cm, r=r, w=[w])
+    iota("ip", [[1, 1]], 0, 1)
+    iota("itb", [[62, 2], [0, 2]], 75)
+    iota("ipick", [[16, 8]], 0)
+    iota("seq", [[17, 17]], 0)
+    iota("kr1", [[1, 32]], 512)
+    iota("tot", [[0, 16], [1, 33]], 0)
+    select(T.ps[0:16, 0:528], T.tot[0:16, :], [[-1, 16], [0, 33]], A.is_gt, 0, 1, ["tot"], "psa")
+    select(T.ps[0:16, 528:1056], T.tot[0:16, :], [[1, 16], [0, 33]], A.is_ge, 0, -1, ["tot"], "psb")
+    iota("val1", [[1, 32], [32, 16]], -256)
+    iota("kr2", [[1, 16]], 256)
+    iota("val2", [[1, 16], [16, 16]], 0)
+    iota("irep", [[4, 33]], 0)
+    iota("ir", [[1, 512]], 0)
+    iota("ones", [[0, 512]], 1)
+    for b in range(4):
+        select(T.te[:, 512 * b:512 * b + 512], T.ones[:, :], [[1, 512]], A.is_equal, -b, -4, ["ones"], "te%d" % b)
+    LANE, ODD, LP1, CN, CP, L33, O16, EVEN, L32, M8, E8, D6, L16, LQ, LR, L4, LB, SO, SO7, L7, LQ4 = range(21)
+    B1, B2 = [], []
+
+    def lin(out, w, src, k, add):
+        act(out, cc(src), AF.Identity, ["lane", "odd"], [w], scale=k, bias=add)
+
+    def neg(k, n, s):
+        ts(T.br[:, k:k + n], T.br[:, k - s:k - s + n], 2.0 ** -s, A.mult, list(B1), "bn%d" % k)
+
+    def pos(k, n, s):
+        act(T.br[:, 146 + k:146 + k + n], T.br[:, 146 + k - s:146 + k - s + n], AF.Identity, list(B2), ["bp%d" % k], scale=2.0 ** s)
+
+    def grow(f, B, n, parts):
+        for p in parts:
+            f(*p)
+        B += [n + "%d" % p[0] for p in parts]
+    for k in range(4):
+        fill(T.br[:, 146 + k:147 + k], 2.0 ** (k - 70), "bp%d" % k)
+        B2.append("bp%d" % k)
+    for k in range(4):
+        fill(T.br[:, k:k + 1], -2.0 ** (75 - k), "bn%d" % k)
+        B1.append("bn%d" % k)
+    ts(T.ip[:, 1:2], T.ip[:, 0:1], 15, A.bitwise_and, ["ip"], "ip1")
+    ts(T.ip[:, 2:3], T.ip[:, 0:1], 4, A.logical_shift_right, ["ip"], "ip2", 1, A.bitwise_and)
+    grow(neg, B1, "bn", [(4, 4, 4), (8, 4, 8), (12, 4, 12)])
+    grow(pos, B2, "bp", [(4, 4, 4), (8, 4, 8), (12, 4, 12)])
+    cp(cc(LANE), T.ip[:, 1:2], ["ip1"], "lane")
+    cp(cc(ODD), T.ip[:, 2:3], ["ip2"], "odd")
+    cp(T.opick[:, :], T.ipick[:, :], ["ipick"], "opick")
+    grow(neg, B1, "bn", [(16, 16, 16), (32, 16, 32), (48, 16, 48)])
+    grow(pos, B2, "bp", [(16, 16, 16), (32, 16, 32), (48, 16, 48)])
+    lin(T.iw[:, 145:146], "iwc", LANE, 0.0, 2.0 ** 69)
+    lin(T.wt[:, 145:146], "wtc", LANE, 0.0, 2.0 ** -69)
+    ts(T.otb[:, 6:7], cc(LANE), 17.0, A.mult, ["lane"], "otbd", 17.0, A.add)
+    ts(T.otb[:, 7:8], cc(LANE), 17.0, A.mult, ["lane"], "otbe", 17.0, A.add)
+    grow(neg, B1, "bn", [(64, 64, 64), (128, 18, 96)])
+    grow(pos, B2, "bp", [(64, 64, 64), (128, 16, 96)])
+    ts(T.otb[:, 0:4], T.itb[:, :], cc(LANE), A.add, ["itb", "lane"], "otba")
+    ts(T.otb[:, 4:5], cc(LANE), 216.0, A.add, ["lane"], "otbb")
+    ts(T.otb[:, 5:6], cc(LANE), 216.0, A.add, ["lane"], "otbc")
+    B = B1 + B2
+    quant("u1", 0, 128, T.tu1, ["tu1"], "qu1")
+    cp(T.tbr[:, 96:128], T.br[:, 0:290].indirect(T.otb[:, 6:8]), B + ["otbd", "otbe"], "tbr3")
+    cp(words(T.qr1[:, :]), words(T.qu1[:, :]).indirect(T.opick[:, :]), ["qu1", "opick"], "qr1")
+    turn(T.tbt[:, 96:128], T.tbr[:, 96:128], ["tbr3"], "tbt3")
+    FT = ["fta", "base"]
+    NT, WT, IW = ["nta", "ntb", "ntc"], ["wta", "wtb", "wtc"], ["iwa", "iwb", "iwc"]
+
+    lin(cc(56), "cb", LANE, -0.9375, -0.9375)
+    lin(cc(CN), "cn", LANE, -0.0625, 1.9375)
+    lin(cc(CP), "cp", LANE, 0.0625, 1.0625)
+    lin(cc(LP1), "lp1", LANE, 1.0, 1.0)
+    lin(T.nt1[:, 145:146], "ntc", LANE, 2.0 ** -73, -7 * 2.0 ** -73)
+    act(T.sr1[:, :], T.su1[:, :].indirect(T.opick[:, :]), AF.Copy, ["qu1", "opick"], ["sr1"])
+    act(T.nt1[:, 0:145], T.br[:, 1:146], AF.Identity, B1 + ["cn"], ["nta"], scale=cc(CN))
+    act(T.nt1[:, 146:289], T.br[:, 146:289], AF.Identity, B2 + ["cp"], ["ntb"], scale=cc(CP))
+
+    def gap(k):
+        if k == 0:
+            act(T.wt[:, 0:145], T.br[:, 1:146], AF.Identity, B1, ["wta"], scale=-1.0)
+            act(T.wt[:, 146:289], T.br[:, 146:289], AF.Identity, B2, ["wtb"])
+            act(T.c[:, 40:44], T.br[:, 79:92:4], AF.Identity, B1, ["crow0"], scale=-1.0)
+            act(T.c[:, 44:46], T.br[:, 95:99:3], AF.Identity, B1, ["crow1"], scale=-1.0)
+        elif k == 1:
+            act(T.iw[:, 0:145], T.br[:, 142:287], AF.Identity, B, ["iwa"])
+            act(T.c[:, 48:53], T.br[:, 220:237:4], AF.Identity, B2, ["drow0"])
+            act(T.c[:, 53:54], T.br[:, 239:240], AF.Identity, B2, ["drow1"])
+        else:
+            lin(cc(E8), "e8", LANE, 0.125, -3.875)
+            lin(cc(L33), "l33", LANE, 33.0, 0.0)
+            lin(cc(L32), "l32", LANE, 32.0, 0.0)
+            lin(cc(O16), "o16", ODD, 16.0, 0.0)
+
+    quant("x", 0, 128, T.tx, ["tx0"], "qx0")
+    quant("x", 128, 128, T.tx, ["tx1"], "qx1")
+    ts(T.tb[:, 18:19], T.tbt[:, 96:97], -1.0, A.mult, ["tbt3"], "tbe")
+    ts(T.tb[:, 17:18], T.tbt[:, 96:97], 1.0, A.mult, ["tbt3"], "tbd")
+    quant("x", 256, 128, T.tx, ["tx2"], "qx2")
+    quant("x", 384, 128, T.tx, ["tx3"], "qx3")
+    cp(T.tbr[:, 0:96], T.br[:, 0:290].indirect(T.otb[:, 0:6]), B + ["otba", "otbb", "otbc"], "tbr")
+    fill(T.ft[:, 0:16], 0.0, "base")
+    ts(T.off[:, 1:2], cc(LANE), 0.0, A.is_equal, ["lane"], "off1", 8.0, A.mult)
+    turn(T.tbt[:, 0:96], T.tbr[:, 0:96], ["tbr"], "tbt")
+    fill(T.ges[:, :], 0.0, "ges0")
+    fill(T.zero[:, :], 0.0, "zero")
+    ts(T.tb[:, 0:8], T.br[:, 1:121:17], T.tbt[:, 0:1], A.mult, B1 + ["tbt"], "tba", -1.0, A.mult)
+    ts(T.tb[:, 9:17], T.br[:, 154:274:17], T.tbt[:, 64:65], A.mult, B2 + ["tbt"], "tbb")
+    ts(T.tb[:, 8:9], T.tbt[:, 32:33], 1.0, A.mult, ["tbt"], "tbc")
+    do("v", V.memset, T.ft[:, 1:2], 1.0, r=["base"], w=["fta"])
+    R = ["qr1", "sr1"]
+    mm("p2", 256, "r1", 0, "x", 0, ["qx0", "qx1"] + R)
+    mm("p3", 256, "r1", 0, "x", 256, ["qx2", "qx3"] + R)
+    for p in ("p0", "p1"):
+        mm(p, 512, "r1", 0, "x", 0, ["qx%d" % j for j in range(4)] + R)
+
+    learn("s", [d for t in X for d in wr[t]])
+    dma("s", T.tu2[:, :], T.u2[:, :], w=["tu2"])
+    dma("s", codes(T.qW[:, :]), T.wc[:, :], w=["qW"])
+    dma("s", T.sW[:, :], T.ws[:, :], w=["sW"])
+    for j in range(1, 8):
+        dma("s", T.ps[16 * j:16 * j + 16, :], T.ps[0:16, :], r=["psa", "psb"], w=["ps%d" % j])
+    PS = ["psa", "psb"] + ["ps%d" % j for j in range(1, 8)]
+
+    def rows(pb, n, ch, a, b):
+        cp(T.srow[:, a:b], T[pb][:, a:b], [pb], "srow%d" % a)
+        if b == n:
+            dma("s", ch[:, :], T.srow[0:128:16, 0:n], r=["srow0", "srow%d" % a], w=["ch"])
+
+    def base(t, h):
+        cp(T.xf[:, :].indirect(T.o1[:, 16 * t + 8 * h:16 * t + 8 * h + 8]), T.txh[:, 512 * h + t:512 * h + 512:4], ["o1_%d" % t, "txh", "xf0"], "xf")
+
+    def jobs1():
+        ts(cc(M8), cc(LANE), 8.0, A.is_lt, ["lane"], "m8")
+        yield
+        ts(T.tr1[:, :], T.kr1[:, :], cc(L32), A.add, ["kr1", "l32"], "tr1")
+        ts(cc(D6), cc(E8), cc(M8), A.mult, ["e8", "m8"], "d6", 4.0, A.add)
+        rows("p1", 512, T.ch1, 0, 256)
+        yield
+        rows("p1", 512, T.ch1, 256, 512)
+        yield
+        ts(cc(60), cc(D6), cc(LP1), A.subtract, ["d6", "lp1"], "cb5")
+        ts(cc(61), cc(D6), -8.0, A.mult, ["d6"], "cb6")
+        quant("u2", 0, 128, T.tu2, ["tu2"], "qu2")
+        yield
+        cp(words(T.qr2[:, :]), words(T.qu2[:, :]).indirect(T.opick[:, :]), ["qu2", "opick"], "qr2")
+        yield
+        ts(T.ip[:, 5:6], T.ip[:, 1:2], 1, A.bitwise_and, ["ip1"], "ip5")
+        ts(cc(SO), cc(LANE), 16.0, A.mult, ["lane", "o16"], "so16", cc(O16), A.add)
+        cp(T.sr2[:, :], T.su2[:, :].indirect(T.opick[:, :]), ["qu2", "opick"], "sr2")
+        yield
+        cp(cc(LB), T.ip[:, 5:6], ["ip5"], "lb")
+        fill(T.R1[:, 0:272], 0.0, "R1")
+        ts(T.sel1[:, 0:1], cc(LB), 240.0, A.mult, ["lb", "so16"], "sel1", cc(SO), A.add)
+        yield
+
+    def jobs2():
+        ts(cc(L16), cc(LANE), 16.0, A.mult, ["lane"], "l16")
+        ts(T.ip[:, 3:4], T.ip[:, 1:2], 2, A.logical_shift_right, ["ip1"], "ip3")
+        ts(T.ip[:, 4:5], T.ip[:, 1:2], 3, A.bitwise_and, ["ip1"], "ip4")
+        ts(T.ip[:, 6:7], T.ip[:, 1:2], 7, A.bitwise_and, ["ip1"], "ip6")
+        quant("E", 0, 128, T.te, ["te0"], "qE0", 0)
+        yield
+        quant("v", 0, 128, T.tv, ["tv"], "qvv")
+        ts(T.tr2[:, :], T.kr2[:, :], cc(L16), A.add, ["kr2", "l16"], "tr2")
+        cp(cc(LQ), T.ip[:, 3:4], ["ip3"], "lq")
+        cp(cc(LR), T.ip[:, 4:5], ["ip4"], "lr")
+        cp(cc(L7), T.ip[:, 6:7], ["ip6"], "l7")
+        yield
+        rows("p3", 256, T.ch2, 0, 256)
+        ts(cc(SO7), cc(L7), 16.0, A.mult, ["l7", "o16"], "so7", cc(O16), A.add)
+        ts(cc(LQ4), cc(ODD), -4.0, A.mult, ["odd", "lq"], "lq4", cc(LQ), A.add)
+        ts(cc(L4), cc(LR), 1024.0, A.add, ["lr"], "l4")
+        yield
+        quant("E", 128, 128, T.te, ["te1"], "qE1", 512)
+        quant("E", 256, 128, T.te, ["te2"], "qE2", 1024)
+        yield
+        quant("E", 384, 128, T.te, ["te3"], "qE3", 1536)
+        base(0, 0)
+        yield
+        ts(T.sel2[:, 0:1], cc(LB), 112.0, A.mult, ["lb", "so7"], "sel2", cc(SO7), A.add)
+        base(0, 1)
+        yield
+        fill(T.R2[:, 0:144], 0.0, "R2")
+        ts(T.orep[:, 0:33], T.irep[:, :], cc(LQ4), A.add, ["irep", "lq4"], "orep", 127.0, A.min)
+        ts(T.sel3[:, 0:1], cc(LB), 496.0, A.mult, ["lb", "so16"], "sel3a", cc(SO), A.add)
+        yield
+
+    def search(n, pa, pb, first, b, ch, jobs):
+        q = n // 16
+
+        def job():
+            for _ in jobs:
+                return
+
+        def count(t, j, tk, p, w, sign=-1.0, buf="sj"):
+            act(T[buf][:, 0:w], T[p][:, 0:w], AF.Sign, [p, tk], [buf, "sm%d" % j], scale=sign, bias=t, accum_out=sm(j))
+
+        def answer(j, n2=0):
+            if n2:
+                ts(T.off[:, 0:1], sm(14), sm(j), A.subtract, ["sm14", "sm%d" % j], "off0", float(n2), A.is_ge)
+            else:
+                ts(T.off[:, 0:1], sm(j), 0.0, A.is_le, ["sm%d" % j], "off0")
+        if first:
+            (p0, w0), (p1, w1) = first
+            count(T.tb[:, 18:19], 1, "tbe", p0, w0, 1.0, "sk")
+            count(T.tb[:, 17:18], 0, "tbd", p1, w1)
+            gap(0)
+        else:
+            fill(sm(1), 0.0, "sm1")
+            count(T.tb[:, 17:18], 0, "tbd", pa, n)
+            job()
+        ts(T.offb[:, 0:1], sm(0), sm(1), A.is_le, ["sm0", "sm1", "lp1"], "offb", cc(LP1), A.mult)
+        cp(T.l64[:, 0:16], T.tb[:, 0:17].indirect(T.offb[:, 0:1]), ["offb", "tba", "tbb", "tbc"], "b16")
+        cp(T.l64[:, 64:80], T.seq[:, 0:17].indirect(T.offb[:, 0:1]), ["offb", "seq"], "s16")
+        red(sm(3), T.l64[:, 0:16], A.max, ["b16"], "sm3")
+        red(sm(5), T.l64[:, 64:80], A.max, ["s16"], "sm5")
+        count(sm(3), 4, "sm3", pa, n)
+        if first:
+            gap(1)
+        ts(sm(2), cc(LP1), sm(5), A.add, ["lp1", "sm5"], "sm2")
+        cp(T.offq[:, 1:2], sm(5), ["sm5"], "offq1")
+        if first:
+            ts(T.iw[:, 146:289], T.br[:, 5:148], -1.0, A.mult, B, "iwb")
+            job()
+        ts(T.offq[:, 0:1], sm(4), 0.0, A.is_le, ["sm4", "sm2"], "offq0", sm(2), A.mult)
+        answer(4)
+        cp(T.l64[:, 96:128], T.nt1[:, 0:289].indirect(T.offq[:, 0:2]), ["offq0", "offq1"] + NT, "n32")
+        act(T.gj[:, 0:16], T.ft[:, 0:8].indirect(T.off[:, 0:1]), AF.Identity, ["off0"] + FT, ["gj", "sm6"], accum_out=sm(6))
+        red(sm(7), T.l64[:, 96:128], A.max, ["n32"], "sm7")
+        ts(T.offn[:, 0:1], sm(6), sm(5), A.add, ["sm6", "sm5"], "offn")
+        cp(T.l64[:, 32:48], T.iw[:, 0:289].indirect(T.offn[:, 0:1]), ["offn"] + IW, "i16")
+        cp(T.l64[:, 48:64], T.wt[:, 0:289].indirect(T.offn[:, 0:1]), ["offn"] + WT, "w16")
+        t, tk = sm(7), "sm7"
+        for r in range(6):
+            nx = "sm%d" % (16 + r)
+
+            def start():
+                ts(T.ft[:, 8:9], t, T.si8[:, r:r + 1], A.mult, [tk, "si8", ["cb", "cb5", "cb6"][max(r - 3, 0)]], "base", cc(56 if r < 4 else 56 + r), A.add)
+            if r == 0:
+                count(t, 8, tk, pa, n)
+                if first:
+                    gap(2)
+                ts(T.si8[:, 0:6], T.c[:, 48:54], T.l64[:, 32:33], A.mult, ["i16", "drow0", "drow1"], "si8")
+                if n < 512:
+                    answer(8)
+                ts(T.sc8[:, 0:6], T.c[:, 40:46], T.l64[:, 48:49], A.mult, ["w16", "crow0", "crow1"], "sc8")
+                start()
+                if n == 512:
+                    answer(8)
+            elif r < 5:
+                count(t, 8 + r, tk, pa, n - b)
+                if b:
+                    ts(T.sjv[:, 0:b], T[pb][:, n - b:n], t, A.is_ge, [pb, tk], "sjv0", 2.0, A.mult)
+                start()
+                if b:
+                    red(sm(14), T.sjv[:, 0:b], A.add, ["sjv0"], "sm14")
+                answer(8 + r, b)
+            else:
+                m = n // 2
+                ts(T.sjv[:, 0:m], T[pb][:, m:n], t, A.is_lt, [pb, tk], "sjv0")
+                act(T.sj[:, 0:m], T[pa][:, 0:m], AF.Sign, [pa, tk], ["sj"], scale=-1.0, bias=t)
+                start()
+                act(T.sk[:, 0:m], T.sj[:, 0:m], AF.Relu, ["sj"], ["sk", "sm13"], accum_out=sm(13))
+                red(sm(14), T.sjv[:, 0:m], A.add, ["sjv0"], "sm14")
+                ts(T.off[:, 0:1], sm(14), sm(13), A.add, ["sm13", "sm14"], "off0", n / 2.0, A.is_le)
+            act(T.gj[:, 0:32], T.ft[:, :].indirect(T.off[:, 0:2]), AF.Identity, ["off0", "off1", "sc8"] + FT, ["gj", nx], scale=T.sc8[:, r:r + 1], accum_out=sm(16 + r))
+            t, tk = sm(16 + r), nx
+            job()
+        for _ in jobs:
+            pass
+        tr, trk = (T.tr1, "tr1") if n == 512 else (T.tr2, "tr2")
+        ts(T.gt[:, 0:q], ch[:, :], t, A.is_gt, ["ch", tk], "gt")
+        ts(T.eq[:, 0:q], ch[:, :], t, A.is_equal, ["ch", tk], "eq")
+        scan(T.ges[:, 1:q + 1], T.gt[:, 0:q], T.zero[:, 0:q], ["gt", "zero", "ges0"], "gs")
+        scan(T.ges[:, 37:q + 37], T.eq[:, 0:q], T.zero[:, 0:q], ["eq", "zero", "ges0"], "es")
+        ts(T.lt[:, 0:q], ch[:, :], t, A.is_lt, ["ch", tk], "lt", 1024.0, A.mult)
+        ts(T.og[:, 0:2], T.ges[:, q:q + 37:36], cc(L33), A.add, ["gs", "es", "l33"], "og")
+        act(T.gj[:, 0:16], T.ps[:, 528:1056].indirect(T.og[:, 0:1]), AF.Identity, ["og"] + PS, ["gj", "sm31"], scale=-1.0, bias=n / 32.0, accum_out=sm(31))
+        act(T.gj[:, 32:64], T.ps[:, 0:528].indirect(T.og[:, 0:2]), AF.Identity, ["og"] + PS, ["gk", "sm32"], accum_out=sm(32))
+        ts(T.ngt[:, 0:q], ch[:, :], t, A.is_le, ["ch", tk], "ngt")
+        tt(T.es2[:, 0:q], T.ges[:, 36:q + 36], T.lt[:, 0:q], A.add, ["es", "ges0", "lt"], "es2")
+        tt(T.trn[:, 0:q], T.ngt[:, 0:q], tr[:, :], A.mult, ["ngt", trk], "trn")
+        ts(T.me[:, 0:q], T.es2[:, 0:q], sm(32), A.add, ["es2", "sm32", "sm31"], "me", sm(31), A.min)
+        ts(T.y1[:, 0:q], T.es2[:, 0:q], sm(32), A.add, ["es2", "sm32", "sm31"], "y1", sm(31), A.is_ge)
+        tt(T.vi[:, 0:q], T.ges[:, 0:q], T.me[:, 0:q], A.add, ["gs", "ges0", "me"], "vi")
+        tt(T.mm[:, 0:q], T.y1[:, 0:q], T.trn[:, 0:q], A.mult, ["y1", "trn"], "mm")
+        tt(T.dd[:, 0:q], T.mm[:, 0:q], T.vi[:, 0:q], A.max, ["mm", "vi"], "dd")
+        so, R, rk, val, vk, Tr = (T.osc1, T.R1, "R1", T.val1, "val1", T.Tr1) if n == 512 else (T.osc2, T.R2, "R2", T.val2, "val2", T.Tr2)
+        ts(so[:, :], T.dd[:, 0:q], cc(O16), A.add, ["dd", "o16"], "so")
+        cp(R[:, :].indirect(so[:, :]), val[:, :], ["so", vk], rk)
+        m = n // 2
+        turn(Tr[:, 0:m], R[:, 0:m], [rk], rk + "a")
+        turn(Tr[:, m:n], R[:, 16:m + 16], [rk], rk + "b")
+
+    L1T, L2T = ["R1a", "R1b", "sel1"], ["R2a", "R2b", "sel2"]
+
+    def pick(c, tr, sel, n, k, add, r, o, w):
+        ts(T[o][:, c:c + 16], T[tr][:, 0:n].indirect(T[sel][:, 0:1]), k, A.mult, r, w, add, A.add)
+
+    def gather(dst, h, t, src, rs, o, eng, w):
+        a = (T[dst][:, 512 * h + t:512 * h + 512:4], src[:, :].indirect(T[o][:, 16 * t + 8 * h:16 * t + 8 * h + 8]))
+        if eng == "a":
+            act(*a, AF.Copy, rs, [w])
+        else:
+            cp(*a, rs, w)
+
+    def relu(dst, h, b, p, eng, w):
+        o, i = T[dst][:, 512 * h + b:512 * h + 512:4], T[p][:, 0:128]
+        if eng == "a":
+            act(o, i, AF.Relu, [p], [w], scale=0.03125)
+        else:
+            ts(o, i, 0.0, A.max, [p], w, 0.03125, A.mult)
+
+    def four(n):
+        return ["%s%d" % (n, t) for t in range(4)]
+
+    search(512, "p0", "p1", (("p2", 256), ("p3", 256)), 64, T.ch1, jobs1())
+    dma("s", T.tv[:, :], T.v[:, :], w=["tv"])
+    dma("s", codes(T.qZ[:, :]), T.zc[:, :], w=["qZ"])
+    dma("s", T.sZ[:, :], T.zs[:, :], w=["sZ"])
+    dma("s", T.xf[:, :], T.x[:, :], w=["xf0"])
+    for t in range(4):
+        pick(16 * t, "Tr1", "sel1", 512, 4.0, 1024.0 + t, L1T, "o1", "o1_%d" % t)
+    FA, FB, HA, HB = four("tfa"), four("tfb"), four("tha"), four("thb")
+    for t in range(4):
+        gather("tf", 0, t, T.tx, X + ["o1_%d" % t], "o1", "avav"[t], FA[t])
+    for t in range(3):
+        gather("tf", 1, t, T.tx, X + ["o1_%d" % t], "o1", "ava"[t], FB[t])
+    quant("F", 0, 128, T.tf, FA, "qFa")
+    gather("tf", 1, 3, T.tx, X + ["o1_3"], "o1", "v", FB[3])
+    quant("F", 128, 128, T.tf, FB, "qFb")
+    PA, PB = ["p2", "p3", "p4", "p5"], ["p6", "p7", "p0", "p1"]
+    for b in range(4):
+        mm(PA[b], 128, "W", 128 * b, "F", 0, ["qW", "sW", "qFa"])
+    for b in range(4):
+        mm(PB[b], 128, "W", 128 * b, "F", 128, ["qW", "sW", "qFb"])
+    for b in range(4):
+        relu("th", 0, b, PA[b], "avav"[b], HA[b])
+    relu("th", 1, 0, PB[0], "a", HB[0])
+    relu("th", 1, 1, PB[1], "v", HB[1])
+    quant("H", 0, 128, T.th, HA, "qHa")
+    relu("th", 1, 2, PB[2], "a", HB[2])
+    relu("th", 1, 3, PB[3], "v", HB[3])
+    quant("H", 128, 128, T.th, HB, "qHb")
+    dma("s", T.txh[:, :], T.tf[:, :], r=FA + FB, w=["txh"])
+    dma("g", T.txh[:, :], T.th[:, :], r=HA + HB, w=["txh"], accum_op=A.add)
+    for p in ("p2", "p3"):
+        mm(p, 256, "r2", 0, "H", 0, ["qHa", "qHb", "qr2", "sr2"])
+    search(256, "p2", "p3", None, 0, T.ch2, jobs2())
+    for t in range(4):
+        pick(16 * t, "Tr2", "sel2", 256, 4.0, float(t), L2T, "o2", "o2_%d" % t)
+    for t in range(4):
+        gather("tg", 0, t, T.th, HA + HB + ["o2_%d" % t], "o2", "avav"[t], "tg%d" % t)
+    quant("G", 0, 128, T.tg, four("tg"), "qG")
+
+    far = [d for d in range(N) if d != rank and topo.die(T.cores[d]) != topo.die(core)]
+    near = [d for d in range(N) if d != rank and topo.die(T.cores[d]) == topo.die(core)]
+    masks = {}
+    for lst, o in ((far, 0), (near, 1)):
+        for j, d in enumerate(lst):
+            e = topo.engines(core, T.cores[d])
+            masks[d] = sum(1 << x for x in (e[4 * j + o], e[4 * j + o + 2]))
+    order = sorted(masks, key=lambda d: (d - rank) % N)
+
+    def swap(a, b, sem):
+        own = slice(16 * rank, 16 * rank + 16)
+        tok = "q" + a
+        dma("s", codes(T["q" + b][:, own]), codes(T["q" + a][:, own]), r=[tok], w=[tok + "o"])
+        dma("s", T["s" + b][:, own], T["s" + a][:, own], r=[tok], w=[tok + "p"])
+        learn("g", wr[tok])
+        for x in "qs":
+            tr = []
+            for d in order:
+                rid, pid, _ = topo.addr(T.cores[d])
+                src, dst = T[x + a][:, 16 * d:16 * d + 16], T[x + b][:, own]
+                if x == "q":
+                    src, dst = codes(src), codes(dst)
+                tr.append(RemoteDMATransfer(dst_ids=[DstId(rid=rid, pnc=pid)], dma_engine_mask=masks[d], remote_sem=T.sem[sem], src=src, dst=dst))
+            g.remote_dma_fused(tr, local_sem=T.sem.sent)
+        total[sem] = 4 * (N - 1)
+        wr[tok + "r"] = [("far", sem, total[sem], {})]
+        total["sent"] = total.get("sent", 0) + 4 * (N - 1)
+    swap("G", "L", "down")
+    pick(64, "Tr1", "sel1", 512, 1.0, 256.0, L1T, "o1", "o1c")
+    pick(64, "Tr2", "sel2", 256, 1.0, 0.0, L2T, "o2", "o2c")
+    act(T.L1r[:, :], T.ir[:, :].indirect(T.o1[:, 64:80]), AF.Identity, ["ir", "o1c"], ["L1r"])
+    act(T.olr[:, :], T.L1r[:, :].indirect(T.o2[:, 64:72]), AF.Identity, ["L1r", "o2c"], ["olr"])
+    dma("s", T.ol[:, :], T.olr[0:128:16, :], r=["olr"], w=["ol"])
+    act(T.gap3[:, :], T.olr[:, :].indirect(T.orep[:, 0:33]), AF.Identity, ["olr", "orep"], ["gap3"], bias=-256.0)
+    ts(T.sel3[:, 1:2], T.sel3[:, 0:1], 256.0, A.add, ["sel3a"], "sel3b")
+    for t, h in ((1, 0), (1, 1), (2, 0)):
+        base(t, h)
+    for b in range(4):
+        mm(PA[b], 128, "Z", 128 * b, "L", 0, ["qZ", "sZ", "qGo", "qGp", "qGr"])
+    for b in range(4):
+        relu("tt", 0, b, PA[b], "avav"[b], "tt%d" % b)
+    quant("T", 0, 128, T.tt, four("tt"), "qT")
+    swap("T", "U", "up")
+    turn(T.Tr3[:, 0:512], T.gap3[:, 0:512], ["gap3"], "Tr3a")
+    turn(T.Tr3[:, 512:1024], T.gap3[:, 16:528], ["gap3"], "Tr3b")
+    ts(T.o3[:, :], T.Tr3[:, :].indirect(T.sel3[:, 0:2]), 4.0, A.mult, ["Tr3a", "Tr3b", "sel3a", "sel3b", "l4"], "o3", cc(L4), A.add)
+    act(T.txg[:, :], T.tx[:, :].indirect(T.o3[:, :]), AF.Copy, X + ["o3"], ["txg"])
+    for t, h in ((2, 1), (3, 0), (3, 1)):
+        base(t, h)
+    for b in range(4):
+        mm(PA[b], 128, "E", 128 * b, "U", 0, ["qE%d" % b, "qTo", "qTp", "qTr"])
+    for b in range(4):
+        tt(T.thn[:, b:512:4], T[PA[b]][:, 0:128], T.tg[:, b:512:4], A.add, [PA[b], "tg%d" % b], "thn%d" % b)
+    for b in range(4):
+        tt(T.txn[:, b:512:4], T.txg[:, b:512:4], T.thn[:, b:512:4], A.add, ["txg", "thn%d" % b], "txn%d" % b)
+    cp(T.xf[:, :].indirect(T.o3[:, :]), T.txn[:, :], ["o3"] + four("txn"), "xf")
+    for h in range(4):
+        quant("N", 128 * h, 128, T.xf, ["xf"], "qN%d" % h)
+        mm(PB[h], 128, "v", 0, "N", 128 * h, ["qvv", "qN%d" % h])
+    for h in range(4):
+        o, i = T.ysb[:, 128 * h:128 * h + 128], T[PB[h]][:, 0:128]
+        if h % 2 == 0:
+            act(o, i, AF.Copy, [PB[h]], ["y%d" % h])
+        else:
+            cp(o, i, [PB[h]], "y%d" % h)
+    dma("s", T.oc[:, 0:1024], codes(T.qN[:, 0:256]), r=["qN0", "qN1"], w=["oc0"])
+    dma("s", T.oc[:, 1024:2048], codes(T.qN[:, 256:512]), r=["qN2", "qN3"], w=["oc1"])
+    for j in range(4):
+        dma("s", T.osc[4 * j:4 * j + 4, :], T.sN[32 * j:32 * j + 4, :], r=["qN%d" % h for h in range(4)], w=["osc%d" % j])
+    dma("a", T.y[:, 0:256], T.ysb[:, 0:256], r=["y0", "y1"], w=["yo0"])
+    dma("s", T.y[:, 256:512], T.ysb[:, 256:512], r=["y2", "y3"], w=["yo1"])
+    for s in sorted(total):
+        if seen.get(s, 0) < total[s]:
+            g.wait_ge(T.sem[s], total[s])

@@ -5,16 +5,16 @@ F8, U8, BF, F32, I32, U16 = "float8_e4m3fn_x4", "uint8", "bfloat16", "float32", 
 SCRATCH = {}
 for _d, _l in (
     (BF, "tu1 512 tu2 512 tv 512 tx 2048 xf 2048 tf 1024 th 1024 txh 1024 tg 512 tt 512 thn 512 txg 512 txn 512 ones 512 te 2048 "
-         "tot 528 ps 1056 val1 512 val2 256 sj 512 sk 512 sjv 512 R1 1056 R2 544 Tr1 512 Tr2 256 Tr3 1024 gap3 528"),
+         "tot 528 ps 1056 val1 512 val2 256 sj 512 sk 512 sjv 7424 R1 1056 R2 544 Tr1 512 Tr2 256 Tr3 1024 gap3 528"),
     (F32, "br 296 wt 296 iw 296 nt1 296 tbr 128 tbt 128 tb 24 seq 24 ft 16 ir 512 kr1 32 kr2 16 tr1 32 tr2 16 zero 32 c 64 gj 64 l64 128 "
-          "sc8 8 si8 8 sm 64 srow 512 ch1 32 ch2 16 gt 32 eq 32 lt 32 ges 72 es2 32 ngt 32 trn 32 y1 32 me 32 dd 32 mm 32 vi 32 "
+          "sc8 8 si8 8 sm 64 srow 1024 ch1 32 ch2 16 gt 32 eq 32 lt 32 ges 72 es2 32 ngt 32 trn 32 y1 32 me 32 dd 32 mm 32 vi 32 "
           "L1r 256 olr 128 ysb 512"),
-    (I32, "ip 8 ipick 8 itb 4 irep 33"),
-    (U16, "opick 8 otb 8 orep 34 off 2 offb 2 offn 2 offq 2 og 2 osc1 32 osc2 16 o1 80 o2 80 o3 32 sel1 2 sel2 2 sel3 2")):
+    (I32, "ip 8 ipick 24 itb 4 irep 33"),
+    (U16, "opick 24 otb 8 orep 34 off 2 offb 2 offn 2 offq 2 og 2 osc1 32 osc2 16 o1 80 o2 80 o3 32 sel1 2 sel2 2 sel3 2")):
     _l = _l.split()
     for _i in range(0, len(_l), 2):
         SCRATCH[_l[_i]] = ("sbuf", [128, int(_l[_i + 1])], _d)
-for _n, _w in (("W", 512), ("Z", 512), ("x", 512), ("N", 512), ("E", 512), ("F", 256), ("H", 256), ("u1", 128), ("u2", 128), ("r1", 128), ("r2", 128), ("v", 128),
+for _n, _w in (("W", 512), ("Z", 512), ("x", 512), ("N", 512), ("E", 512), ("F", 256), ("H", 256), ("u1", 128), ("u2", 128), ("r1", 128), ("r2", 384), ("v", 128),
                ("G", 128), ("L", 128), ("T", 128), ("U", 128)):
     SCRATCH["q" + _n] = ("sbuf", [128, _w], F8)
     SCRATCH["s" + _n] = ("sbuf", [128, _w], U8)
@@ -93,8 +93,8 @@ def rank_program(g, core, T, topo):
     def tt(out, a, b, op, r, w):
         do("v", V.tensor_tensor, out, a, b, op, r=r, w=[w])
 
-    def red(out, in_, op, r, w):
-        do("v", V.tensor_reduce, out, in_, AxisListType.X, op, r=r, w=[w])
+    def red(out, in_, op, r, w, **k):
+        do("v", V.tensor_reduce, out, in_, AxisListType.X, op, r=r, w=[w], **k)
 
     def scan(out, a, z, r, w):
         do("v", V.tensor_tensor_scan, out, a, z, 0.0, A.add, A.add, r=r, w=[w])
@@ -142,6 +142,7 @@ def rank_program(g, core, T, topo):
     iota("ipick", [[16, 8]], 0)
     iota("seq", [[17, 17]], 0)
     iota("kr1", [[1, 32]], 512)
+    do("g", g.iota, T.ipick[:, 8:24], [[16, 2], [32, 4], [0, 2]], 0, 0, w=["ipick2"])
     iota("tot", [[0, 16], [1, 33]], 0)
     select(T.ps[0:16, 0:528], T.tot[0:16, :], [[-1, 16], [0, 33]], A.is_gt, 0, 1, ["tot"], "psa")
     select(T.ps[0:16, 528:1056], T.tot[0:16, :], [[1, 16], [0, 33]], A.is_ge, 0, -1, ["tot"], "psb")
@@ -153,7 +154,7 @@ def rank_program(g, core, T, topo):
     iota("ones", [[0, 512]], 1)
     for b in range(4):
         select(T.te[:, 512 * b:512 * b + 512], T.ones[:, :], [[1, 512]], A.is_equal, -b, -4, ["ones"], "te%d" % b)
-    LANE, ODD, LP1, CN, CP, L33, O16, EVEN, L32, M8, E8, D6, L16, LQ, LR, L4, LB, SO, SO7, L7, LQ4 = range(21)
+    LANE, ODD, LP1, CN, CP, L33, O16, EVEN, L32, M8, E8, D6, L16, LQ, LR, L4, LB, SO, SO7, L7, LQ4, NODD, LM8 = range(23)
     B1, B2 = [], []
 
     def lin(out, w, src, k, add):
@@ -181,7 +182,7 @@ def rank_program(g, core, T, topo):
     grow(pos, B2, "bp", [(4, 4, 4), (8, 4, 8), (12, 4, 12)])
     cp(cc(LANE), T.ip[:, 1:2], ["ip1"], "lane")
     cp(cc(ODD), T.ip[:, 2:3], ["ip2"], "odd")
-    cp(T.opick[:, :], T.ipick[:, :], ["ipick"], "opick")
+    cp(T.opick[:, 0:8], T.ipick[:, 0:8], ["ipick"], "opick")
     grow(neg, B1, "bn", [(16, 16, 16), (32, 16, 32), (48, 16, 48)])
     grow(pos, B2, "bp", [(16, 16, 16), (32, 16, 32), (48, 16, 48)])
     lin(T.iw[:, 145:146], "iwc", LANE, 0.0, 2.0 ** 69)
@@ -196,7 +197,7 @@ def rank_program(g, core, T, topo):
     B = B1 + B2
     quant("u1", 0, 128, T.tu1, ["tu1"], "qu1")
     cp(T.tbr[:, 96:128], T.br[:, 0:290].indirect(T.otb[:, 6:8]), B + ["otbd", "otbe"], "tbr3")
-    cp(words(T.qr1[:, :]), words(T.qu1[:, :]).indirect(T.opick[:, :]), ["qu1", "opick"], "qr1")
+    cp(words(T.qr1[:, :]), words(T.qu1[:, :]).indirect(T.opick[:, 0:8]), ["qu1", "opick"], "qr1")
     turn(T.tbt[:, 96:128], T.tbr[:, 96:128], ["tbr3"], "tbt3")
     FT = ["fta", "base"]
     NT, WT, IW = ["nta", "ntb", "ntc"], ["wta", "wtb", "wtc"], ["iwa", "iwb", "iwc"]
@@ -206,7 +207,7 @@ def rank_program(g, core, T, topo):
     lin(cc(CP), "cp", LANE, 0.0625, 1.0625)
     lin(cc(LP1), "lp1", LANE, 1.0, 1.0)
     lin(T.nt1[:, 145:146], "ntc", LANE, 2.0 ** -73, -7 * 2.0 ** -73)
-    act(T.sr1[:, :], T.su1[:, :].indirect(T.opick[:, :]), AF.Copy, ["qu1", "opick"], ["sr1"])
+    act(T.sr1[:, :], T.su1[:, :].indirect(T.opick[:, 0:8]), AF.Copy, ["qu1", "opick"], ["sr1"])
     act(T.nt1[:, 0:145], T.br[:, 1:146], AF.Identity, B1 + ["cn"], ["nta"], scale=cc(CN))
     act(T.nt1[:, 146:289], T.br[:, 146:289], AF.Identity, B2 + ["cp"], ["ntb"], scale=cc(CP))
 
@@ -264,8 +265,15 @@ def rank_program(g, core, T, topo):
     def base(t, h):
         cp(T.xf[:, :].indirect(T.o1[:, 16 * t + 8 * h:16 * t + 8 * h + 8]), T.txh[:, 512 * h + t:512 * h + 512:4], ["o1_%d" % t, "txh", "xf0"], "xf")
 
+    def pick_q(k):
+        cp(words(T.qr2[:, 128 * k:128 * k + 128]), words(T.qu2[:, :]).indirect(T.opick[:, 8 * k:8 * k + 8]), ["qu2", "opick", "opick2"], "qr2%d" % k)
+
+    def pick_s(k):
+        act(T.sr2[:, 128 * k:128 * k + 128], T.su2[:, :].indirect(T.opick[:, 8 * k:8 * k + 8]), AF.Copy, ["qu2", "opick", "opick2"], ["sr2%d" % k])
+
     def jobs1():
         ts(cc(M8), cc(LANE), 8.0, A.is_lt, ["lane"], "m8")
+        cp(T.opick[:, 8:24], T.ipick[:, 8:24], ["ipick2"], "opick2")
         yield
         ts(T.tr1[:, :], T.kr1[:, :], cc(L32), A.add, ["kr1", "l32"], "tr1")
         ts(cc(D6), cc(E8), cc(M8), A.mult, ["e8", "m8"], "d6", 4.0, A.add)
@@ -277,52 +285,19 @@ def rank_program(g, core, T, topo):
         ts(cc(61), cc(D6), -8.0, A.mult, ["d6"], "cb6")
         quant("u2", 0, 128, T.tu2, ["tu2"], "qu2")
         yield
-        cp(words(T.qr2[:, :]), words(T.qu2[:, :]).indirect(T.opick[:, :]), ["qu2", "opick"], "qr2")
+        pick_q(0)
+        pick_q(1)
         yield
         ts(T.ip[:, 5:6], T.ip[:, 1:2], 1, A.bitwise_and, ["ip1"], "ip5")
         ts(cc(SO), cc(LANE), 16.0, A.mult, ["lane", "o16"], "so16", cc(O16), A.add)
-        cp(T.sr2[:, :], T.su2[:, :].indirect(T.opick[:, :]), ["qu2", "opick"], "sr2")
+        pick_q(2)
         yield
         cp(cc(LB), T.ip[:, 5:6], ["ip5"], "lb")
         fill(T.R1[:, 0:272], 0.0, "R1")
         ts(T.sel1[:, 0:1], cc(LB), 240.0, A.mult, ["lb", "so16"], "sel1", cc(SO), A.add)
         yield
 
-    def jobs2():
-        ts(cc(L16), cc(LANE), 16.0, A.mult, ["lane"], "l16")
-        ts(T.ip[:, 3:4], T.ip[:, 1:2], 2, A.logical_shift_right, ["ip1"], "ip3")
-        ts(T.ip[:, 4:5], T.ip[:, 1:2], 3, A.bitwise_and, ["ip1"], "ip4")
-        ts(T.ip[:, 6:7], T.ip[:, 1:2], 7, A.bitwise_and, ["ip1"], "ip6")
-        quant("E", 0, 128, T.te, ["te0"], "qE0", 0)
-        yield
-        quant("v", 0, 128, T.tv, ["tv"], "qvv")
-        ts(T.tr2[:, :], T.kr2[:, :], cc(L16), A.add, ["kr2", "l16"], "tr2")
-        cp(cc(LQ), T.ip[:, 3:4], ["ip3"], "lq")
-        cp(cc(LR), T.ip[:, 4:5], ["ip4"], "lr")
-        cp(cc(L7), T.ip[:, 6:7], ["ip6"], "l7")
-        yield
-        rows("p3", 256, T.ch2, 0, 256)
-        ts(cc(SO7), cc(L7), 16.0, A.mult, ["l7", "o16"], "so7", cc(O16), A.add)
-        ts(cc(LQ4), cc(ODD), -4.0, A.mult, ["odd", "lq"], "lq4", cc(LQ), A.add)
-        ts(cc(L4), cc(LR), 1024.0, A.add, ["lr"], "l4")
-        yield
-        quant("E", 128, 128, T.te, ["te1"], "qE1", 512)
-        quant("E", 256, 128, T.te, ["te2"], "qE2", 1024)
-        yield
-        quant("E", 384, 128, T.te, ["te3"], "qE3", 1536)
-        base(0, 0)
-        yield
-        ts(T.sel2[:, 0:1], cc(LB), 112.0, A.mult, ["lb", "so7"], "sel2", cc(SO7), A.add)
-        base(0, 1)
-        yield
-        fill(T.R2[:, 0:144], 0.0, "R2")
-        ts(T.orep[:, 0:33], T.irep[:, :], cc(LQ4), A.add, ["irep", "lq4"], "orep", 127.0, A.min)
-        ts(T.sel3[:, 0:1], cc(LB), 496.0, A.mult, ["lb", "so16"], "sel3a", cc(SO), A.add)
-        yield
-
-    def search(n, pa, pb, first, b, ch, jobs):
-        q = n // 16
-
+    def search(n, pa, pb, first, b, jobs):
         def job():
             for _ in jobs:
                 return
@@ -335,28 +310,21 @@ def rank_program(g, core, T, topo):
                 ts(T.off[:, 0:1], sm(14), sm(j), A.subtract, ["sm14", "sm%d" % j], "off0", float(n2), A.is_ge)
             else:
                 ts(T.off[:, 0:1], sm(j), 0.0, A.is_le, ["sm%d" % j], "off0")
-        if first:
-            (p0, w0), (p1, w1) = first
-            count(T.tb[:, 18:19], 1, "tbe", p0, w0, 1.0, "sk")
-            count(T.tb[:, 17:18], 0, "tbd", p1, w1)
-            gap(0)
-        else:
-            fill(sm(1), 0.0, "sm1")
-            count(T.tb[:, 17:18], 0, "tbd", pa, n)
-            job()
+        (p0, w0), (p1, w1) = first
+        count(T.tb[:, 18:19], 1, "tbe", p0, w0, 1.0, "sk")
+        count(T.tb[:, 17:18], 0, "tbd", p1, w1)
+        gap(0)
         ts(T.offb[:, 0:1], sm(0), sm(1), A.is_le, ["sm0", "sm1", "lp1"], "offb", cc(LP1), A.mult)
         cp(T.l64[:, 0:16], T.tb[:, 0:17].indirect(T.offb[:, 0:1]), ["offb", "tba", "tbb", "tbc"], "b16")
         cp(T.l64[:, 64:80], T.seq[:, 0:17].indirect(T.offb[:, 0:1]), ["offb", "seq"], "s16")
         red(sm(3), T.l64[:, 0:16], A.max, ["b16"], "sm3")
         red(sm(5), T.l64[:, 64:80], A.max, ["s16"], "sm5")
         count(sm(3), 4, "sm3", pa, n)
-        if first:
-            gap(1)
+        gap(1)
         ts(sm(2), cc(LP1), sm(5), A.add, ["lp1", "sm5"], "sm2")
         cp(T.offq[:, 1:2], sm(5), ["sm5"], "offq1")
-        if first:
-            ts(T.iw[:, 146:289], T.br[:, 5:148], -1.0, A.mult, B, "iwb")
-            job()
+        ts(T.iw[:, 146:289], T.br[:, 5:148], -1.0, A.mult, B, "iwb")
+        job()
         ts(T.offq[:, 0:1], sm(4), 0.0, A.is_le, ["sm4", "sm2"], "offq0", sm(2), A.mult)
         answer(4)
         cp(T.l64[:, 96:128], T.nt1[:, 0:289].indirect(T.offq[:, 0:2]), ["offq0", "offq1"] + NT, "n32")
@@ -373,22 +341,16 @@ def rank_program(g, core, T, topo):
                 ts(T.ft[:, 8:9], t, T.si8[:, r:r + 1], A.mult, [tk, "si8", ["cb", "cb5", "cb6"][max(r - 3, 0)]], "base", cc(56 if r < 4 else 56 + r), A.add)
             if r == 0:
                 count(t, 8, tk, pa, n)
-                if first:
-                    gap(2)
+                gap(2)
                 ts(T.si8[:, 0:6], T.c[:, 48:54], T.l64[:, 32:33], A.mult, ["i16", "drow0", "drow1"], "si8")
-                if n < 512:
-                    answer(8)
                 ts(T.sc8[:, 0:6], T.c[:, 40:46], T.l64[:, 48:49], A.mult, ["w16", "crow0", "crow1"], "sc8")
                 start()
-                if n == 512:
-                    answer(8)
+                answer(8)
             elif r < 5:
                 count(t, 8 + r, tk, pa, n - b)
-                if b:
-                    ts(T.sjv[:, 0:b], T[pb][:, n - b:n], t, A.is_ge, [pb, tk], "sjv0", 2.0, A.mult)
+                ts(T.sjv[:, 0:b], T[pb][:, n - b:n], t, A.is_ge, [pb, tk], "sjv0", 2.0, A.mult)
                 start()
-                if b:
-                    red(sm(14), T.sjv[:, 0:b], A.add, ["sjv0"], "sm14")
+                red(sm(14), T.sjv[:, 0:b], A.add, ["sjv0"], "sm14")
                 answer(8 + r, b)
             else:
                 m = n // 2
@@ -403,16 +365,66 @@ def rank_program(g, core, T, topo):
             job()
         for _ in jobs:
             pass
+        return t, tk
+
+    def ranks(pm, pe, po, ps_):
+        NV = 10
+        w = T.srow
+        raw, mk, gm, gin, gout, bm, bmt = (w[:, 768:784], w[:, 784:800], w[:, 800:816], 832, 864, 896, 928)
+
+        def bound(i):
+            k = 512 + 32 * (i % 8) + 16 * (i // 8)
+            return w[:, k:k + 1]
+
+        def flags(i, a=0, b=256):
+            return T.sjv[:, 512 + 256 * i + a:512 + 256 * i + b]
+
+        def total_v(i):
+            scan(T.sjv[:, 4608 + 128 * i:4736 + 128 * i], flags(i, 0, 128), flags(i, 128, 256), ["fl%d" % i], "sc%d" % i)
+
+        def total_a(i):
+            k = 5888 + 256 * (i - NV)
+            act(T.sjv[:, k:k + 256], flags(i), AF.Relu, ["fl%d" % i], ["sc%d" % i], scale=-1.0, accum_out=w[:, 768 + i:769 + i])
+        turn(w[:, 512:768], T[pm][:, 0:256], [pm], "trs")
+        for i in range(NV, 16):
+            act(flags(i), T[ps_][:, 0:256], AF.Sign, [ps_, "trs"], ["fl%d" % i], scale=-1.0, bias=bound(i))
+            if i > NV:
+                total_a(i - 1)
+        total_a(15)
+        for i in range(NV):
+            p = pe if i < 8 else po
+            ts(flags(i), T[p][:, 0:256], bound(i), A.is_gt, [p, "trs"], "fl%d" % i)
+            if i:
+                total_v(i - 1)
+        total_v(NV - 1)
+        cp(w[:, 768:768 + NV], T.sjv[:, 4608 + 127:4608 + 128 * NV:128], ["sc%d" % i for i in range(NV)], "rawv")
+        RAW = ["rawv"] + ["sc%d" % i for i in range(NV, 16)]
+        act(w[:, gin:gin + 32:2], raw, AF.Identity, RAW + ["even"], ["gin0"], scale=cc(EVEN))
+        act(w[:, gin + 1:gin + 32:2], raw, AF.Identity, RAW + ["nodd"], ["gin1"], scale=cc(NODD))
+        ts(mk, raw, 128.0, A.is_ge, RAW, "mk", -1000.0, A.mult)
+        tt(gm, raw, mk, A.add, RAW + ["mk"], "gm")
+        red(sm(40), w[:, 800:808], A.max, ["gm"], "sm40")
+        red(sm(41), w[:, 808:816], A.max, ["gm"], "sm41")
+        turn(w[:, gout:gout + 32], w[:, gin:gin + 32], ["gin0", "gin1"], "gout")
+        ts(w[:, bm:bm + 16], T.zero[:, 0:16], sm(40), A.add, ["zero", "sm40"], "bm0")
+        ts(w[:, bm + 16:bm + 32], T.zero[:, 0:16], sm(41), A.add, ["zero", "sm41"], "bm1")
+        tt(T.ch2[:, :], w[:, gout:gout + 16], w[:, gout + 16:gout + 32], A.add, ["gout"], "ch2")
+        turn(w[:, bmt:bmt + 32], w[:, bm:bm + 32], ["bm0", "bm1"], "bmt")
+        red(sm(42), w[:, bmt:bmt + 32], A.max, ["bmt"], "sm42", negate=True)
+        return sm(42), "sm42"
+
+    def listed(n, ch, ck, t, tk):
+        q = n // 16
         tr, trk = (T.tr1, "tr1") if n == 512 else (T.tr2, "tr2")
-        ts(T.gt[:, 0:q], ch[:, :], t, A.is_gt, ["ch", tk], "gt")
-        ts(T.eq[:, 0:q], ch[:, :], t, A.is_equal, ["ch", tk], "eq")
+        ts(T.gt[:, 0:q], ch[:, :], t, A.is_gt, [ck, tk], "gt")
+        ts(T.eq[:, 0:q], ch[:, :], t, A.is_equal, [ck, tk], "eq")
         scan(T.ges[:, 1:q + 1], T.gt[:, 0:q], T.zero[:, 0:q], ["gt", "zero", "ges0"], "gs")
         scan(T.ges[:, 37:q + 37], T.eq[:, 0:q], T.zero[:, 0:q], ["eq", "zero", "ges0"], "es")
-        ts(T.lt[:, 0:q], ch[:, :], t, A.is_lt, ["ch", tk], "lt", 1024.0, A.mult)
+        ts(T.lt[:, 0:q], ch[:, :], t, A.is_lt, [ck, tk], "lt", 1024.0, A.mult)
         ts(T.og[:, 0:2], T.ges[:, q:q + 37:36], cc(L33), A.add, ["gs", "es", "l33"], "og")
         act(T.gj[:, 0:16], T.ps[:, 528:1056].indirect(T.og[:, 0:1]), AF.Identity, ["og"] + PS, ["gj", "sm31"], scale=-1.0, bias=n / 32.0, accum_out=sm(31))
         act(T.gj[:, 32:64], T.ps[:, 0:528].indirect(T.og[:, 0:2]), AF.Identity, ["og"] + PS, ["gk", "sm32"], accum_out=sm(32))
-        ts(T.ngt[:, 0:q], ch[:, :], t, A.is_le, ["ch", tk], "ngt")
+        ts(T.ngt[:, 0:q], ch[:, :], t, A.is_le, [ck, tk], "ngt")
         tt(T.es2[:, 0:q], T.ges[:, 36:q + 36], T.lt[:, 0:q], A.add, ["es", "ges0", "lt"], "es2")
         tt(T.trn[:, 0:q], T.ngt[:, 0:q], tr[:, :], A.mult, ["ngt", trk], "trn")
         ts(T.me[:, 0:q], T.es2[:, 0:q], sm(32), A.add, ["es2", "sm32", "sm31"], "me", sm(31), A.min)
@@ -449,7 +461,18 @@ def rank_program(g, core, T, topo):
     def four(n):
         return ["%s%d" % (n, t) for t in range(4)]
 
-    search(512, "p0", "p1", (("p2", 256), ("p3", 256)), 64, T.ch1, jobs1())
+    t1, k1 = search(512, "p0", "p1", (("p2", 256), ("p3", 256)), 64, jobs1())
+    pick_s(0)
+    listed(512, T.ch1, "ch", t1, k1)
+    pick_s(1)
+    pick_s(2)
+    lin(cc(L16), "l16", LANE, 16.0, 0.0)
+    lin(cc(LM8), "lm8", LANE, 1.0, -8.0)
+    lin(cc(EVEN), "even", ODD, 1.0, -1.0)
+    lin(cc(NODD), "nodd", ODD, -1.0, 0.0)
+    act(cc(L7), cc(M8), AF.Identity, ["m8", "lm8"], ["l7"], scale=8.0, bias=cc(LM8))
+    act(T.tr2[:, :], T.kr2[:, :], AF.Identity, ["kr2", "l16"], ["tr2"], bias=cc(L16))
+    act(cc(SO7), cc(L7), AF.Identity, ["l7", "o16"], ["so7"], scale=16.0, bias=cc(O16))
     dma("s", T.tv[:, :], T.v[:, :], w=["tv"])
     dma("s", codes(T.qZ[:, :]), T.zc[:, :], w=["qZ"])
     dma("s", T.sZ[:, :], T.zs[:, :], w=["sZ"])
@@ -479,9 +502,15 @@ def rank_program(g, core, T, topo):
     quant("H", 128, 128, T.th, HB, "qHb")
     dma("s", T.txh[:, :], T.tf[:, :], r=FA + FB, w=["txh"])
     dma("g", T.txh[:, :], T.th[:, :], r=HA + HB, w=["txh"], accum_op=A.add)
-    for p in ("p2", "p3"):
-        mm(p, 256, "r2", 0, "H", 0, ["qHa", "qHb", "qr2", "sr2"])
-    search(256, "p2", "p3", None, 0, T.ch2, jobs2())
+    for p, k in (("p2", 0), ("p4", 1), ("p3", 2), ("p5", 2)):
+        mm(p, 256, "r2", 128 * k, "H", 0, ["qHa", "qHb", "qr2%d" % k, "sr2%d" % k])
+    ts(T.sel2[:, 0:1], cc(LB), 112.0, A.mult, ["lb", "so7"], "sel2", cc(SO7), A.add)
+    fill(T.R2[:, 0:144], 0.0, "R2")
+    ts(T.ip[:, 3:4], T.ip[:, 1:2], 2, A.logical_shift_right, ["ip1"], "ip3")
+    ts(T.ip[:, 4:5], T.ip[:, 1:2], 3, A.bitwise_and, ["ip1"], "ip4")
+    quant("E", 0, 128, T.te, ["te0"], "qE0", 0)
+    t2, k2 = ranks("p2", "p4", "p5", "p3")
+    listed(256, T.ch2, "ch2", t2, k2)
     for t in range(4):
         pick(16 * t, "Tr2", "sel2", 256, 4.0, float(t), L2T, "o2", "o2_%d" % t)
     for t in range(4):
@@ -516,15 +545,26 @@ def rank_program(g, core, T, topo):
         wr[tok + "r"] = [("far", sem, total[sem], {})]
         total["sent"] = total.get("sent", 0) + 4 * (N - 1)
     swap("G", "L", "down")
+    cp(cc(LQ), T.ip[:, 3:4], ["ip3"], "lq")
+    cp(cc(LR), T.ip[:, 4:5], ["ip4"], "lr")
     pick(64, "Tr1", "sel1", 512, 1.0, 256.0, L1T, "o1", "o1c")
     pick(64, "Tr2", "sel2", 256, 1.0, 0.0, L2T, "o2", "o2c")
+    ts(cc(LQ4), cc(ODD), -4.0, A.mult, ["odd", "lq"], "lq4", cc(LQ), A.add)
+    ts(cc(L4), cc(LR), 1024.0, A.add, ["lr"], "l4")
+    ts(T.sel3[:, 0:1], cc(LB), 496.0, A.mult, ["lb", "so16"], "sel3a", cc(SO), A.add)
+    ts(T.orep[:, 0:33], T.irep[:, :], cc(LQ4), A.add, ["irep", "lq4"], "orep", 127.0, A.min)
     act(T.L1r[:, :], T.ir[:, :].indirect(T.o1[:, 64:80]), AF.Identity, ["ir", "o1c"], ["L1r"])
     act(T.olr[:, :], T.L1r[:, :].indirect(T.o2[:, 64:72]), AF.Identity, ["L1r", "o2c"], ["olr"])
     dma("s", T.ol[:, :], T.olr[0:128:16, :], r=["olr"], w=["ol"])
     act(T.gap3[:, :], T.olr[:, :].indirect(T.orep[:, 0:33]), AF.Identity, ["olr", "orep"], ["gap3"], bias=-256.0)
     ts(T.sel3[:, 1:2], T.sel3[:, 0:1], 256.0, A.add, ["sel3a"], "sel3b")
-    for t, h in ((1, 0), (1, 1), (2, 0)):
-        base(t, h)
+    base(0, 0)
+    quant("E", 128, 128, T.te, ["te1"], "qE1", 512)
+    base(0, 1)
+    quant("E", 256, 128, T.te, ["te2"], "qE2", 1024)
+    base(1, 0)
+    quant("E", 384, 128, T.te, ["te3"], "qE3", 1536)
+    base(1, 1)
     for b in range(4):
         mm(PA[b], 128, "Z", 128 * b, "L", 0, ["qZ", "sZ", "qGo", "qGp", "qGr"])
     for b in range(4):
@@ -533,9 +573,12 @@ def rank_program(g, core, T, topo):
     swap("T", "U", "up")
     turn(T.Tr3[:, 0:512], T.gap3[:, 0:512], ["gap3"], "Tr3a")
     turn(T.Tr3[:, 512:1024], T.gap3[:, 16:528], ["gap3"], "Tr3b")
+    base(2, 0)
     ts(T.o3[:, :], T.Tr3[:, :].indirect(T.sel3[:, 0:2]), 4.0, A.mult, ["Tr3a", "Tr3b", "sel3a", "sel3b", "l4"], "o3", cc(L4), A.add)
     act(T.txg[:, :], T.tx[:, :].indirect(T.o3[:, :]), AF.Copy, X + ["o3"], ["txg"])
-    for t, h in ((2, 1), (3, 0), (3, 1)):
+    base(2, 1)
+    quant("v", 0, 128, T.tv, ["tv"], "qvv")
+    for t, h in ((3, 0), (3, 1)):
         base(t, h)
     for b in range(4):
         mm(PA[b], 128, "E", 128 * b, "U", 0, ["qE%d" % b, "qTo", "qTp", "qTr"])

@@ -4,18 +4,18 @@ from concourse.mybir import dt, AluOpType as A, AxisListType, ActivationFunction
 F8, U8, BF, F32, I32, U16 = "float8_e4m3fn_x4", "uint8", "bfloat16", "float32", "int32", "uint16"
 SCRATCH = {}
 for _d, _l in (
-    (BF, "tu1 512 tu2 512 tv 512 tx 2048 xf 2048 tf 1024 th 1024 txh 1024 tg 512 tt 512 thn 512 txg 512 txn 512 ones 512 te 2048 "
-         "tot 528 ps 1056 val1 512 val2 256 sj 512 sk 512 sjv 7424 R1 1056 R2 544 Tr1 512 Tr2 256 Tr3 1024 gap3 528"),
-    (F32, "br 296 wt 296 iw 296 nt1 296 tbr 128 tbt 128 tb 24 seq 24 ft 16 ir 512 kr1 32 kr2 16 tr1 32 tr2 16 zero 32 c 64 gj 64 l64 128 "
-          "sc8 8 si8 8 sm 64 srow 1024 ch1 32 ch2 16 gt 32 eq 32 lt 32 ges 72 es2 32 ngt 32 trn 32 y1 32 me 32 dd 32 mm 32 vi 32 "
-          "L1r 256 olr 128 ysb 512"),
-    (I32, "ip 8 ipick 24 itb 4 irep 33"),
-    (U16, "opick 24 otb 8 orep 34 off 2 offb 2 offn 2 offq 2 og 2 osc1 32 osc2 16 o1 80 o2 80 o3 32 sel1 2 sel2 2 sel3 2")):
+    (BF, "tu1 512 tu2 512 tv 512 tx 2048 xf 2048 wn 3584 tf 1024 th 1024 hp 1024 tg 512 tt 512 thn 512 txg 512 ones 128 te 528 "
+         "val1 512 val2 256 sj 512 sk 512 sjv 7424 R1 4896 R2 2464 Tr1 512 Tr2 256 mul 448 br 296"),
+    (F32, "tbr 128 tbt 128 kr 128 kt 128 ks 48 ku 32 arow 8 ar 8 X1 32 W2 96 X2 96 crow 8 ft 16 cb 8 ir 1024 tr1 32 tr2 16 c 32 gj 64 l64 32 "
+          "sm 64 srow 1024 ch1 32 ch2 16 GE 72 MK 72 sg 32 es2 32 D0 96 D1 200 DO 96 E0 72 E1 72 EO 104 "
+          "L1r 256 olr 128 M1 256 v3 128 Mr 528 TrM 1024 ysb 512"),
+    (I32, "ipick 24"),
+    (U16, "opick 24 off 2 og 4 osc1 32 osc2 16 o1 32 o2 80 oM 32 sel1 2 sel2 2 sel3 2")):
     _l = _l.split()
     for _i in range(0, len(_l), 2):
         SCRATCH[_l[_i]] = ("sbuf", [128, int(_l[_i + 1])], _d)
 for _n, _w in (("W", 512), ("Z", 512), ("x", 512), ("N", 512), ("E", 512), ("F", 256), ("H", 256), ("u1", 128), ("u2", 128), ("r1", 128), ("r2", 384), ("v", 128),
-               ("G", 128), ("L", 128), ("T", 128), ("U", 128)):
+               ("G", 240), ("T", 240)):
     SCRATCH["q" + _n] = ("sbuf", [128, _w], F8)
     SCRATCH["s" + _n] = ("sbuf", [128, _w], U8)
 for _i in range(8):
@@ -52,7 +52,7 @@ def rank_program(g, core, T, topo):
     def deps_of(r, w):
         deps = []
         for t in r:
-            deps += wr.get(t, [])
+            deps += wr[t]
         for t in w:
             deps += wr.get(t, []) + rd.get(t, [])
         return deps
@@ -96,14 +96,14 @@ def rank_program(g, core, T, topo):
     def red(out, in_, op, r, w, **k):
         do("v", V.tensor_reduce, out, in_, AxisListType.X, op, r=r, w=[w], **k)
 
-    def scan(out, a, z, r, w):
-        do("v", V.tensor_tensor_scan, out, a, z, 0.0, A.add, A.add, r=r, w=[w])
+    def scan(out, a, z, r, w, first=0.0, op0=A.add, op1=A.add):
+        do("v", V.tensor_tensor_scan, out, a, z, first, op0, op1, r=r, w=[w])
 
     def turn(out, in_, r, w):
         do("v", V.transpose, out, in_, r=r, w=[w])
 
-    def fill(ap, x, w):
-        do("v", V.memset, ap, x, w=[w])
+    def fill(ap, x, w, r=()):
+        do("v", V.memset, ap, x, r=r, w=[w])
 
     def cp(out, in_, r, w):
         do("v", V.tensor_copy, out, in_, r=r, w=[w])
@@ -123,147 +123,153 @@ def rank_program(g, core, T, topo):
     def sm(j):
         return T.sm[:, j:j + 1]
 
+    def four(n):
+        return ["%s%d" % (n, t) for t in range(4)]
+
     dma("s", T.tu1[:, :], T.u1[:, :], w=["tu1"])
     for j in range(4):
         dma("a" if j % 2 == 0 else "s", T.tx[:, 512 * j:512 * j + 512], T.x[:, 512 * j:512 * j + 512], w=["tx%d" % j])
-    X = ["tx%d" % j for j in range(4)]
+    X = four("tx")
 
-    def iota(n, pattern, base, cm=0):
+    def iota(n, pattern, base, cm=0, at=0, w=None):
         k = 1
         for _s, m in pattern:
             k *= m
         f = {} if SCRATCH[n][2] == I32 else {"allow_small_or_imprecise_dtypes": True}
-        do("g", g.iota, T[n][:, 0:k], pattern, base, cm, w=[n], **f)
+        do("g", g.iota, T[n][:, at:at + k], pattern, base, cm, w=[w or n], **f)
 
     def select(out, src, pattern, op, base, cm, r, w):
         do("g", g.affine_select, out, src, pattern, op, 0.0, base, cm, r=r, w=[w])
-    iota("ip", [[1, 1]], 0, 1)
-    iota("itb", [[62, 2], [0, 2]], 75)
+
+    def plane(out, src, n, r, w):
+        select(out, src, [[0, n]], A.is_ge, 0, 0, r, w)
     iota("ipick", [[16, 8]], 0)
-    iota("seq", [[17, 17]], 0)
-    iota("kr1", [[1, 32]], 512)
-    do("g", g.iota, T.ipick[:, 8:24], [[16, 2], [32, 4], [0, 2]], 0, 0, w=["ipick2"])
-    iota("tot", [[0, 16], [1, 33]], 0)
-    select(T.ps[0:16, 0:528], T.tot[0:16, :], [[-1, 16], [0, 33]], A.is_gt, 0, 1, ["tot"], "psa")
-    select(T.ps[0:16, 528:1056], T.tot[0:16, :], [[1, 16], [0, 33]], A.is_ge, 0, -1, ["tot"], "psb")
+    iota("kr", [[0, 2], [1, 16]], 0, w="kr0")
+    iota("kr", [[1, 2], [0, 16]], 0, at=32, w="kr1")
+    iota("arow", [[2, 8]], 0)
+    iota("ipick", [[16, 2], [32, 4], [0, 2]], 0, at=8, w="ipick2")
+    iota("kr", [[16, 2], [32, 8], [256, 2]], 0, at=64, w="kr2")
+    iota("kr", [[16, 2], [32, 8], [512, 2]], 0, at=96, w="kr3")
+    iota("ks", [[0, 5], [32, 4], [128, 2]], 0, at=8 - (rank + 1) % N)
+    iota("tr1", [[1, 32]], 512, 32)
+    iota("ir", [[1, 1024]], 0)
     iota("val1", [[1, 32], [32, 16]], -256)
-    iota("kr2", [[1, 16]], 256)
+    for t in range(4):
+        plane(T.wn[:, 896 * t:896 * t + 512], T.tx[:, t:2048:4], 512, X, "xp%d" % t)
+    iota("tr2", [[1, 16]], 256, 16)
     iota("val2", [[1, 16], [16, 16]], 0)
-    iota("irep", [[4, 33]], 0)
-    iota("ir", [[1, 512]], 0)
-    iota("ones", [[0, 512]], 1)
-    for b in range(4):
-        select(T.te[:, 512 * b:512 * b + 512], T.ones[:, :], [[1, 512]], A.is_equal, -b, -4, ["ones"], "te%d" % b)
-    LANE, ODD, LP1, CN, CP, L33, O16, EVEN, L32, M8, E8, D6, L16, LQ, LR, L4, LB, SO, SO7, L7, LQ4, NODD, LM8 = range(23)
-    B1, B2 = [], []
+    iota("M1", [[1, 256]], 512)
+    iota("v3", [[1, 128]], 768)
+
+    br = T.br
+    fill(T.mul[:, 0:146], 0.5, "mul0")
+    fill(T.mul[:, 146:290], 2.0, "mul1")
+    fill(T.mul[:, 290:434], 1.0, "mul2")
+    fill(T.X1[:, :], 0.0, "X1z")
+    scan(br[:, 0:146], T.mul[:, 0:146], T.mul[:, 0:146], ["mul0"], "bn", -2.0 ** 76, A.mult, A.min)
+    scan(br[:, 146:290], T.mul[:, 146:290], T.mul[:, 290:434], ["mul1", "mul2"], "bp", 2.0 ** -71, A.mult, A.mult)
+    fill(T.W2[:, :], 0.0, "W2z")
+    fill(T.ft[:, :], 0.0, "ftz")
+    B = ["bn", "bp"]
+    for h in range(2):
+        cp(T.tbr[:, 16 * h:16 * h + 16], br[:, 17:289:17], B, "tba%d" % h)
+        cp(T.tbr[:, 32 + 16 * h:48 + 16 * h], br[:, 137:153], B, "tbb%d" % h)
+        act(T.tbr[:, 64 + 16 * h:80 + 16 * h], br[:, 75:91], AF.Identity, B, ["tbc%d" % h], scale=-1.0)
+        act(T.tbr[:, 96 + 16 * h:112 + 16 * h], br[:, 201:217], AF.Identity, B, ["tbd%d" % h], scale=-1.0)
+    cp(T.opick[:, 0:8], T.ipick[:, 0:8], ["ipick"], "opick")
+    turn(T.kt[:, 0:64], T.kr[:, 0:64], ["kr0", "kr1"], "lane")
+    turn(T.tbt[:, :], T.tbr[:, :], ["tb%s%d" % (x, h) for x in "abcd" for h in range(2)], "tbt")
+    B1, T8, QL, PL = (T.tbt[:, 32 * j:32 * j + 1] for j in range(4))
+    LANE, ODD = T.kt[:, 0:1], T.kt[:, 32:33]
+    NB1, LP1, CN, CP, L33, O16, EVEN, NODD, L2, Z12, M8, D6, CB, CB6, L16, Z14, NO16, SQ, S0, SH, L64, BA, BE, BR1, BR2 = range(25)
+    W2 = T.W2
+    WT = ["W2z"]
+    for k, (o, i, s) in enumerate(((W2[:, 0:30:2], br[:, 61:76], -1.0), (W2[:, 30:32], br[:, 75:77], -1.0), (W2[:, 32:48:2], br[:, 69:77], -1.0),
+                                   (W2[:, 48:50], br[:, 215:217], 1.0), (W2[:, 51:52], br[:, 76:77], 1.0), (W2[:, 53:64:2], br[:, 215:221], 1.0),
+                                   (W2[:, 64:66], br[:, 215:217], 1.0), (W2[:, 67:96:2], br[:, 216:231], 1.0))):
+        act(o, i, AF.Identity, B + ["W2z"], ["W2%d" % k], scale=s)
+        WT.append("W2%d" % k)
+    K17 = 2.0 ** 17 - 1
+    fill(T.D0[:, 0:96:3], 0.0, "D0a")
+    fill(T.D0[:, 2:96:3], 1.0, "D0c")
+    fill(T.MK[:, :], 1.0, "MK1")
+    ts(cc(NB1), B1, -1.0, A.mult, ["tbt"], "nb1")
+    ts(T.X1[:, 19:32:2], br[:, 153:256:17], PL, A.mult, B + ["tbt", "X1z"], "X1a", -2.0 ** 16 * K17, A.mult)
+    ts(T.X1[:, 0:14:2], br[:, 34:137:17], QL, A.mult, B + ["tbt", "X1z"], "X1b", 2.0 ** 16 * K17, A.mult)
+    ts(T.X1[:, 17:18], PL, -2.0 ** -47, A.mult, ["tbt", "X1z"], "X1c", T8, A.subtract)
+    ts(T.X1[:, 14:15], QL, -2.0 ** -45, A.mult, ["tbt", "X1z"], "X1d")
+    cp(T.X1[:, 15:16], T8, ["tbt", "X1z"], "X1e")
+    X1T = ["X1" + x for x in "zabcde"]
+    quant("u1", 0, 128, T.tu1, ["tu1"], "qu1")
+    ts(cc(Z12), LANE, 0.0, A.is_equal, ["lane"], "z12", 12.0, A.mult)
+    ts(cc(Z14), LANE, 15.0, A.is_equal, ["lane"], "z14", 14.0, A.mult)
+    cp(words(T.qr1[:, :]), words(T.qu1[:, :]).indirect(T.opick[:, 0:8]), ["qu1", "opick"], "qr1")
 
     def lin(out, w, src, k, add):
-        act(out, cc(src), AF.Identity, ["lane", "odd"], [w], scale=k, bias=add)
-
-    def neg(k, n, s):
-        ts(T.br[:, k:k + n], T.br[:, k - s:k - s + n], 2.0 ** -s, A.mult, list(B1), "bn%d" % k)
-
-    def pos(k, n, s):
-        act(T.br[:, 146 + k:146 + k + n], T.br[:, 146 + k - s:146 + k - s + n], AF.Identity, list(B2), ["bp%d" % k], scale=2.0 ** s)
-
-    def grow(f, B, n, parts):
-        for p in parts:
-            f(*p)
-        B += [n + "%d" % p[0] for p in parts]
-    for k in range(4):
-        fill(T.br[:, 146 + k:147 + k], 2.0 ** (k - 70), "bp%d" % k)
-        B2.append("bp%d" % k)
-    for k in range(4):
-        fill(T.br[:, k:k + 1], -2.0 ** (75 - k), "bn%d" % k)
-        B1.append("bn%d" % k)
-    ts(T.ip[:, 1:2], T.ip[:, 0:1], 15, A.bitwise_and, ["ip"], "ip1")
-    ts(T.ip[:, 2:3], T.ip[:, 0:1], 4, A.logical_shift_right, ["ip"], "ip2", 1, A.bitwise_and)
-    grow(neg, B1, "bn", [(4, 4, 4), (8, 4, 8), (12, 4, 12)])
-    grow(pos, B2, "bp", [(4, 4, 4), (8, 4, 8), (12, 4, 12)])
-    cp(cc(LANE), T.ip[:, 1:2], ["ip1"], "lane")
-    cp(cc(ODD), T.ip[:, 2:3], ["ip2"], "odd")
-    cp(T.opick[:, 0:8], T.ipick[:, 0:8], ["ipick"], "opick")
-    grow(neg, B1, "bn", [(16, 16, 16), (32, 16, 32), (48, 16, 48)])
-    grow(pos, B2, "bp", [(16, 16, 16), (32, 16, 32), (48, 16, 48)])
-    lin(T.iw[:, 145:146], "iwc", LANE, 0.0, 2.0 ** 69)
-    lin(T.wt[:, 145:146], "wtc", LANE, 0.0, 2.0 ** -69)
-    ts(T.otb[:, 6:7], cc(LANE), 17.0, A.mult, ["lane"], "otbd", 17.0, A.add)
-    ts(T.otb[:, 7:8], cc(LANE), 17.0, A.mult, ["lane"], "otbe", 17.0, A.add)
-    grow(neg, B1, "bn", [(64, 64, 64), (128, 18, 96)])
-    grow(pos, B2, "bp", [(64, 64, 64), (128, 16, 96)])
-    ts(T.otb[:, 0:4], T.itb[:, :], cc(LANE), A.add, ["itb", "lane"], "otba")
-    ts(T.otb[:, 4:5], cc(LANE), 216.0, A.add, ["lane"], "otbb")
-    ts(T.otb[:, 5:6], cc(LANE), 216.0, A.add, ["lane"], "otbc")
-    B = B1 + B2
-    quant("u1", 0, 128, T.tu1, ["tu1"], "qu1")
-    cp(T.tbr[:, 96:128], T.br[:, 0:290].indirect(T.otb[:, 6:8]), B + ["otbd", "otbe"], "tbr3")
-    cp(words(T.qr1[:, :]), words(T.qu1[:, :]).indirect(T.opick[:, 0:8]), ["qu1", "opick"], "qr1")
-    turn(T.tbt[:, 96:128], T.tbr[:, 96:128], ["tbr3"], "tbt3")
-    FT = ["fta", "base"]
-    NT, WT, IW = ["nta", "ntb", "ntc"], ["wta", "wtb", "wtc"], ["iwa", "iwb", "iwc"]
-
-    lin(cc(56), "cb", LANE, -0.9375, -0.9375)
-    lin(cc(CN), "cn", LANE, -0.0625, 1.9375)
+        act(out, src, AF.Identity, ["lane"], [w], scale=k, bias=add)
+    lin(cc(L2), "l2", LANE, 2.0, 0.0)
+    lin(cc(CN), "cn", LANE, 0.0625, -1.9375)
     lin(cc(CP), "cp", LANE, 0.0625, 1.0625)
+    lin(cc(CB), "cbl", LANE, -0.9375, -0.9375)
     lin(cc(LP1), "lp1", LANE, 1.0, 1.0)
-    lin(T.nt1[:, 145:146], "ntc", LANE, 2.0 ** -73, -7 * 2.0 ** -73)
+    lin(cc(L16), "l16", LANE, 0.0625, 0.0625)
+    lin(T.X2[:, 49:50], "X2c", LANE, 0.0625, -0.4375)
+    lin(T.X2[:, 50:51], "X2d", LANE, 0.0, 0.0)
+    lin(T.X2[:, 51:52], "X2e", LANE, -0.03125, 0.96875)
     act(T.sr1[:, :], T.su1[:, :].indirect(T.opick[:, 0:8]), AF.Copy, ["qu1", "opick"], ["sr1"])
-    act(T.nt1[:, 0:145], T.br[:, 1:146], AF.Identity, B1 + ["cn"], ["nta"], scale=cc(CN))
-    act(T.nt1[:, 146:289], T.br[:, 146:289], AF.Identity, B2 + ["cp"], ["ntb"], scale=cc(CP))
+    act(T.X2[:, 0:49], W2[:, 0:49], AF.Identity, WT + ["cn"], ["X2a"], scale=cc(CN))
+    act(T.X2[:, 52:96], W2[:, 52:96], AF.Identity, WT + ["cp"], ["X2b"], scale=cc(CP))
+    X2T = ["X2" + x for x in "abcde"]
+    act(T.cb[:, 2:4], T.arow[:, 0:2], AF.Identity, ["arow", "cbl"], ["cb1"], scale=0.5, bias=cc(CB))
+    act(T.crow[:, 0:5], br[:, 79:96:4], AF.Identity, B, ["crow0"], scale=-1.0)
+    act(T.crow[:, 5:6], br[:, 98:99], AF.Identity, B, ["crow1"], scale=-1.0)
+    act(T.cb[:, 0:2], T.cb[:, 2:4], AF.Identity, ["cb1"], ["cb0"], scale=0.0625)
+    U = 2.0 ** -10
+    act(cc(SQ), LANE, AF.Square, ["lane"], ["sq"], bias=-0.5)
+    lin(cc(L33), "l33", LANE, -64.0, 960.0)
+    lin(cc(BA), "ba", LANE, 64.0, -1024.0)
+    lin(cc(BE), "be", LANE, 64.0 * U, -1.0)
+    act(cc(S0), cc(SQ), AF.Identity, ["sq"], ["s0"], scale=-32 * U, bias=8 * U)
 
     def gap(k):
-        if k == 0:
-            act(T.wt[:, 0:145], T.br[:, 1:146], AF.Identity, B1, ["wta"], scale=-1.0)
-            act(T.wt[:, 146:289], T.br[:, 146:289], AF.Identity, B2, ["wtb"])
-            act(T.c[:, 40:44], T.br[:, 79:92:4], AF.Identity, B1, ["crow0"], scale=-1.0)
-            act(T.c[:, 44:46], T.br[:, 95:99:3], AF.Identity, B1, ["crow1"], scale=-1.0)
-        elif k == 1:
-            act(T.iw[:, 0:145], T.br[:, 142:287], AF.Identity, B, ["iwa"])
-            act(T.c[:, 48:53], T.br[:, 220:237:4], AF.Identity, B2, ["drow0"])
-            act(T.c[:, 53:54], T.br[:, 239:240], AF.Identity, B2, ["drow1"])
-        else:
-            lin(cc(E8), "e8", LANE, 0.125, -3.875)
-            lin(cc(L33), "l33", LANE, 33.0, 0.0)
-            lin(cc(L32), "l32", LANE, 32.0, 0.0)
+        if k < 2:
+            p = ("p3", "p4")[k]
+            act(T.srow[:, 256 + 128 * k:384 + 128 * k], T[p][:, 0:128], AF.Copy, [p], ["srow%d" % (k + 1), p + "s"])
+            if k == 1:
+                dma("s", T.ch1[:, :], T.srow[0:128:16, 0:512], r=["srow0", "srow1", "srow2"], w=["ch"])
+                dma("s", codes(T.qW[:, :]), T.wc[:, :], w=["qW"])
+                dma("s", T.sW[:, :], T.ws[:, :], w=["sW"])
+        elif k == 2:
+            act(cc(SH), ODD, AF.Identity, ["lane", "s0"], ["sh"], scale=8 * U, bias=cc(S0))
+            lin(cc(BR1), "br512", ODD, 0.5 * U, 496 * U)
+        elif k == 3:
+            act(cc(L64), cc(SH), AF.Identity, ["sh", "l33"], ["l64"], scale=-1024.0, bias=cc(L33))
+            act(T.GE[:, 32:33], cc(SH), AF.Identity, ["sh"], ["GEz"])
+        elif k == 4:
+            act(cc(CB6), cc(D6), AF.Identity, ["d6"], ["cb6"], scale=-8.0)
+            act(T.D1[:, 2:3], cc(SH), AF.Identity, ["sh"], ["D1z"])
+        elif k == 5:
+            act(T.cb[:, 6:8], T.arow[:, 0:2], AF.Identity, ["arow", "cb6"], ["cb3"], scale=0.5, bias=cc(CB6))
             lin(cc(O16), "o16", ODD, 16.0, 0.0)
+        elif k == 6:
+            act(T.D1[:, 0:96:3], T.tr1[:, :], AF.Identity, ["tr1"], ["trn"], scale=U)
 
-    quant("x", 0, 128, T.tx, ["tx0"], "qx0")
-    quant("x", 128, 128, T.tx, ["tx1"], "qx1")
-    ts(T.tb[:, 18:19], T.tbt[:, 96:97], -1.0, A.mult, ["tbt3"], "tbe")
-    ts(T.tb[:, 17:18], T.tbt[:, 96:97], 1.0, A.mult, ["tbt3"], "tbd")
-    quant("x", 256, 128, T.tx, ["tx2"], "qx2")
-    quant("x", 384, 128, T.tx, ["tx3"], "qx3")
-    cp(T.tbr[:, 0:96], T.br[:, 0:290].indirect(T.otb[:, 0:6]), B + ["otba", "otbb", "otbc"], "tbr")
-    fill(T.ft[:, 0:16], 0.0, "base")
-    ts(T.off[:, 1:2], cc(LANE), 0.0, A.is_equal, ["lane"], "off1", 8.0, A.mult)
-    turn(T.tbt[:, 0:96], T.tbr[:, 0:96], ["tbr"], "tbt")
-    fill(T.ges[:, :], 0.0, "ges0")
-    fill(T.zero[:, :], 0.0, "zero")
-    ts(T.tb[:, 0:8], T.br[:, 1:121:17], T.tbt[:, 0:1], A.mult, B1 + ["tbt"], "tba", -1.0, A.mult)
-    ts(T.tb[:, 9:17], T.br[:, 154:274:17], T.tbt[:, 64:65], A.mult, B2 + ["tbt"], "tbb")
-    ts(T.tb[:, 8:9], T.tbt[:, 32:33], 1.0, A.mult, ["tbt"], "tbc")
-    do("v", V.memset, T.ft[:, 1:2], 1.0, r=["base"], w=["fta"])
     R = ["qr1", "sr1"]
-    mm("p2", 256, "r1", 0, "x", 0, ["qx0", "qx1"] + R)
-    mm("p3", 256, "r1", 0, "x", 256, ["qx2", "qx3"] + R)
-    for p in ("p0", "p1"):
-        mm(p, 512, "r1", 0, "x", 0, ["qx%d" % j for j in range(4)] + R)
+    for j in range(4):
+        quant("x", 128 * j, 128, T.tx, ["tx%d" % j], "qx%d" % j)
+    QX = four("qx")
+    mm("p2", 256, "r1", 0, "x", 0, QX[0:2] + R)
+    mm("p3", 128, "r1", 0, "x", 256, QX[2:3] + R)
+    mm("p4", 128, "r1", 0, "x", 384, QX[3:4] + R)
+    mm("p0", 384, "r1", 0, "x", 0, QX[0:3] + R)
+    mm("p1", 384, "r1", 0, "x", 128, QX[1:4] + R)
+    ts(T.ar[:, :], T.arow[:, :], cc(Z12), A.max, ["arow", "z12", "z14"], "ar", cc(Z14), A.max)
+    ts(cc(M8), LANE, 8.0, A.is_ge, ["lane"], "m8", 4.0, A.mult)
+    cp(T.opick[:, 8:24], T.ipick[:, 8:24], ["ipick2"], "opick2")
+    turn(T.kt[:, 64:128], T.kr[:, 64:128], ["kr2", "kr3"], "kt2")
 
     learn("s", [d for t in X for d in wr[t]])
     dma("s", T.tu2[:, :], T.u2[:, :], w=["tu2"])
-    dma("s", codes(T.qW[:, :]), T.wc[:, :], w=["qW"])
-    dma("s", T.sW[:, :], T.ws[:, :], w=["sW"])
-    for j in range(1, 8):
-        dma("s", T.ps[16 * j:16 * j + 16, :], T.ps[0:16, :], r=["psa", "psb"], w=["ps%d" % j])
-    PS = ["psa", "psb"] + ["ps%d" % j for j in range(1, 8)]
-
-    def rows(pb, n, ch, a, b):
-        cp(T.srow[:, a:b], T[pb][:, a:b], [pb], "srow%d" % a)
-        if b == n:
-            dma("s", ch[:, :], T.srow[0:128:16, 0:n], r=["srow0", "srow%d" % a], w=["ch"])
-
-    def base(t, h):
-        cp(T.xf[:, :].indirect(T.o1[:, 16 * t + 8 * h:16 * t + 8 * h + 8]), T.txh[:, 512 * h + t:512 * h + 512:4], ["o1_%d" % t, "txh", "xf0"], "xf")
 
     def pick_q(k):
         cp(words(T.qr2[:, 128 * k:128 * k + 128]), words(T.qu2[:, :]).indirect(T.opick[:, 8 * k:8 * k + 8]), ["qu2", "opick", "opick2"], "qr2%d" % k)
@@ -271,169 +277,184 @@ def rank_program(g, core, T, topo):
     def pick_s(k):
         act(T.sr2[:, 128 * k:128 * k + 128], T.su2[:, :].indirect(T.opick[:, 8 * k:8 * k + 8]), AF.Copy, ["qu2", "opick", "opick2"], ["sr2%d" % k])
 
-    def jobs1():
-        ts(cc(M8), cc(LANE), 8.0, A.is_lt, ["lane"], "m8")
-        cp(T.opick[:, 8:24], T.ipick[:, 8:24], ["ipick2"], "opick2")
-        yield
-        ts(T.tr1[:, :], T.kr1[:, :], cc(L32), A.add, ["kr1", "l32"], "tr1")
-        ts(cc(D6), cc(E8), cc(M8), A.mult, ["e8", "m8"], "d6", 4.0, A.add)
-        rows("p1", 512, T.ch1, 0, 256)
-        yield
-        rows("p1", 512, T.ch1, 256, 512)
-        yield
-        ts(cc(60), cc(D6), cc(LP1), A.subtract, ["d6", "lp1"], "cb5")
-        ts(cc(61), cc(D6), -8.0, A.mult, ["d6"], "cb6")
-        quant("u2", 0, 128, T.tu2, ["tu2"], "qu2")
-        yield
-        pick_q(0)
-        pick_q(1)
-        yield
-        ts(T.ip[:, 5:6], T.ip[:, 1:2], 1, A.bitwise_and, ["ip1"], "ip5")
-        ts(cc(SO), cc(LANE), 16.0, A.mult, ["lane", "o16"], "so16", cc(O16), A.add)
-        pick_q(2)
-        yield
-        cp(cc(LB), T.ip[:, 5:6], ["ip5"], "lb")
-        fill(T.R1[:, 0:272], 0.0, "R1")
-        ts(T.sel1[:, 0:1], cc(LB), 240.0, A.mult, ["lb", "so16"], "sel1", cc(SO), A.add)
-        yield
+    def job(k):
+        if k == 0:
+            cp(T.srow[:, 0:256], T.p2[:, 0:256], ["p2", "sm1"], "srow0")
+        elif k == 2:
+            ts(cc(D6), cc(LP1), 0.125, A.mult, ["lp1", "m8"], "d6", cc(M8), A.max)
+            fill(T.MK[:, 32:33], 0.0, "MK", ["MK1"])
+            fill(T.R1[:, 0:272], 0.0, "R1")
+        elif k == 3:
+            ts(T.cb[:, 4:6], T.cb[:, 2:4], cc(D6), A.add, ["cb1", "d6", "l16"], "cb2", cc(L16), A.subtract)
+            quant("u2", 0, 128, T.tu2, ["tu2"], "qu2")
+        elif k < 7:
+            pick_q(k - 4)
+        else:
+            cp(T.sel1[:, 0:1], T.kt[:, 64:65], ["kt2"], "sel1")
+            fill(T.E0[:, :], 0.0, "E0")
+            fill(T.R2[:, 0:144], 0.0, "R2")
 
-    def search(n, pa, pb, first, b, jobs):
-        def job():
-            for _ in jobs:
-                return
-
+    def search():
         def count(t, j, tk, p, w, sign=-1.0, buf="sj"):
             act(T[buf][:, 0:w], T[p][:, 0:w], AF.Sign, [p, tk], [buf, "sm%d" % j], scale=sign, bias=t, accum_out=sm(j))
 
-        def answer(j, n2=0):
-            if n2:
-                ts(T.off[:, 0:1], sm(14), sm(j), A.subtract, ["sm14", "sm%d" % j], "off0", float(n2), A.is_ge)
-            else:
-                ts(T.off[:, 0:1], sm(j), 0.0, A.is_le, ["sm%d" % j], "off0")
-        (p0, w0), (p1, w1) = first
-        count(T.tb[:, 18:19], 1, "tbe", p0, w0, 1.0, "sk")
-        count(T.tb[:, 17:18], 0, "tbd", p1, w1)
+        def flags(t, tk, p, a, b, op=A.is_ge, k=2.0, w=()):
+            do("v", V.tensor_scalar, T.sjv[:, 0:b], T[p][:, a:a + b], t, k, op, A.mult, r=[p, tk], w=["fl"] + list(w))
+
+        def total_of(b, first):
+            scan(T.sjv[:, 512:512 + b // 2], T.sjv[:, 0:b // 2], T.sjv[:, b // 2:b], ["fl"], "cv", first)
+            return T.sjv[:, 511 + b // 2:512 + b // 2]
+
+        def answer(v, vk, j, at, ak, op=A.is_ge):
+            ts(T.off[:, 0:1], v, sm(j), op, [vk, "sm%d" % j, ak], "off", at, A.add)
+
+        def gather_sum(tab, n, r, j, **k):
+            act(T.gj[:, 0:16], tab[:, 0:n].indirect(T.off[:, 0:1]), AF.Identity, ["off"] + r, ["gj", "sm%d" % j], accum_out=sm(j), **k)
+        count(cc(NB1), 0, "nb1", "p2", 256, 1.0, "sk")
+        count(cc(NB1), 1, "nb1", "p3", 128, 1.0, "sj")
+        count(B1, 2, "tbt", "p4", 128, -1.0, "sk")
         gap(0)
-        ts(T.offb[:, 0:1], sm(0), sm(1), A.is_le, ["sm0", "sm1", "lp1"], "offb", cc(LP1), A.mult)
-        cp(T.l64[:, 0:16], T.tb[:, 0:17].indirect(T.offb[:, 0:1]), ["offb", "tba", "tbb", "tbc"], "b16")
-        cp(T.l64[:, 64:80], T.seq[:, 0:17].indirect(T.offb[:, 0:1]), ["offb", "seq"], "s16")
-        red(sm(3), T.l64[:, 0:16], A.max, ["b16"], "sm3")
-        red(sm(5), T.l64[:, 64:80], A.max, ["s16"], "sm5")
-        count(sm(3), 4, "sm3", pa, n)
+        ts(sm(3), sm(0), sm(1), A.add, ["sm0", "sm1"], "sm3")
+        answer(sm(2), "sm2", 3, cc(L2), "l2", A.is_le)
+        gather_sum(T.X1, 32, X1T, 4)
+        job(0)
+        count(sm(4), 5, "sm4", "p0", 384)
+        flags(sm(4), "sm4", "p4", 0, 128, w=["p4s"])
         gap(1)
-        ts(sm(2), cc(LP1), sm(5), A.add, ["lp1", "sm5"], "sm2")
-        cp(T.offq[:, 1:2], sm(5), ["sm5"], "offq1")
-        ts(T.iw[:, 146:289], T.br[:, 5:148], -1.0, A.mult, B, "iwb")
-        job()
-        ts(T.offq[:, 0:1], sm(4), 0.0, A.is_le, ["sm4", "sm2"], "offq0", sm(2), A.mult)
-        answer(4)
-        cp(T.l64[:, 96:128], T.nt1[:, 0:289].indirect(T.offq[:, 0:2]), ["offq0", "offq1"] + NT, "n32")
-        act(T.gj[:, 0:16], T.ft[:, 0:8].indirect(T.off[:, 0:1]), AF.Identity, ["off0"] + FT, ["gj", "sm6"], accum_out=sm(6))
-        red(sm(7), T.l64[:, 96:128], A.max, ["n32"], "sm7")
-        ts(T.offn[:, 0:1], sm(6), sm(5), A.add, ["sm6", "sm5"], "offn")
-        cp(T.l64[:, 32:48], T.iw[:, 0:289].indirect(T.offn[:, 0:1]), ["offn"] + IW, "i16")
-        cp(T.l64[:, 48:64], T.wt[:, 0:289].indirect(T.offn[:, 0:1]), ["offn"] + WT, "w16")
-        t, tk = sm(7), "sm7"
+        ts(sm(6), sm(4), T8, A.is_gt, ["sm4", "tbt"], "sm6", 32.0, A.mult)
+        ts(sm(7), sm(4), T8, A.is_ge, ["sm4", "tbt"], "sm7", 32.0, A.mult)
+        ts(sm(8), sm(4), QL, A.mult, ["sm4", "tbt"], "sm8", 2.0 ** -69, A.max)
+        v = total_of(128, -128.0)
+        ts(sm(9), sm(6), sm(7), A.add, ["sm6", "sm7", "l2"], "sm9", cc(L2), A.add)
+        ts(sm(10), sm(4), PL, A.mult, ["sm4", "sm8", "tbt"], "sm10", sm(8), A.max)
+        answer(v, "cv", 5, sm(9), "sm9")
+        gather_sum(T.X2, 96, X2T + ["sm10"], 11, scale=sm(10))
+        ts(T.l64[:, 0:16], W2[:, :].indirect(T.off[:, 0:1]), sm(10), A.mult, ["off", "sm10"] + WT, "w16")
+        red(sm(12), T.l64[:, 0:16], A.add, ["w16"], "sm12")
+        t, tk = sm(11), "sm11"
         for r in range(6):
-            nx = "sm%d" % (16 + r)
+            b = 128 if r == 0 else 176
 
             def start():
-                ts(T.ft[:, 8:9], t, T.si8[:, r:r + 1], A.mult, [tk, "si8", ["cb", "cb5", "cb6"][max(r - 3, 0)]], "base", cc(56 if r < 4 else 56 + r), A.add)
-            if r == 0:
-                count(t, 8, tk, pa, n)
-                gap(2)
-                ts(T.si8[:, 0:6], T.c[:, 48:54], T.l64[:, 32:33], A.mult, ["i16", "drow0", "drow1"], "si8")
-                ts(T.sc8[:, 0:6], T.c[:, 40:46], T.l64[:, 48:49], A.mult, ["w16", "crow0", "crow1"], "sc8")
+                if r == 0:
+                    ts(T.ft[:, 1:12:2], T.crow[:, 0:6], sm(12), A.mult, ["sm12", "crow0", "crow1", "ftz"], "steps")
+                    ts(T.ft[:, 12:14], T.cb[:, 0:2], sm(12), A.mult, ["sm12", "cb0", "ftz", tk], "base", t, A.add)
+                else:
+                    k = max(r - 2, 1)
+                    ts(T.ft[:, 12:14], T.cb[:, 2 * k:2 * k + 2], T.ft[:, 2 * r + 1:2 * r + 2], A.mult, ["steps", "cb%d" % k, tk], "base", t, A.add)
+            if r < 5:
+                count(t, 16 + r, tk, "p0", 512 - b)
+                gap(2 + r)
+                flags(t, tk, "p1", 384 - b, b)
                 start()
-                answer(8)
-            elif r < 5:
-                count(t, 8 + r, tk, pa, n - b)
-                ts(T.sjv[:, 0:b], T[pb][:, n - b:n], t, A.is_ge, [pb, tk], "sjv0", 2.0, A.mult)
-                start()
-                red(sm(14), T.sjv[:, 0:b], A.add, ["sjv0"], "sm14")
-                answer(8 + r, b)
+                v = total_of(b, -float(b))
             else:
-                m = n // 2
-                ts(T.sjv[:, 0:m], T[pb][:, m:n], t, A.is_lt, [pb, tk], "sjv0")
-                act(T.sj[:, 0:m], T[pa][:, 0:m], AF.Sign, [pa, tk], ["sj"], scale=-1.0, bias=t)
+                act(T.sj[:, 0:176], T.p0[:, 0:176], AF.Sign, ["p0", tk], ["sj"], scale=-1.0, bias=t)
+                flags(t, tk, "p1", 48, 336, A.is_lt, -1.0)
+                act(T.sk[:, 0:176], T.sj[:, 0:176], AF.Relu, ["sj"], ["sk", "sm21"], accum_out=sm(21))
                 start()
-                act(T.sk[:, 0:m], T.sj[:, 0:m], AF.Relu, ["sj"], ["sk", "sm13"], accum_out=sm(13))
-                red(sm(14), T.sjv[:, 0:m], A.add, ["sjv0"], "sm14")
-                ts(T.off[:, 0:1], sm(14), sm(13), A.add, ["sm13", "sm14"], "off0", n / 2.0, A.is_le)
-            act(T.gj[:, 0:32], T.ft[:, :].indirect(T.off[:, 0:2]), AF.Identity, ["off0", "off1", "sc8"] + FT, ["gj", nx], scale=T.sc8[:, r:r + 1], accum_out=sm(16 + r))
-            t, tk = sm(16 + r), nx
-            job()
-        for _ in jobs:
-            pass
+                v = total_of(336, 256.0)
+            answer(v, "cv", 16 + r, T.ar[:, r:r + 1], "ar")
+            gather_sum(T.ft, 16, ["steps", "base", "ftz"], 24 + r)
+            t, tk = sm(24 + r), "sm%d" % (24 + r)
+            job(2 + r)
         return t, tk
 
-    def ranks(pm, pe, po, ps_):
-        NV = 10
+    def ranks():
         w = T.srow
-        raw, mk, gm, gin, gout, bm, bmt = (w[:, 768:784], w[:, 784:800], w[:, 800:816], 832, 864, 896, 928)
+        rawe, rawo = T.sjv[:, 4608 + 127:4608 + 1024:128], w[:, 776:784]
 
         def bound(i):
             k = 512 + 32 * (i % 8) + 16 * (i // 8)
-            return w[:, k:k + 1]
+            return w[:, k:k + 1], "tr" + "ab"[i % 8 // 4]
 
         def flags(i, a=0, b=256):
             return T.sjv[:, 512 + 256 * i + a:512 + 256 * i + b]
 
+        def over(i, p, a, b):
+            t, tk = bound(i)
+            do("v", V.tensor_scalar, flags(i, a, b), T[p][:, 0:b - a], t, None, A.is_gt, r=[p, tk], w=["fl%d_%d" % (i, a)] + (["cv"] if i == 0 else []))
+
         def total_v(i):
-            scan(T.sjv[:, 4608 + 128 * i:4736 + 128 * i], flags(i, 0, 128), flags(i, 128, 256), ["fl%d" % i], "sc%d" % i)
+            k = 4608 + 128 * (i if i < 8 else i - 6)
+            scan(T.sjv[:, k:k + 128], flags(i, 0, 128), flags(i, 128, 256), ["fl%d_0" % i] + (["fl%d_128" % i] if i < 8 else []), "sc%d" % i)
 
         def total_a(i):
-            k = 5888 + 256 * (i - NV)
+            k = 5888 + 256 * (i - 8)
             act(T.sjv[:, k:k + 256], flags(i), AF.Relu, ["fl%d" % i], ["sc%d" % i], scale=-1.0, accum_out=w[:, 768 + i:769 + i])
-        turn(w[:, 512:768], T[pm][:, 0:256], [pm], "trs")
-        for i in range(NV, 16):
-            act(flags(i), T[ps_][:, 0:256], AF.Sign, [ps_, "trs"], ["fl%d" % i], scale=-1.0, bias=bound(i))
-            if i > NV:
+
+        def sign(i):
+            t, tk = bound(i)
+            act(flags(i), T.p4[:, 0:256], AF.Sign, ["p4", tk], ["fl%d" % i], scale=-1.0, bias=t)
+        turn(w[:, 512:640], T.p2[:, 0:128], ["p2"], "tra")
+        ts(T.sel2[:, 0:1], T.ku[:, 0:1], cc(O16), A.add, ["ku", "o16"], "sel2")
+        for i in range(4):
+            over(i, "p3", 0, 128)
+        over(0, "p5", 128, 256)
+        turn(w[:, 640:768], T.p6[:, 0:128], ["p6"], "trb")
+        for i in range(8, 14):
+            sign(i)
+            if i > 8:
                 total_a(i - 1)
-        total_a(15)
-        for i in range(NV):
-            p = pe if i < 8 else po
-            ts(flags(i), T[p][:, 0:256], bound(i), A.is_gt, [p, "trs"], "fl%d" % i)
-            if i:
-                total_v(i - 1)
-        total_v(NV - 1)
-        cp(w[:, 768:768 + NV], T.sjv[:, 4608 + 127:4608 + 128 * NV:128], ["sc%d" % i for i in range(NV)], "rawv")
-        RAW = ["rawv"] + ["sc%d" % i for i in range(NV, 16)]
-        act(w[:, gin:gin + 32:2], raw, AF.Identity, RAW + ["even"], ["gin0"], scale=cc(EVEN))
-        act(w[:, gin + 1:gin + 32:2], raw, AF.Identity, RAW + ["nodd"], ["gin1"], scale=cc(NODD))
-        ts(mk, raw, 128.0, A.is_ge, RAW, "mk", -1000.0, A.mult)
-        tt(gm, raw, mk, A.add, RAW + ["mk"], "gm")
-        red(sm(40), w[:, 800:808], A.max, ["gm"], "sm40")
-        red(sm(41), w[:, 808:816], A.max, ["gm"], "sm41")
-        turn(w[:, gout:gout + 32], w[:, gin:gin + 32], ["gin0", "gin1"], "gout")
-        ts(w[:, bm:bm + 16], T.zero[:, 0:16], sm(40), A.add, ["zero", "sm40"], "bm0")
-        ts(w[:, bm + 16:bm + 32], T.zero[:, 0:16], sm(41), A.add, ["zero", "sm41"], "bm1")
-        tt(T.ch2[:, :], w[:, gout:gout + 16], w[:, gout + 16:gout + 32], A.add, ["gout"], "ch2")
-        turn(w[:, bmt:bmt + 32], w[:, bm:bm + 32], ["bm0", "bm1"], "bmt")
-        red(sm(42), w[:, bmt:bmt + 32], A.max, ["bmt"], "sm42", negate=True)
+        total_a(13)
+        for i in range(1, 4):
+            over(i, "p5", 128, 256)
+            total_v(i - 1)
+        over(14, "p7", 0, 256)
+        total_v(3)
+        over(15, "p7", 0, 256)
+        total_v(14)
+        for i in range(4, 8):
+            over(i, "p3", 0, 128)
+            if i == 4:
+                total_v(15)
+            over(i, "p5", 128, 256)
+            if i == 4:
+                cp(w[:, 782:784], T.sjv[:, 4608 + 1024 + 127:4608 + 1280:128], ["sc14", "sc15"], "rawv")
+        for i in range(4, 8):
+            total_v(i)
+        re_, ro = ["sc%d" % i for i in range(8)], ["rawv"] + ["sc%d" % i for i in range(8, 14)]
+        both = ((rawe, re_, 0), (rawo, ro, 1))
+        act(w[:, 792:800], rawo, AF.Sign, ro, ["mk1"], scale=-1.0, bias=127.5)
+        ts(w[:, 784:792], rawe, 128.0, A.is_lt, re_, "mk0")
+        for raw, rr, h in both:
+            ts(T.EO[:, 72 + 16 * h:88 + 16 * h:2], raw, cc(EVEN), A.mult, rr + ["even"], "gin0%d" % h, -500.0, A.add)
+        for raw, rr, h in both[::-1]:
+            act(T.EO[:, 73 + 16 * h:88 + 16 * h:2], raw, AF.Identity, rr + ["nodd"], ["gin1%d" % h], scale=cc(NODD), bias=-500.0)
+        for raw, rr, h in both:
+            tt(T.E1[:, 48 * h:48 * h + 8], raw, w[:, 784 + 8 * h:792 + 8 * h], A.mult, rr + ["mk%d" % h, "E1"], "gm%d" % h)
+        scan(T.EO[:, 0:72], T.E0[:, :], T.E1[:, :], ["gm0", "gm1", "E0a", "E0b", "E1"], "EO", -5000.0, A.add, A.max)
+        turn(w[:, 992:1024], T.EO[:, 72:104], ["gin00", "gin01", "gin10", "gin11"], "gout")
+        turn(w[:, 928:992], T.EO[:, 8:72], ["EO"], "bmt")
+        tt(T.ch2[:, :], w[:, 992:1008], w[:, 1008:1024], A.add, ["gout"], "ch2")
+        red(sm(42), w[:, 928:992], A.max, ["bmt"], "sm42", negate=True)
         return sm(42), "sm42"
 
     def listed(n, ch, ck, t, tk):
         q = n // 16
-        tr, trk = (T.tr1, "tr1") if n == 512 else (T.tr2, "tr2")
-        ts(T.gt[:, 0:q], ch[:, :], t, A.is_gt, [ck, tk], "gt")
-        ts(T.eq[:, 0:q], ch[:, :], t, A.is_equal, [ck, tk], "eq")
-        scan(T.ges[:, 1:q + 1], T.gt[:, 0:q], T.zero[:, 0:q], ["gt", "zero", "ges0"], "gs")
-        scan(T.ges[:, 37:q + 37], T.eq[:, 0:q], T.zero[:, 0:q], ["eq", "zero", "ges0"], "es")
-        ts(T.lt[:, 0:q], ch[:, :], t, A.is_lt, [ck, tk], "lt", 1024.0, A.mult)
-        ts(T.og[:, 0:2], T.ges[:, q:q + 37:36], cc(L33), A.add, ["gs", "es", "l33"], "og")
-        act(T.gj[:, 0:16], T.ps[:, 528:1056].indirect(T.og[:, 0:1]), AF.Identity, ["og"] + PS, ["gj", "sm31"], scale=-1.0, bias=n / 32.0, accum_out=sm(31))
-        act(T.gj[:, 32:64], T.ps[:, 0:528].indirect(T.og[:, 0:2]), AF.Identity, ["og"] + PS, ["gk", "sm32"], accum_out=sm(32))
-        ts(T.ngt[:, 0:q], ch[:, :], t, A.is_le, [ck, tk], "ngt")
-        tt(T.es2[:, 0:q], T.ges[:, 36:q + 36], T.lt[:, 0:q], A.add, ["es", "ges0", "lt"], "es2")
-        tt(T.trn[:, 0:q], T.ngt[:, 0:q], tr[:, :], A.mult, ["ngt", trk], "trn")
-        ts(T.me[:, 0:q], T.es2[:, 0:q], sm(32), A.add, ["es2", "sm32", "sm31"], "me", sm(31), A.min)
-        ts(T.y1[:, 0:q], T.es2[:, 0:q], sm(32), A.add, ["es2", "sm32", "sm31"], "y1", sm(31), A.is_ge)
-        tt(T.vi[:, 0:q], T.ges[:, 0:q], T.me[:, 0:q], A.add, ["gs", "ges0", "me"], "vi")
-        tt(T.mm[:, 0:q], T.y1[:, 0:q], T.trn[:, 0:q], A.mult, ["y1", "trn"], "mm")
-        tt(T.dd[:, 0:q], T.mm[:, 0:q], T.vi[:, 0:q], A.max, ["mm", "vi"], "dd")
+        D0, D1, es = T.D0, T.D1, T.D1[:, 3 * q + 5:6 * q + 5:3]
+        ts(T.GE[:, 32 - q:32], ch[:, :], t, A.is_gt, [ck, tk], "gt", U, A.mult)
+        ts(T.GE[:, 33:33 + q], ch[:, :], t, A.is_equal, [ck, tk], "eq", U, A.mult)
+        if n == 256:
+            ts(sm(31), t, U, A.mult, [tk, "br256"], "sm31", cc(BR2), A.add)
+        act(T.sg[:, 0:q], ch[:, :], AF.Sign, [ck, tk], ["sg"], scale=-1.0, bias=t)
+        scan(D1[:, 5:6 * q + 8:3], T.MK[:, 32 - q:33 + q], T.GE[:, 32 - q:33 + q], ["gt", "eq", "MK", "GEz", "sh"], "gs", cc(SH), A.mult, A.add)
+        ts(T.og[:, 0:3:2], D1[:, 3 * q + 2:6 * q + 6:3 * q + 3], 1024.0, A.mult, ["gs", "l64"], "og", cc(L64), A.add)
+        if n == 512:
+            act(T.gj[:, 0:16], T.ir[:, :].indirect(T.og[:, 0:1]), AF.Identity, ["og", "ir", "br512"], ["gj", "sm31"], scale=-U, bias=cc(BR1), accum_out=sm(31))
+        act(T.gj[:, 16:32], T.ir[:, :].indirect(T.og[:, 2:3]), AF.Relu, ["og", "ir", "be"], ["gk", "sm32"], scale=U, bias=cc(BE), accum_out=sm(32))
+        act(T.gj[:, 32:48], T.ir[:, :].indirect(T.og[:, 0:1]), AF.Relu, ["og", "ir", "ba"], ["gl", "sm33"], bias=cc(BA), accum_out=sm(33))
+        tt(T.es2[:, 0:q], es, T.sg[:, 0:q], A.add, ["gs", "sg"], "es2")
+        if n == 512:
+            fill(T.E1[:, :], -5000.0, "E1")
+            turn(T.ku[:, :], T.ks[:, 8:40], ["ks"], "ku")
+        else:
+            quant("v", 0, 128, T.tv, ["tv"], "qvv")
+        ts(D1[:, 1:3 * q:3], es, sm(32), A.add, ["gs", "sm32", "sm31"], "me", sm(31), A.min)
+        ts(D0[:, 1:3 * q:3], T.es2[:, 0:q], sm(32), A.add, ["es2", "sm32", "sm31"], "y1", sm(31), A.is_ge)
+        scan(T.DO[:, 0:3 * q], D0[:, 0:3 * q], D1[:, 0:3 * q], ["me", "y1", "trn", "gs", "D0a", "D0c", "D1z"], "dd", 0.0, A.mult, A.add)
         so, R, rk, val, vk, Tr = (T.osc1, T.R1, "R1", T.val1, "val1", T.Tr1) if n == 512 else (T.osc2, T.R2, "R2", T.val2, "val2", T.Tr2)
-        ts(so[:, :], T.dd[:, 0:q], cc(O16), A.add, ["dd", "o16"], "so")
+        ts(so[:, :], T.DO[:, 2:3 * q:3], 1024.0, A.mult, ["dd", "sm33"], "so", sm(33), A.add)
         cp(R[:, :].indirect(so[:, :]), val[:, :], ["so", vk], rk)
         m = n // 2
         turn(Tr[:, 0:m], R[:, 0:m], [rk], rk + "a")
@@ -444,12 +465,11 @@ def rank_program(g, core, T, topo):
     def pick(c, tr, sel, n, k, add, r, o, w):
         ts(T[o][:, c:c + 16], T[tr][:, 0:n].indirect(T[sel][:, 0:1]), k, A.mult, r, w, add, A.add)
 
-    def gather(dst, h, t, src, rs, o, eng, w):
-        a = (T[dst][:, 512 * h + t:512 * h + 512:4], src[:, :].indirect(T[o][:, 16 * t + 8 * h:16 * t + 8 * h + 8]))
+    def gather(out, win, off, rs, eng, w):
         if eng == "a":
-            act(*a, AF.Copy, rs, [w])
+            act(out, win.indirect(off), AF.Copy, rs, [w])
         else:
-            cp(*a, rs, w)
+            cp(out, win.indirect(off), rs, w)
 
     def relu(dst, h, b, p, eng, w):
         o, i = T[dst][:, 512 * h + b:512 * h + 512:4], T[p][:, 0:128]
@@ -458,63 +478,61 @@ def rank_program(g, core, T, topo):
         else:
             ts(o, i, 0.0, A.max, [p], w, 0.03125, A.mult)
 
-    def four(n):
-        return ["%s%d" % (n, t) for t in range(4)]
-
-    t1, k1 = search(512, "p0", "p1", (("p2", 256), ("p3", 256)), 64, jobs1())
-    pick_s(0)
+    t1, k1 = search()
     listed(512, T.ch1, "ch", t1, k1)
-    pick_s(1)
-    pick_s(2)
-    lin(cc(L16), "l16", LANE, 16.0, 0.0)
-    lin(cc(LM8), "lm8", LANE, 1.0, -8.0)
+    for k in range(3):
+        pick_s(k)
     lin(cc(EVEN), "even", ODD, 1.0, -1.0)
     lin(cc(NODD), "nodd", ODD, -1.0, 0.0)
-    act(cc(L7), cc(M8), AF.Identity, ["m8", "lm8"], ["l7"], scale=8.0, bias=cc(LM8))
-    act(T.tr2[:, :], T.kr2[:, :], AF.Identity, ["kr2", "l16"], ["tr2"], bias=cc(L16))
-    act(cc(SO7), cc(L7), AF.Identity, ["l7", "o16"], ["so7"], scale=16.0, bias=cc(O16))
+    lin(cc(NO16), "no16", ODD, -16.0, 0.0)
+    lin(cc(BR2), "br256", ODD, 8 * U, 1128 * U)
+    act(T.D1[:, 0:48:3], T.tr2[:, :], AF.Identity, ["tr2"], ["trn"], scale=U)
     dma("s", T.tv[:, :], T.v[:, :], w=["tv"])
     dma("s", codes(T.qZ[:, :]), T.zc[:, :], w=["qZ"])
     dma("s", T.sZ[:, :], T.zs[:, :], w=["sZ"])
-    dma("s", T.xf[:, :], T.x[:, :], w=["xf0"])
-    for t in range(4):
-        pick(16 * t, "Tr1", "sel1", 512, 4.0, 1024.0 + t, L1T, "o1", "o1_%d" % t)
+    pick(0, "Tr1", "sel1", 512, 1.0, 256.0, L1T, "o1", "o1")
     FA, FB, HA, HB = four("tfa"), four("tfb"), four("tha"), four("thb")
+
+    def gather_f(h, t, eng):
+        gather(T.tf[:, 512 * h + t:512 * h + 512:4], T.wn[:, 896 * t:896 * t + 512], T.o1[:, 8 * h:8 * h + 8], ["xp%d" % t, "o1"], eng, (FA, FB)[h][t])
+    fill(T.E0[:, 8:57:48], 1000.0, "E0a", ["E0"])
     for t in range(4):
-        gather("tf", 0, t, T.tx, X + ["o1_%d" % t], "o1", "avav"[t], FA[t])
+        gather_f(0, t, "avav"[t])
     for t in range(3):
-        gather("tf", 1, t, T.tx, X + ["o1_%d" % t], "o1", "ava"[t], FB[t])
+        gather_f(1, t, "ava"[t])
     quant("F", 0, 128, T.tf, FA, "qFa")
-    gather("tf", 1, 3, T.tx, X + ["o1_3"], "o1", "v", FB[3])
+    gather_f(1, 3, "v")
+    fill(T.E0[:, 24:25], -3000.0, "E0b", ["E0"])
     quant("F", 128, 128, T.tf, FB, "qFb")
     PA, PB = ["p2", "p3", "p4", "p5"], ["p6", "p7", "p0", "p1"]
     for b in range(4):
-        mm(PA[b], 128, "W", 128 * b, "F", 0, ["qW", "sW", "qFa"])
+        do("t", P.matmul_mx, T[PA[b]][:, 0:128], T.qW[:, 128 * b:128 * b + 128], T.sW[:, 128 * b:128 * b + 128], T.qF[:, 0:128], T.sF[:, 0:128], True, True,
+           r=["qW", "sW", "qFa"], w=[PA[b], PA[b] + "s"])
     for b in range(4):
         mm(PB[b], 128, "W", 128 * b, "F", 128, ["qW", "sW", "qFb"])
     for b in range(4):
         relu("th", 0, b, PA[b], "avav"[b], HA[b])
     relu("th", 1, 0, PB[0], "a", HB[0])
-    relu("th", 1, 1, PB[1], "v", HB[1])
     quant("H", 0, 128, T.th, HA, "qHa")
+    relu("th", 1, 1, PB[1], "v", HB[1])
+    for p, k in (("p2", 0), ("p3", 1)):
+        mm(p, 128, "r2", 128 * k, "H", 0, ["qHa", "qr2%d" % k, "sr2%d" % k])
     relu("th", 1, 2, PB[2], "a", HB[2])
     relu("th", 1, 3, PB[3], "v", HB[3])
     quant("H", 128, 128, T.th, HB, "qHb")
-    dma("s", T.txh[:, :], T.tf[:, :], r=FA + FB, w=["txh"])
-    dma("g", T.txh[:, :], T.th[:, :], r=HA + HB, w=["txh"], accum_op=A.add)
-    for p, k in (("p2", 0), ("p4", 1), ("p3", 2), ("p5", 2)):
-        mm(p, 256, "r2", 128 * k, "H", 0, ["qHa", "qHb", "qr2%d" % k, "sr2%d" % k])
-    ts(T.sel2[:, 0:1], cc(LB), 112.0, A.mult, ["lb", "so7"], "sel2", cc(SO7), A.add)
-    fill(T.R2[:, 0:144], 0.0, "R2")
-    ts(T.ip[:, 3:4], T.ip[:, 1:2], 2, A.logical_shift_right, ["ip1"], "ip3")
-    ts(T.ip[:, 4:5], T.ip[:, 1:2], 3, A.bitwise_and, ["ip1"], "ip4")
-    quant("E", 0, 128, T.te, ["te0"], "qE0", 0)
-    t2, k2 = ranks("p2", "p4", "p5", "p3")
+    for p, k, c in (("p4", 2, 0), ("p5", 1, 128), ("p6", 0, 128), ("p7", 2, 0)):
+        mm(p, 256 - c, "r2", 128 * k, "H", c, ["qHa", "qHb", "qr2%d" % k, "sr2%d" % k])
+    for t in range(4):
+        plane(T.hp[:, 256 * t:256 * t + 256], T.th[:, t:1024:4], 256, [HA[t], HB[t]], "hp%d" % t)
+    iota("te", [[0, 528]], 0, w="tez")
+    iota("ones", [[0, 128]], 1)
+    select(T.te[:, 3:515:4], T.ones[:, :], [[1, 128]], A.is_equal, 0, -1, ["ones", "tez"], "te")
+    t2, k2 = ranks()
     listed(256, T.ch2, "ch2", t2, k2)
+    act(T.Mr[:, :], T.ir[:, 0:528], AF.Identity, ["ir", "no16"], ["Mr"], bias=cc(NO16))
+    pick(64, "Tr2", "sel2", 256, 1.0, 0.0, L2T, "o2", "o2")
     for t in range(4):
-        pick(16 * t, "Tr2", "sel2", 256, 4.0, float(t), L2T, "o2", "o2_%d" % t)
-    for t in range(4):
-        gather("tg", 0, t, T.th, HA + HB + ["o2_%d" % t], "o2", "avav"[t], "tg%d" % t)
+        gather(T.tg[:, t:512:4], T.hp[:, 256 * t:256 * t + 256], T.o2[:, 64:72], ["hp%d" % t, "o2"], "avav"[t], "tg%d" % t)
     quant("G", 0, 128, T.tg, four("tg"), "qG")
 
     far = [d for d in range(N) if d != rank and topo.die(T.cores[d]) != topo.die(core)]
@@ -526,17 +544,15 @@ def rank_program(g, core, T, topo):
             masks[d] = sum(1 << x for x in (e[4 * j + o], e[4 * j + o + 2]))
     order = sorted(masks, key=lambda d: (d - rank) % N)
 
-    def swap(a, b, sem):
-        own = slice(16 * rank, 16 * rank + 16)
+    def swap(a, src0, dst0, sem):
         tok = "q" + a
-        dma("s", codes(T["q" + b][:, own]), codes(T["q" + a][:, own]), r=[tok], w=[tok + "o"])
-        dma("s", T["s" + b][:, own], T["s" + a][:, own], r=[tok], w=[tok + "p"])
         learn("g", wr[tok])
         for x in "qs":
             tr = []
             for d in order:
                 rid, pid, _ = topo.addr(T.cores[d])
-                src, dst = T[x + a][:, 16 * d:16 * d + 16], T[x + b][:, own]
+                i, o = src0 + 16 * ((d - rank - 1) % N), dst0 + 16 * ((rank - d - 1) % N)
+                src, dst = T[x + a][:, i:i + 16], T[x + a][:, o:o + 16]
                 if x == "q":
                     src, dst = codes(src), codes(dst)
                 tr.append(RemoteDMATransfer(dst_ids=[DstId(rid=rid, pnc=pid)], dma_engine_mask=masks[d], remote_sem=T.sem[sem], src=src, dst=dst))
@@ -544,64 +560,82 @@ def rank_program(g, core, T, topo):
         total[sem] = 4 * (N - 1)
         wr[tok + "r"] = [("far", sem, total[sem], {})]
         total["sent"] = total.get("sent", 0) + 4 * (N - 1)
-    swap("G", "L", "down")
-    cp(cc(LQ), T.ip[:, 3:4], ["ip3"], "lq")
-    cp(cc(LR), T.ip[:, 4:5], ["ip4"], "lr")
-    pick(64, "Tr1", "sel1", 512, 1.0, 256.0, L1T, "o1", "o1c")
-    pick(64, "Tr2", "sel2", 256, 1.0, 0.0, L2T, "o2", "o2c")
-    ts(cc(LQ4), cc(ODD), -4.0, A.mult, ["odd", "lq"], "lq4", cc(LQ), A.add)
-    ts(cc(L4), cc(LR), 1024.0, A.add, ["lr"], "l4")
-    ts(T.sel3[:, 0:1], cc(LB), 496.0, A.mult, ["lb", "so16"], "sel3a", cc(SO), A.add)
-    ts(T.orep[:, 0:33], T.irep[:, :], cc(LQ4), A.add, ["irep", "lq4"], "orep", 127.0, A.min)
-    act(T.L1r[:, :], T.ir[:, :].indirect(T.o1[:, 64:80]), AF.Identity, ["ir", "o1c"], ["L1r"])
-    act(T.olr[:, :], T.L1r[:, :].indirect(T.o2[:, 64:72]), AF.Identity, ["L1r", "o2c"], ["olr"])
-    dma("s", T.ol[:, :], T.olr[0:128:16, :], r=["olr"], w=["ol"])
-    act(T.gap3[:, :], T.olr[:, :].indirect(T.orep[:, 0:33]), AF.Identity, ["olr", "orep"], ["gap3"], bias=-256.0)
-    ts(T.sel3[:, 1:2], T.sel3[:, 0:1], 256.0, A.add, ["sel3a"], "sel3b")
-    base(0, 0)
-    quant("E", 128, 128, T.te, ["te1"], "qE1", 512)
-    base(0, 1)
-    quant("E", 256, 128, T.te, ["te2"], "qE2", 1024)
-    base(1, 0)
-    quant("E", 384, 128, T.te, ["te3"], "qE3", 1536)
-    base(1, 1)
+    swap("G", 0, 128, "down")
+    for t in range(4):
+        pick(16 * t, "Tr2", "sel2", 256, 4.0, float(t), L2T, "o2", "o2_%d" % t)
+    act(T.L1r[:, :], T.ir[:, 0:512].indirect(T.o1[:, 0:16]), AF.Identity, ["ir", "o1"], ["L1r"])
+    act(T.olr[:, :], T.L1r[:, :].indirect(T.o2[:, 64:72]), AF.Identity, ["L1r", "o2"], ["olr"])
+    turned = 16 * (N - 1 - rank)
+    dma("s", T.ol[:, 0:128 - turned], T.olr[0:128:16, turned:128], r=["olr"], w=["ol"])
+    if turned:
+        dma("s", T.ol[:, 128 - turned:128], T.olr[0:128:16, 0:turned], r=["olr"], w=["ol2"])
+    for t in range(4):
+        gather(T.txg[:, 128 * t:128 * t + 128], T.tf[:, :], T.o2[:, 16 * t:16 * t + 8], FA + FB + ["o2_%d" % t], "a", "txg%d" % t)
+    cp(T.sel3[:, 0:1], T.kt[:, 96:97], ["kt2"], "sel3a")
+    ts(T.o1[:, 16:32], T.o1[:, 0:16], cc(O16), A.add, ["o1", "o16"], "o1s")
+    cp(T.M1[:, :].indirect(T.o2[:, 64:72]), T.v3[:, :], ["o2", "v3"], "M1")
+    ts(T.sel3[:, 1:2], T.kt[:, 96:97], 256.0, A.add, ["kt2"], "sel3b")
+    cp(T.Mr[:, :].indirect(T.o1[:, 16:32]), T.M1[:, :], ["o1s", "M1"], "Mr")
     for b in range(4):
-        mm(PA[b], 128, "Z", 128 * b, "L", 0, ["qZ", "sZ", "qGo", "qGp", "qGr"])
+        quant("E", 128 * b, 128, T.te, ["te", "tez"], "qE%d" % b, 3 - b)
+    for b in range(4):
+        mm(PA[b], 128, "Z", 128 * b, "G", 112, ["qZ", "sZ", "qG", "qGr"])
     for b in range(4):
         relu("tt", 0, b, PA[b], "avav"[b], "tt%d" % b)
-    quant("T", 0, 128, T.tt, four("tt"), "qT")
-    swap("T", "U", "up")
-    turn(T.Tr3[:, 0:512], T.gap3[:, 0:512], ["gap3"], "Tr3a")
-    turn(T.Tr3[:, 512:1024], T.gap3[:, 16:528], ["gap3"], "Tr3b")
-    base(2, 0)
-    ts(T.o3[:, :], T.Tr3[:, :].indirect(T.sel3[:, 0:2]), 4.0, A.mult, ["Tr3a", "Tr3b", "sel3a", "sel3b", "l4"], "o3", cc(L4), A.add)
-    act(T.txg[:, :], T.tx[:, :].indirect(T.o3[:, :]), AF.Copy, X + ["o3"], ["txg"])
-    base(2, 1)
-    quant("v", 0, 128, T.tv, ["tv"], "qvv")
-    for t, h in ((3, 0), (3, 1)):
-        base(t, h)
+    quant("T", 112, 128, T.tt, four("tt"), "qT", 0)
+    swap("T", 128, 0, "up")
+    turn(T.TrM[:, 0:512], T.Mr[:, 0:512], ["Mr"], "TrMa")
+    turn(T.TrM[:, 512:1024], T.Mr[:, 16:528], ["Mr"], "TrMb")
+    for t in range(4):
+        tt(T.wn[:, 896 * t + 512:896 * t + 768], T.tf[:, t:1024:4], T.hp[:, 256 * t:256 * t + 256], A.add, [FA[t], FB[t], "hp%d" % t], "xh%d" % t)
+        if t == 0:
+            cp(T.oM[:, :], T.TrM[:, :].indirect(T.sel3[:, 0:2]), ["TrMa", "TrMb", "sel3a", "sel3b"], "oM")
     for b in range(4):
-        mm(PA[b], 128, "E", 128 * b, "U", 0, ["qE%d" % b, "qTo", "qTp", "qTr"])
-    for b in range(4):
-        tt(T.thn[:, b:512:4], T[PA[b]][:, 0:128], T.tg[:, b:512:4], A.add, [PA[b], "tg%d" % b], "thn%d" % b)
-    for b in range(4):
-        tt(T.txn[:, b:512:4], T.txg[:, b:512:4], T.thn[:, b:512:4], A.add, ["txg", "thn%d" % b], "txn%d" % b)
-    cp(T.xf[:, :].indirect(T.o3[:, :]), T.txn[:, :], ["o3"] + four("txn"), "xf")
-    for h in range(4):
-        quant("N", 128 * h, 128, T.xf, ["xf"], "qN%d" % h)
-        mm(PB[h], 128, "v", 0, "N", 128 * h, ["qvv", "qN%d" % h])
-    for h in range(4):
-        o, i = T.ysb[:, 128 * h:128 * h + 128], T[PB[h]][:, 0:128]
-        if h % 2 == 0:
-            act(o, i, AF.Copy, [PB[h]], ["y%d" % h])
+        mm(PA[b], 128, "E", 128 * b, "T", 0, ["qE%d" % b, "qT", "qTr"])
+
+    def hn(b):
+        tt(T.thn[:, 128 * b:128 * b + 128], T[PA[b]][:, 0:128], T.tg[:, b:512:4], A.add, [PA[b], "tg%d" % b], "thn%d" % b)
+
+    def xn(b):
+        tt(T.wn[:, 896 * b + 768:896 * b + 896], T.txg[:, 128 * b:128 * b + 128], T.thn[:, 128 * b:128 * b + 128], A.add, ["txg%d" % b, "thn%d" % b], "xn%d" % b)
+
+    def back(h, t, eng):
+        gather(T.xf[:, 1024 * h + t:1024 * h + 1024:4], T.wn[:, 896 * t:896 * t + 896], T.oM[:, 16 * h:16 * h + 16],
+               ["oM", "xp%d" % t, "xh%d" % t, "xn%d" % t], eng, "xf%d%d" % (h, t))
+
+    def result(c):
+        quant("N", 128 * c, 128, T.xf, four("xf%d" % (c // 2)), "qN%d" % c)
+        mm(PB[c], 128, "v", 0, "N", 128 * c, ["qvv", "qN%d" % c])
+
+    def out(c, eng):
+        o, i = T.ysb[:, 128 * c:128 * c + 128], T[PB[c]][:, 0:128]
+        if eng == "a":
+            act(o, i, AF.Copy, [PB[c]], ["y%d" % c])
         else:
-            cp(o, i, [PB[h]], "y%d" % h)
+            cp(o, i, [PB[c]], "y%d" % c)
+
+    def scales(q, j):
+        dma(q, T.osc[4 * j:4 * j + 4, :], T.sN[32 * j:32 * j + 4, :], r=four("qN"), w=["osc%d" % j])
+    for f, b in ((hn, 0), (hn, 1), (xn, 0), (hn, 2), (xn, 1), (hn, 3), (xn, 2), (xn, 3)):
+        f(b)
+    for h, t, eng in ((0, 0, "a"), (0, 1, "a"), (0, 2, "v"), (0, 3, "v"), (1, 0, "a"), (1, 1, "a"), (1, 2, "a")):
+        back(h, t, eng)
+    result(0)
+    result(1)
     dma("s", T.oc[:, 0:1024], codes(T.qN[:, 0:256]), r=["qN0", "qN1"], w=["oc0"])
-    dma("s", T.oc[:, 1024:2048], codes(T.qN[:, 256:512]), r=["qN2", "qN3"], w=["oc1"])
-    for j in range(4):
-        dma("s", T.osc[4 * j:4 * j + 4, :], T.sN[32 * j:32 * j + 4, :], r=["qN%d" % h for h in range(4)], w=["osc%d" % j])
+    back(1, 3, "v")
+    out(0, "v")
+    result(2)
+    result(3)
+    out(1, "a")
     dma("a", T.y[:, 0:256], T.ysb[:, 0:256], r=["y0", "y1"], w=["yo0"])
-    dma("s", T.y[:, 256:512], T.ysb[:, 256:512], r=["y2", "y3"], w=["yo1"])
+    dma("s", T.oc[:, 1024:2048], codes(T.qN[:, 256:512]), r=["qN2", "qN3"], w=["oc1"])
+    for j in range(3):
+        scales("s", j)
+    out(2, "a")
+    out(3, "v")
+    dma("a", T.y[:, 256:512], T.ysb[:, 256:512], r=["y2", "y3"], w=["yo1"])
+    scales("a", 3)
     for s in sorted(total):
         if seen.get(s, 0) < total[s]:
             g.wait_ge(T.sem[s], total[s])

@@ -5,12 +5,12 @@ F8, U8, BF, F32, I32, U16 = "float8_e4m3fn_x4", "uint8", "bfloat16", "float32", 
 SCRATCH = {}
 for _d, _l in (
     (BF, "tu1 512 tu2 512 tv 512 tx 2048 xf 2048 wn 3584 tf 1024 th 1024 hp 1024 tg 512 tt 512 thn 512 txg 512 ones 128 te 528 "
-         "val1 512 val2 256 sj 512 sk 512 sjv 7424 R1 4896 R2 2464 Tr1 512 Tr2 256 mul 448 br 296"),
-    (F32, "tbr 128 tbt 128 kr 128 kt 128 ks 48 ku 32 arow 8 ar 8 X1 32 W2 96 X2 96 crow 8 ft 16 cb 8 ir 1024 tr1 32 tr2 16 c 32 gj 64 l64 32 "
-          "sm 64 srow 1024 ch1 32 ch2 16 GE 72 MK 72 sg 32 es2 32 D0 96 D1 200 DO 96 E0 72 E1 72 EO 104 "
+         "val1 256 RS 592 upd 544 val2 256 sj 512 sk 512 sjv 7424 R1 4896 R2 2464 Tr1 512 Tr2 256 mul 448 br 296"),
+    (F32, "tbr 128 tbt 128 kr 128 kt 128 ks 48 ku 32 arow 8 ar 8 X1 32 C1 32 W2 96 X2 96 crow 8 ft 16 cb 8 ir 1280 tr1 16 P0 128 P1 272 PO 128 tr2 16 c 40 gj 64 l64 32 "
+          "sm 64 srow 1024 ch1 32 ch2 16 GE 72 MK 72 sg 32 es2 32 D0 48 D1 104 DO 48 E0 72 E1 72 EO 104 "
           "L1r 256 olr 128 M1 256 v3 128 Mr 528 TrM 1024 ysb 512"),
     (I32, "ipick 24"),
-    (U16, "opick 24 off 2 og 4 osc1 32 osc2 16 o1 32 o2 80 oM 32 sel1 2 sel2 2 sel3 2")):
+    (U16, "opick 24 off 2 og 4 osc1 16 osc2 16 o1 64 o2 80 oM 32 sel1 2 sel2 2 sel3 2")):
     _l = _l.split()
     for _i in range(0, len(_l), 2):
         SCRATCH[_l[_i]] = ("sbuf", [128, int(_l[_i + 1])], _d)
@@ -127,8 +127,9 @@ def rank_program(g, core, T, topo):
         return ["%s%d" % (n, t) for t in range(4)]
 
     dma("s", T.tu1[:, :], T.u1[:, :], w=["tu1"])
-    for j in range(4):
-        dma("a" if j % 2 == 0 else "s", T.tx[:, 512 * j:512 * j + 512], T.x[:, 512 * j:512 * j + 512], w=["tx%d" % j])
+    dma("s", T.tx[:, 0:1024], T.x[:, 0:1024], w=["tx0", "tx1"])
+    dma("s", T.tx[:, 1024:1536], T.x[:, 1024:1536], w=["tx2"])
+    dma("s", T.tx[:, 1536:2048], T.x[:, 1536:2048], w=["tx3"])
     X = four("tx")
 
     def iota(n, pattern, base, cm=0, at=0, w=None):
@@ -148,15 +149,22 @@ def rank_program(g, core, T, topo):
     iota("kr", [[1, 2], [0, 16]], 0, at=32, w="kr1")
     iota("arow", [[2, 8]], 0)
     iota("ipick", [[16, 2], [32, 4], [0, 2]], 0, at=8, w="ipick2")
-    iota("kr", [[16, 2], [32, 8], [256, 2]], 0, at=64, w="kr2")
+    iota("kr", [[0, 2], [32, 4], [128, 2]], 0, at=64, w="kr2")
+    iota("kr", [[0, 2], [32, 4], [128, 2]], 16, at=80, w="kr2b")
     iota("kr", [[16, 2], [32, 8], [512, 2]], 0, at=96, w="kr3")
     iota("ks", [[0, 5], [32, 4], [128, 2]], 0, at=8 - (rank + 1) % N)
-    iota("tr1", [[1, 32]], 512, 32)
-    iota("ir", [[1, 1024]], 0)
-    iota("val1", [[1, 32], [32, 16]], -256)
+    iota("tr1", [[1, 16]], 544, 16)
+    iota("P1", [[0, 272]], 0, w="P1z")
+    iota("ir", [[1, 1280]], 0)
+    iota("P0", [[0, 128]], 0, w="P0z")
+    iota("MK", [[0, 72]], 1, w="MK1")
+    iota("val1", [[2, 16], [32, 16]], -255)
     for t in range(4):
         plane(T.wn[:, 896 * t:896 * t + 512], T.tx[:, t:2048:4], 512, X, "xp%d" % t)
+    iota("E0", [[0, 72]], 0)
+    iota("E1", [[0, 72]], -5000)
     iota("tr2", [[1, 16]], 256, 16)
+    iota("R2", [[0, 144]], 0)
     iota("val2", [[1, 16], [16, 16]], 0)
     iota("M1", [[1, 256]], 512)
     iota("v3", [[1, 128]], 768)
@@ -168,6 +176,7 @@ def rank_program(g, core, T, topo):
     fill(T.X1[:, :], 0.0, "X1z")
     scan(br[:, 0:146], T.mul[:, 0:146], T.mul[:, 0:146], ["mul0"], "bn", -2.0 ** 76, A.mult, A.min)
     scan(br[:, 146:290], T.mul[:, 146:290], T.mul[:, 290:434], ["mul1", "mul2"], "bp", 2.0 ** -71, A.mult, A.mult)
+    fill(T.C1[:, :], 0.0, "C1z")
     fill(T.W2[:, :], 0.0, "W2z")
     fill(T.ft[:, :], 0.0, "ftz")
     B = ["bn", "bp"]
@@ -181,7 +190,8 @@ def rank_program(g, core, T, topo):
     turn(T.tbt[:, :], T.tbr[:, :], ["tb%s%d" % (x, h) for x in "abcd" for h in range(2)], "tbt")
     B1, T8, QL, PL = (T.tbt[:, 32 * j:32 * j + 1] for j in range(4))
     LANE, ODD = T.kt[:, 0:1], T.kt[:, 32:33]
-    NB1, LP1, CN, CP, L33, O16, EVEN, NODD, L2, Z12, M8, D6, CB, CB6, L16, Z14, NO16, SQ, S0, SH, L64, BA, BE, BR1, BR2 = range(25)
+    (NB1, LP1, CN, CP, L33, O16, EVEN, NODD, L2, Z12, M8, D6, CB, CB6, L16, Z14, NO16, SQ, S0, SH, L64, BA, BE, BR1, BR2, BA2,
+     O4, BE2, L8, O8, SG, CC, LX, LZ) = range(34)
     W2 = T.W2
     WT = ["W2z"]
     for k, (o, i, s) in enumerate(((W2[:, 0:30:2], br[:, 61:76], -1.0), (W2[:, 30:32], br[:, 75:77], -1.0), (W2[:, 32:48:2], br[:, 69:77], -1.0),
@@ -190,24 +200,21 @@ def rank_program(g, core, T, topo):
         act(o, i, AF.Identity, B + ["W2z"], ["W2%d" % k], scale=s)
         WT.append("W2%d" % k)
     K17 = 2.0 ** 17 - 1
-    fill(T.D0[:, 0:96:3], 0.0, "D0a")
-    fill(T.D0[:, 2:96:3], 1.0, "D0c")
-    fill(T.MK[:, :], 1.0, "MK1")
-    ts(cc(NB1), B1, -1.0, A.mult, ["tbt"], "nb1")
-    ts(T.X1[:, 19:32:2], br[:, 153:256:17], PL, A.mult, B + ["tbt", "X1z"], "X1a", -2.0 ** 16 * K17, A.mult)
-    ts(T.X1[:, 0:14:2], br[:, 34:137:17], QL, A.mult, B + ["tbt", "X1z"], "X1b", 2.0 ** 16 * K17, A.mult)
-    ts(T.X1[:, 17:18], PL, -2.0 ** -47, A.mult, ["tbt", "X1z"], "X1c", T8, A.subtract)
-    ts(T.X1[:, 14:15], QL, -2.0 ** -45, A.mult, ["tbt", "X1z"], "X1d")
-    cp(T.X1[:, 15:16], T8, ["tbt", "X1z"], "X1e")
-    X1T = ["X1" + x for x in "zabcde"]
-    quant("u1", 0, 128, T.tu1, ["tu1"], "qu1")
     ts(cc(Z12), LANE, 0.0, A.is_equal, ["lane"], "z12", 12.0, A.mult)
     ts(cc(Z14), LANE, 15.0, A.is_equal, ["lane"], "z14", 14.0, A.mult)
+    ts(cc(NB1), B1, -1.0, A.mult, ["tbt"], "nb1")
+    X1T = ["X1" + x for x in "zabcde"]
+    quant("u1", 0, 128, T.tu1, ["tu1"], "qu1")
+    ts(T.ar[:, :], T.arow[:, :], cc(Z12), A.max, ["arow", "z12", "z14"], "ar", cc(Z14), A.max)
+    ts(cc(M8), LANE, 8.0, A.is_ge, ["lane"], "m8", 4.0, A.mult)
     cp(words(T.qr1[:, :]), words(T.qu1[:, :]).indirect(T.opick[:, 0:8]), ["qu1", "opick"], "qr1")
 
-    def lin(out, w, src, k, add):
-        act(out, src, AF.Identity, ["lane"], [w], scale=k, bias=add)
+    def lin(out, w, src, k, add, r=()):
+        act(out, src, AF.Identity, ["lane"] + list(r), [w], scale=k, bias=add)
     lin(cc(L2), "l2", LANE, 2.0, 0.0)
+    lin(T.C1[:, 14:15], "C1a", LANE, 2.0, 0.0, ["C1z"])
+    lin(T.C1[:, 15:16], "C1b", LANE, 2.0, 32.0, ["C1z"])
+    lin(T.C1[:, 17:18], "C1c", LANE, 0.0, 32.0, ["C1z"])
     lin(cc(CN), "cn", LANE, 0.0625, -1.9375)
     lin(cc(CP), "cp", LANE, 0.0625, 1.0625)
     lin(cc(CB), "cbl", LANE, -0.9375, -0.9375)
@@ -225,11 +232,6 @@ def rank_program(g, core, T, topo):
     act(T.crow[:, 5:6], br[:, 98:99], AF.Identity, B, ["crow1"], scale=-1.0)
     act(T.cb[:, 0:2], T.cb[:, 2:4], AF.Identity, ["cb1"], ["cb0"], scale=0.0625)
     U = 2.0 ** -10
-    act(cc(SQ), LANE, AF.Square, ["lane"], ["sq"], bias=-0.5)
-    lin(cc(L33), "l33", LANE, -64.0, 960.0)
-    lin(cc(BA), "ba", LANE, 64.0, -1024.0)
-    lin(cc(BE), "be", LANE, 64.0 * U, -1.0)
-    act(cc(S0), cc(SQ), AF.Identity, ["sq"], ["s0"], scale=-32 * U, bias=8 * U)
 
     def gap(k):
         if k < 2:
@@ -240,33 +242,48 @@ def rank_program(g, core, T, topo):
                 dma("s", codes(T.qW[:, :]), T.wc[:, :], w=["qW"])
                 dma("s", T.sW[:, :], T.ws[:, :], w=["sW"])
         elif k == 2:
-            act(cc(SH), ODD, AF.Identity, ["lane", "s0"], ["sh"], scale=8 * U, bias=cc(S0))
-            lin(cc(BR1), "br512", ODD, 0.5 * U, 496 * U)
+            act(cc(SQ), LANE, AF.Square, ["lane"], ["sq"])
+            lin(cc(O8), "o8", ODD, 8.0, 0.0)
+            lin(cc(S0), "s0", LANE, -620 * U, 320 * U)
+            lin(cc(BE), "be512", LANE, 40.0 * U, -640 * U)
         elif k == 3:
-            act(cc(L64), cc(SH), AF.Identity, ["sh", "l33"], ["l64"], scale=-1024.0, bias=cc(L33))
-            act(T.GE[:, 32:33], cc(SH), AF.Identity, ["sh"], ["GEz"])
+            act(cc(SG), ODD, AF.Identity, ["lane", "s0"], ["sh512"], scale=8 * U, bias=cc(S0))
+            act(cc(BR1), cc(SQ), AF.Identity, ["sq", "o8"], ["br512"], scale=20.0, bias=cc(O8))
+            lin(cc(L64), "l64", LANE, -40.0, 1240.0)
+            lin(cc(BA2), "ba512", LANE, -80.0, 0.0)
         elif k == 4:
             act(cc(CB6), cc(D6), AF.Identity, ["d6"], ["cb6"], scale=-8.0)
-            act(T.D1[:, 2:3], cc(SH), AF.Identity, ["sh"], ["D1z"])
+            act(cc(CC), cc(BR1), AF.Identity, ["br512"], ["cc"], scale=U, bias=4736 * U)
+            act(cc(LX), cc(SG), AF.Identity, ["sh512", "l64"], ["lx"], scale=-1024.0, bias=cc(L64))
+            act(T.P1[:, 4:128:8], T.tr1[:, :], AF.Identity, ["tr1", "P1z"], ["P1b"], scale=U / 2)
         elif k == 5:
             act(T.cb[:, 6:8], T.arow[:, 0:2], AF.Identity, ["arow", "cb6"], ["cb3"], scale=0.5, bias=cc(CB6))
-            lin(cc(O16), "o16", ODD, 16.0, 0.0)
+            act(T.GE[:, 32:33], cc(SG), AF.Identity, ["sh512"], ["GEz"], bias=-640 * U)
+            lin(cc(L8), "l8", LANE, 660.0, -320.0)
         elif k == 6:
-            act(T.D1[:, 0:96:3], T.tr1[:, :], AF.Identity, ["tr1"], ["trn"], scale=U)
+            act(T.P1[:, 7:8], cc(SG), AF.Identity, ["sh512", "P1z"], ["P1a"])
+            act(T.P1[:, 5:128:8], T.tr1[:, :], AF.Identity, ["tr1", "P1z"], ["P1c"], scale=0.0, bias=U / 2)
+            act(cc(LZ), ODD, AF.Identity, ["lane", "l8"], ["lz"], scale=-8.0, bias=cc(L8))
 
     R = ["qr1", "sr1"]
-    for j in range(4):
+    for j in range(2):
         quant("x", 128 * j, 128, T.tx, ["tx%d" % j], "qx%d" % j)
+    ts(T.X1[:, 19:32:2], br[:, 153:256:17], PL, A.mult, B + ["tbt", "X1z"], "X1a", -2.0 ** 16 * K17, A.mult)
+    ts(T.X1[:, 0:14:2], br[:, 34:137:17], QL, A.mult, B + ["tbt", "X1z"], "X1b", 2.0 ** 16 * K17, A.mult)
+    for j in range(2, 4):
+        quant("x", 128 * j, 128, T.tx, ["tx%d" % j], "qx%d" % j)
+    ts(T.X1[:, 17:18], PL, -2.0 ** -47, A.mult, ["tbt", "X1z"], "X1c", T8, A.subtract)
+    ts(T.X1[:, 14:15], QL, -2.0 ** -45, A.mult, ["tbt", "X1z"], "X1d")
+    cp(T.X1[:, 15:16], T8, ["tbt", "X1z"], "X1e")
     QX = four("qx")
     mm("p2", 256, "r1", 0, "x", 0, QX[0:2] + R)
     mm("p3", 128, "r1", 0, "x", 256, QX[2:3] + R)
     mm("p4", 128, "r1", 0, "x", 384, QX[3:4] + R)
-    mm("p0", 384, "r1", 0, "x", 0, QX[0:3] + R)
+    mm("p0", 400, "r1", 0, "x", 0, QX + R)
     mm("p1", 384, "r1", 0, "x", 128, QX[1:4] + R)
-    ts(T.ar[:, :], T.arow[:, :], cc(Z12), A.max, ["arow", "z12", "z14"], "ar", cc(Z14), A.max)
-    ts(cc(M8), LANE, 8.0, A.is_ge, ["lane"], "m8", 4.0, A.mult)
     cp(T.opick[:, 8:24], T.ipick[:, 8:24], ["ipick2"], "opick2")
-    turn(T.kt[:, 64:128], T.kr[:, 64:128], ["kr2", "kr3"], "kt2")
+    turn(T.kt[:, 64:128], T.kr[:, 64:128], ["kr2", "kr2b", "kr3"], "kt2")
+    fill(T.R1[:, 0:272], -1000.0, "R1")
 
     learn("s", [d for t in X for d in wr[t]])
     dma("s", T.tu2[:, :], T.u2[:, :], w=["tu2"])
@@ -282,17 +299,18 @@ def rank_program(g, core, T, topo):
             cp(T.srow[:, 0:256], T.p2[:, 0:256], ["p2", "sm1"], "srow0")
         elif k == 2:
             ts(cc(D6), cc(LP1), 0.125, A.mult, ["lp1", "m8"], "d6", cc(M8), A.max)
-            fill(T.MK[:, 32:33], 0.0, "MK", ["MK1"])
-            fill(T.R1[:, 0:272], 0.0, "R1")
+            fill(T.D0[:, 0:48:3], 0.0, "D0a")
+            fill(T.D0[:, 2:48:3], 1.0, "D0c")
         elif k == 3:
             ts(T.cb[:, 4:6], T.cb[:, 2:4], cc(D6), A.add, ["cb1", "d6", "l16"], "cb2", cc(L16), A.subtract)
+            fill(T.upd[:, 0:544:2], 2.0, "up0")
             quant("u2", 0, 128, T.tu2, ["tu2"], "qu2")
         elif k < 7:
             pick_q(k - 4)
         else:
+            fill(T.MK[:, 32:33], 0.0, "MK", ["MK1"])
             cp(T.sel1[:, 0:1], T.kt[:, 64:65], ["kt2"], "sel1")
-            fill(T.E0[:, :], 0.0, "E0")
-            fill(T.R2[:, 0:144], 0.0, "R2")
+            fill(T.upd[:, 1:544:2], -1.0, "up1")
 
     def search():
         def count(t, j, tk, p, w, sign=-1.0, buf="sj"):
@@ -317,24 +335,23 @@ def rank_program(g, core, T, topo):
         ts(sm(3), sm(0), sm(1), A.add, ["sm0", "sm1"], "sm3")
         answer(sm(2), "sm2", 3, cc(L2), "l2", A.is_le)
         gather_sum(T.X1, 32, X1T, 4)
+        cp(T.l64[:, 16:32], T.C1[:, :].indirect(T.off[:, 0:1]), ["off", "C1a", "C1b", "C1c"], "c16")
         job(0)
-        count(sm(4), 5, "sm4", "p0", 384)
-        flags(sm(4), "sm4", "p4", 0, 128, w=["p4s"])
+        count(sm(4), 5, "sm4", "p0", 400)
+        flags(sm(4), "sm4", "p4", 16, 112, w=["p4s"])
+        red(sm(9), T.l64[:, 16:32], A.add, ["c16"], "sm9")
         gap(1)
-        ts(sm(6), sm(4), T8, A.is_gt, ["sm4", "tbt"], "sm6", 32.0, A.mult)
-        ts(sm(7), sm(4), T8, A.is_ge, ["sm4", "tbt"], "sm7", 32.0, A.mult)
         ts(sm(8), sm(4), QL, A.mult, ["sm4", "tbt"], "sm8", 2.0 ** -69, A.max)
-        v = total_of(128, -128.0)
-        ts(sm(9), sm(6), sm(7), A.add, ["sm6", "sm7", "l2"], "sm9", cc(L2), A.add)
+        v = total_of(112, -112.0)
         ts(sm(10), sm(4), PL, A.mult, ["sm4", "sm8", "tbt"], "sm10", sm(8), A.max)
         answer(v, "cv", 5, sm(9), "sm9")
         gather_sum(T.X2, 96, X2T + ["sm10"], 11, scale=sm(10))
         ts(T.l64[:, 0:16], W2[:, :].indirect(T.off[:, 0:1]), sm(10), A.mult, ["off", "sm10"] + WT, "w16")
+        fill(T.R1[:, 272:544], -1000.0, "R1z")
         red(sm(12), T.l64[:, 0:16], A.add, ["w16"], "sm12")
         t, tk = sm(11), "sm11"
+        b = 112
         for r in range(6):
-            b = 128 if r == 0 else 176
-
             def start():
                 if r == 0:
                     ts(T.ft[:, 1:12:2], T.crow[:, 0:6], sm(12), A.mult, ["sm12", "crow0", "crow1", "ftz"], "steps")
@@ -349,11 +366,11 @@ def rank_program(g, core, T, topo):
                 start()
                 v = total_of(b, -float(b))
             else:
-                act(T.sj[:, 0:176], T.p0[:, 0:176], AF.Sign, ["p0", tk], ["sj"], scale=-1.0, bias=t)
-                flags(t, tk, "p1", 48, 336, A.is_lt, -1.0)
-                act(T.sk[:, 0:176], T.sj[:, 0:176], AF.Relu, ["sj"], ["sk", "sm21"], accum_out=sm(21))
+                act(T.sj[:, 0:192], T.p0[:, 0:192], AF.Sign, ["p0", tk], ["sj"], scale=-1.0, bias=t)
+                flags(t, tk, "p1", 64, 320, A.is_lt, -1.0)
+                act(T.sk[:, 0:192], T.sj[:, 0:192], AF.Relu, ["sj"], ["sk", "sm21"], accum_out=sm(21))
                 start()
-                v = total_of(336, 256.0)
+                v = total_of(320, 256.0)
             answer(v, "cv", 16 + r, T.ar[:, r:r + 1], "ar")
             gather_sum(T.ft, 16, ["steps", "base", "ftz"], 24 + r)
             t, tk = sm(24 + r), "sm%d" % (24 + r)
@@ -381,36 +398,42 @@ def rank_program(g, core, T, topo):
 
         def total_a(i):
             k = 5888 + 256 * (i - 8)
-            act(T.sjv[:, k:k + 256], flags(i), AF.Relu, ["fl%d" % i], ["sc%d" % i], scale=-1.0, accum_out=w[:, 768 + i:769 + i])
+            act(T.sjv[:, k:k + 256], flags(i), AF.Relu, ["fl%d_0" % i, "fl%d_128" % i], ["sc%d" % i], scale=-1.0, accum_out=w[:, 768 + i:769 + i])
 
-        def sign(i):
+        def sign(i, a):
             t, tk = bound(i)
-            act(flags(i), T.p4[:, 0:256], AF.Sign, ["p4", tk], ["fl%d" % i], scale=-1.0, bias=t)
+            p = "p6" if a else "p4"
+            act(flags(i, a, a + 128), T[p][:, 0:128], AF.Sign, [p, tk], ["fl%d_%d" % (i, a)], scale=-1.0, bias=t)
         turn(w[:, 512:640], T.p2[:, 0:128], ["p2"], "tra")
         ts(T.sel2[:, 0:1], T.ku[:, 0:1], cc(O16), A.add, ["ku", "o16"], "sel2")
         for i in range(4):
             over(i, "p3", 0, 128)
         over(0, "p5", 128, 256)
-        turn(w[:, 640:768], T.p6[:, 0:128], ["p6"], "trb")
+        turn(w[:, 640:768], T.p7[:, 0:128], ["p7"], "trb")
+        for i in range(8, 12):
+            sign(i, 0)
         for i in range(8, 14):
-            sign(i)
-            if i > 8:
-                total_a(i - 1)
-        total_a(13)
+            if i > 11:
+                sign(i, 0)
+            sign(i, 128)
+            if i > 9:
+                total_a(i - 2)
+        total_a(12)
         for i in range(1, 4):
             over(i, "p5", 128, 256)
-            total_v(i - 1)
-        over(14, "p7", 0, 256)
-        total_v(3)
-        over(15, "p7", 0, 256)
-        total_v(14)
+        over(14, "p0", 0, 256)
+        over(15, "p0", 0, 256)
         for i in range(4, 8):
             over(i, "p3", 0, 128)
-            if i == 4:
+            if i == 5:
+                total_v(14)
                 total_v(15)
             over(i, "p5", 128, 256)
-            if i == 4:
-                cp(w[:, 782:784], T.sjv[:, 4608 + 1024 + 127:4608 + 1280:128], ["sc14", "sc15"], "rawv")
+            if i < 6:
+                total_v(2 * i - 8)
+                total_v(2 * i - 7)
+        act(w[:, 782:784], T.sjv[:, 4608 + 1024 + 127:4608 + 1280:128], AF.Identity, ["sc14", "sc15"], ["rawv"])
+        total_a(13)
         for i in range(4, 8):
             total_v(i)
         re_, ro = ["sc%d" % i for i in range(8)], ["rawv"] + ["sc%d" % i for i in range(8, 14)]
@@ -421,7 +444,7 @@ def rank_program(g, core, T, topo):
             ts(T.EO[:, 72 + 16 * h:88 + 16 * h:2], raw, cc(EVEN), A.mult, rr + ["even"], "gin0%d" % h, -500.0, A.add)
         for raw, rr, h in both[::-1]:
             act(T.EO[:, 73 + 16 * h:88 + 16 * h:2], raw, AF.Identity, rr + ["nodd"], ["gin1%d" % h], scale=cc(NODD), bias=-500.0)
-        for raw, rr, h in both:
+        for raw, rr, h in both[::-1]:
             tt(T.E1[:, 48 * h:48 * h + 8], raw, w[:, 784 + 8 * h:792 + 8 * h], A.mult, rr + ["mk%d" % h, "E1"], "gm%d" % h)
         scan(T.EO[:, 0:72], T.E0[:, :], T.E1[:, :], ["gm0", "gm1", "E0a", "E0b", "E1"], "EO", -5000.0, A.add, A.max)
         turn(w[:, 992:1024], T.EO[:, 72:104], ["gin00", "gin01", "gin10", "gin11"], "gout")
@@ -430,37 +453,68 @@ def rank_program(g, core, T, topo):
         red(sm(42), w[:, 928:992], A.max, ["bmt"], "sm42", negate=True)
         return sm(42), "sm42"
 
-    def listed(n, ch, ck, t, tk):
+    def flags_of(n, ch, ck, t, tk):
         q = n // 16
-        D0, D1, es = T.D0, T.D1, T.D1[:, 3 * q + 5:6 * q + 5:3]
         ts(T.GE[:, 32 - q:32], ch[:, :], t, A.is_gt, [ck, tk], "gt", U, A.mult)
         ts(T.GE[:, 33:33 + q], ch[:, :], t, A.is_equal, [ck, tk], "eq", U, A.mult)
-        if n == 256:
-            ts(sm(31), t, U, A.mult, [tk, "br256"], "sm31", cc(BR2), A.add)
-        act(T.sg[:, 0:q], ch[:, :], AF.Sign, [ck, tk], ["sg"], scale=-1.0, bias=t)
-        scan(D1[:, 5:6 * q + 8:3], T.MK[:, 32 - q:33 + q], T.GE[:, 32 - q:33 + q], ["gt", "eq", "MK", "GEz", "sh"], "gs", cc(SH), A.mult, A.add)
-        ts(T.og[:, 0:3:2], D1[:, 3 * q + 2:6 * q + 6:3 * q + 3], 1024.0, A.mult, ["gs", "l64"], "og", cc(L64), A.add)
-        if n == 512:
-            act(T.gj[:, 0:16], T.ir[:, :].indirect(T.og[:, 0:1]), AF.Identity, ["og", "ir", "br512"], ["gj", "sm31"], scale=-U, bias=cc(BR1), accum_out=sm(31))
-        act(T.gj[:, 16:32], T.ir[:, :].indirect(T.og[:, 2:3]), AF.Relu, ["og", "ir", "be"], ["gk", "sm32"], scale=U, bias=cc(BE), accum_out=sm(32))
-        act(T.gj[:, 32:48], T.ir[:, :].indirect(T.og[:, 0:1]), AF.Relu, ["og", "ir", "ba"], ["gl", "sm33"], bias=cc(BA), accum_out=sm(33))
-        tt(T.es2[:, 0:q], es, T.sg[:, 0:q], A.add, ["gs", "sg"], "es2")
-        if n == 512:
-            fill(T.E1[:, :], -5000.0, "E1")
-            turn(T.ku[:, :], T.ks[:, 8:40], ["ks"], "ku")
-        else:
-            quant("v", 0, 128, T.tv, ["tv"], "qvv")
-        ts(D1[:, 1:3 * q:3], es, sm(32), A.add, ["gs", "sm32", "sm31"], "me", sm(31), A.min)
-        ts(D0[:, 1:3 * q:3], T.es2[:, 0:q], sm(32), A.add, ["es2", "sm32", "sm31"], "y1", sm(31), A.is_ge)
-        scan(T.DO[:, 0:3 * q], D0[:, 0:3 * q], D1[:, 0:3 * q], ["me", "y1", "trn", "gs", "D0a", "D0c", "D1z"], "dd", 0.0, A.mult, A.add)
-        so, R, rk, val, vk, Tr = (T.osc1, T.R1, "R1", T.val1, "val1", T.Tr1) if n == 512 else (T.osc2, T.R2, "R2", T.val2, "val2", T.Tr2)
-        ts(so[:, :], T.DO[:, 2:3 * q:3], 1024.0, A.mult, ["dd", "sm33"], "so", sm(33), A.add)
-        cp(R[:, :].indirect(so[:, :]), val[:, :], ["so", vk], rk)
-        m = n // 2
-        turn(Tr[:, 0:m], R[:, 0:m], [rk], rk + "a")
-        turn(Tr[:, m:n], R[:, 16:m + 16], [rk], rk + "b")
 
-    L1T, L2T = ["R1a", "R1b", "sel1"], ["R2a", "R2b", "sel2"]
+    def running(n, D1, k, a, first, ch, ck, t, tk, r):
+        q = n // 16
+        act(T.sg[:, 0:q], ch[:, :], AF.Sign, [ck, tk], ["sg"], scale=-1.0, bias=t)
+        scan(D1[:, a:a + 2 * k * q + 1:k], T.MK[:, 32 - q:33 + q], T.GE[:, 32 - q:33 + q], ["gt", "eq", "MK", "GEz", "sh%d" % n] + r, "gs", first, A.mult, A.add)
+
+    def others(out, off, r, j, k, add):
+        act(out, T.ir[:, :].indirect(off), AF.Relu, ["ir"] + r, ["gk%d" % j, "sm%d" % j], scale=k, bias=add, accum_out=sm(j))
+
+    def list1(ch, ck, t, tk):
+        D1 = T.P1
+        flags_of(512, ch, ck, t, tk)
+        running(512, D1, 4, 11, cc(SG), ch, ck, t, tk, ["P1z"])
+        ts(T.og[:, 0:2], D1[:, 135:268:132], 1024.0, A.mult, ["gs", "lx"], "og", cc(LX), A.add)
+        ts(T.og[:, 2:3], D1[:, 135:136], 1024.0, A.mult, ["gs", "lz"], "og2", cc(LZ), A.add)
+        others(T.gj[:, 16:48], T.og[:, 0:2], ["og", "be512"], 32, U, cc(BE))
+        others(T.gj[:, 48:64], T.og[:, 2:3], ["og2", "ba512"], 33, 2.0, cc(BA2))
+        tt(T.es2[:, :], D1[:, 139:267:4], T.sg[:, :], A.add, ["gs", "sg"], "es2")
+        SM = ["sm32", "cc"]
+        fill(T.P0[:, 7:128:8], 1.0, "P0c", ["P0z"])
+        turn(T.ku[:, :], T.ks[:, 8:40], ["ks"], "ku")
+        ts(T.P0[:, 5:128:8], T.es2[:, 1:32:2], sm(32), A.add, ["es2", "P0z"] + SM, "yo", cc(CC), A.is_ge)
+        ts(T.P0[:, 6:128:8], T.es2[:, 0:32:2], sm(32), A.add, ["es2", "P0z"] + SM, "ye", cc(CC), A.is_ge)
+        ts(D1[:, 6:128:8], D1[:, 139:267:8], sm(32), A.add, ["gs", "P1z"] + SM, "me", cc(CC), A.min)
+        scan(T.PO[:, :], T.P0[:, :], D1[:, 0:128], ["me", "yo", "ye", "gs", "P0c", "P1a", "P1b", "P1c"], "dd", 0.0, A.mult, A.add)
+        ts(T.osc1[:, :], T.PO[:, 7:128:8], 2048.0, A.mult, ["dd", "sm33"], "so", sm(33), A.subtract)
+        cp(T.R1[:, :].indirect(T.osc1[:, :]), T.val1[:, :], ["so", "val1", "R1z"], "R1")
+        scan(T.RS[:, 0:288], T.upd[:, 0:288], T.R1[:, 0:288], ["R1", "up0", "up1"], "RS0", -2000.0, A.add, A.max)
+        scan(T.RS[:, 302:592], T.upd[:, 0:290], T.R1[:, 254:544], ["R1", "up0", "up1"], "RS1", -2000.0, A.add, A.max)
+        for h in range(2):
+            for j in range(2):
+                a = 304 * h + 32 * j + 1
+                turn(T.Tr1[:, 256 * h + 128 * j:256 * h + 128 * j + 128], T.RS[:, a:a + 255:2], ["RS%d" % h], "R1%d%d" % (h, j))
+
+    def list2(ch, ck, t, tk):
+        D1 = T.D1
+        es = D1[:, 53:101:3]
+        flags_of(256, ch, ck, t, tk)
+        ts(sm(31), t, U, A.mult, [tk, "br256"], "sm31", cc(BR2), A.add)
+        for j, e in ((34, 1.0), (35, -1.0)):
+            act(T.l64[:, 16 * j - 544:16 * j - 528], ch[:, :], AF.Sign, [ck, tk], ["gm%d" % j, "sm%d" % j], scale=-1.0 - e * 2.0 ** -12, bias=t, accum_out=sm(j))
+        running(256, D1, 3, 5, cc(SH), ch, ck, t, tk, [])
+        ts(T.og[:, 2:3], sm(34), sm(35), A.subtract, ["sm34", "sm35", "l33"], "og2", cc(L33), A.add)
+        ts(T.og[:, 0:1], sm(34), -0.5, A.mult, ["sm34", "l8"], "og", cc(L8), A.add)
+        others(T.gj[:, 16:32], T.og[:, 2:3], ["og2", "be256"], 32, U / 2, cc(BE2))
+        others(T.gj[:, 48:64], T.og[:, 0:1], ["og", "ba256"], 33, 1.0, cc(BA))
+        tt(T.es2[:, 0:16], es, T.sg[:, 0:16], A.add, ["gs", "sg"], "es2")
+        SM = ["sm32", "sm31"]
+        quant("v", 0, 128, T.tv, ["tv"], "qvv")
+        ts(D1[:, 1:48:3], es, sm(32), A.add, ["gs"] + SM, "me", sm(31), A.min)
+        ts(T.D0[:, 1:48:3], T.es2[:, 0:16], sm(32), A.add, ["es2"] + SM, "y1", sm(31), A.is_ge)
+        scan(T.DO[:, :], T.D0[:, :], D1[:, 0:48], ["me", "y1", "trn", "gs", "D0a", "D0c", "D1z"], "dd", 0.0, A.mult, A.add)
+        ts(T.osc2[:, :], T.DO[:, 2:48:3], 1024.0, A.mult, ["dd", "sm33"], "so", sm(33), A.add)
+        cp(T.R2[:, :].indirect(T.osc2[:, :]), T.val2[:, :], ["so", "val2"], "R2")
+        turn(T.Tr2[:, 0:128], T.R2[:, 0:128], ["R2"], "R2a")
+        turn(T.Tr2[:, 128:256], T.R2[:, 16:144], ["R2"], "R2b")
+
+    L2T = ["R2a", "R2b", "sel2"]
 
     def pick(c, tr, sel, n, k, add, r, o, w):
         ts(T[o][:, c:c + 16], T[tr][:, 0:n].indirect(T[sel][:, 0:1]), k, A.mult, r, w, add, A.add)
@@ -479,30 +533,43 @@ def rank_program(g, core, T, topo):
             ts(o, i, 0.0, A.max, [p], w, 0.03125, A.mult)
 
     t1, k1 = search()
-    listed(512, T.ch1, "ch", t1, k1)
-    for k in range(3):
-        pick_s(k)
+    list1(T.ch1, "ch", t1, k1)
+    lin(cc(L33), "l33", LANE, -40.0, 600.0)
+    act(cc(SQ), LANE, AF.Square, ["lane"], ["sq"], bias=-0.5)
+    lin(cc(O16), "o16", ODD, 16.0, 0.0)
     lin(cc(EVEN), "even", ODD, 1.0, -1.0)
     lin(cc(NODD), "nodd", ODD, -1.0, 0.0)
     lin(cc(NO16), "no16", ODD, -16.0, 0.0)
     lin(cc(BR2), "br256", ODD, 8 * U, 1128 * U)
+    act(cc(S0), cc(SQ), AF.Identity, ["sq"], ["s0"], scale=-20 * U, bias=5 * U)
+    pick_s(0)
+    act(cc(SH), ODD, AF.Identity, ["lane", "s0"], ["sh256"], scale=8 * U, bias=cc(S0))
+    lin(cc(BA), "ba256", LANE, 40.0, -640.0)
+    lin(cc(O4), "o4", ODD, 4 * U, 0.0)
+    lin(cc(BE2), "be256", LANE, 20.0 * U, -320 * U)
+    lin(cc(L8), "l8", LANE, -40.0, 608.0)
+    pick_s(1)
     act(T.D1[:, 0:48:3], T.tr2[:, :], AF.Identity, ["tr2"], ["trn"], scale=U)
+    act(T.D1[:, 2:3], cc(SH), AF.Identity, ["sh256"], ["D1z"])
+    act(T.E0[:, 8:57:48], T.arow[:, 0:2], AF.Identity, ["E0", "arow"], ["E0a"], scale=0.0, bias=1000.0)
+    act(T.E0[:, 24:25], ODD, AF.Identity, ["E0", "lane"], ["E0b"], scale=0.0, bias=-3000.0)
+    act(T.GE[:, 32:33], cc(SH), AF.Identity, ["sh256", "o4"], ["GEz"], scale=0.5, bias=cc(O4))
+    pick_s(2)
     dma("s", T.tv[:, :], T.v[:, :], w=["tv"])
     dma("s", codes(T.qZ[:, :]), T.zc[:, :], w=["qZ"])
     dma("s", T.sZ[:, :], T.zs[:, :], w=["sZ"])
-    pick(0, "Tr1", "sel1", 512, 1.0, 256.0, L1T, "o1", "o1")
+    for h in range(2):
+        ts(T.o1[:, 16 * h:16 * h + 16], T.Tr1[:, 256 * h:256 * h + 256].indirect(T.sel1[:, 0:1]), 256.0, A.add, ["R1%d0" % h, "R1%d1" % h, "sel1"], "o1%d" % h)
     FA, FB, HA, HB = four("tfa"), four("tfb"), four("tha"), four("thb")
 
     def gather_f(h, t, eng):
-        gather(T.tf[:, 512 * h + t:512 * h + 512:4], T.wn[:, 896 * t:896 * t + 512], T.o1[:, 8 * h:8 * h + 8], ["xp%d" % t, "o1"], eng, (FA, FB)[h][t])
-    fill(T.E0[:, 8:57:48], 1000.0, "E0a", ["E0"])
+        gather(T.tf[:, 512 * h + t:512 * h + 512:4], T.wn[:, 896 * t:896 * t + 512], T.o1[:, 16 * h:16 * h + 8], ["xp%d" % t, "o1%d" % h], eng, (FA, FB)[h][t])
     for t in range(4):
         gather_f(0, t, "avav"[t])
     for t in range(3):
         gather_f(1, t, "ava"[t])
     quant("F", 0, 128, T.tf, FA, "qFa")
     gather_f(1, 3, "v")
-    fill(T.E0[:, 24:25], -3000.0, "E0b", ["E0"])
     quant("F", 128, 128, T.tf, FB, "qFb")
     PA, PB = ["p2", "p3", "p4", "p5"], ["p6", "p7", "p0", "p1"]
     for b in range(4):
@@ -515,12 +582,12 @@ def rank_program(g, core, T, topo):
     relu("th", 1, 0, PB[0], "a", HB[0])
     quant("H", 0, 128, T.th, HA, "qHa")
     relu("th", 1, 1, PB[1], "v", HB[1])
-    for p, k in (("p2", 0), ("p3", 1)):
+    for p, k in (("p2", 0), ("p3", 1), ("p4", 2)):
         mm(p, 128, "r2", 128 * k, "H", 0, ["qHa", "qr2%d" % k, "sr2%d" % k])
     relu("th", 1, 2, PB[2], "a", HB[2])
     relu("th", 1, 3, PB[3], "v", HB[3])
     quant("H", 128, 128, T.th, HB, "qHb")
-    for p, k, c in (("p4", 2, 0), ("p5", 1, 128), ("p6", 0, 128), ("p7", 2, 0)):
+    for p, k, c in (("p5", 1, 128), ("p6", 2, 128), ("p7", 0, 128), ("p0", 2, 0)):
         mm(p, 256 - c, "r2", 128 * k, "H", c, ["qHa", "qHb", "qr2%d" % k, "sr2%d" % k])
     for t in range(4):
         plane(T.hp[:, 256 * t:256 * t + 256], T.th[:, t:1024:4], 256, [HA[t], HB[t]], "hp%d" % t)
@@ -528,7 +595,7 @@ def rank_program(g, core, T, topo):
     iota("ones", [[0, 128]], 1)
     select(T.te[:, 3:515:4], T.ones[:, :], [[1, 128]], A.is_equal, 0, -1, ["ones", "tez"], "te")
     t2, k2 = ranks()
-    listed(256, T.ch2, "ch2", t2, k2)
+    list2(T.ch2, "ch2", t2, k2)
     act(T.Mr[:, :], T.ir[:, 0:528], AF.Identity, ["ir", "no16"], ["Mr"], bias=cc(NO16))
     pick(64, "Tr2", "sel2", 256, 1.0, 0.0, L2T, "o2", "o2")
     for t in range(4):
@@ -561,22 +628,25 @@ def rank_program(g, core, T, topo):
         wr[tok + "r"] = [("far", sem, total[sem], {})]
         total["sent"] = total.get("sent", 0) + 4 * (N - 1)
     swap("G", 0, 128, "down")
+    for h in range(2):
+        cp(T.o1[:, 32 + 8 * h:40 + 8 * h], T.o1[:, 16 * h:16 * h + 8], ["o1%d" % h], "o1c%d" % h)
     for t in range(4):
         pick(16 * t, "Tr2", "sel2", 256, 4.0, float(t), L2T, "o2", "o2_%d" % t)
-    act(T.L1r[:, :], T.ir[:, 0:512].indirect(T.o1[:, 0:16]), AF.Identity, ["ir", "o1"], ["L1r"])
+    act(T.L1r[:, :], T.ir[:, 0:512].indirect(T.o1[:, 32:48]), AF.Identity, ["ir", "o1c0", "o1c1"], ["L1r"])
+    for t in range(4):
+        gather(T.txg[:, 128 * t:128 * t + 128], T.tf[:, :], T.o2[:, 16 * t:16 * t + 8], FA + FB + ["o2_%d" % t], "a", "txg%d" % t)
     act(T.olr[:, :], T.L1r[:, :].indirect(T.o2[:, 64:72]), AF.Identity, ["L1r", "o2"], ["olr"])
     turned = 16 * (N - 1 - rank)
     dma("s", T.ol[:, 0:128 - turned], T.olr[0:128:16, turned:128], r=["olr"], w=["ol"])
     if turned:
         dma("s", T.ol[:, 128 - turned:128], T.olr[0:128:16, 0:turned], r=["olr"], w=["ol2"])
-    for t in range(4):
-        gather(T.txg[:, 128 * t:128 * t + 128], T.tf[:, :], T.o2[:, 16 * t:16 * t + 8], FA + FB + ["o2_%d" % t], "a", "txg%d" % t)
-    cp(T.sel3[:, 0:1], T.kt[:, 96:97], ["kt2"], "sel3a")
-    ts(T.o1[:, 16:32], T.o1[:, 0:16], cc(O16), A.add, ["o1", "o16"], "o1s")
+    ts(T.o1[:, 48:64], T.o1[:, 32:48], cc(O16), A.add, ["o1c0", "o1c1", "o16"], "o1s")
     cp(T.M1[:, :].indirect(T.o2[:, 64:72]), T.v3[:, :], ["o2", "v3"], "M1")
+    cp(T.sel3[:, 0:1], T.kt[:, 96:97], ["kt2"], "sel3a")
     ts(T.sel3[:, 1:2], T.kt[:, 96:97], 256.0, A.add, ["kt2"], "sel3b")
-    cp(T.Mr[:, :].indirect(T.o1[:, 16:32]), T.M1[:, :], ["o1s", "M1"], "Mr")
-    for b in range(4):
+    quant("E", 0, 128, T.te, ["te", "tez"], "qE0", 3)
+    cp(T.Mr[:, :].indirect(T.o1[:, 48:64]), T.M1[:, :], ["o1s", "M1"], "Mr")
+    for b in range(1, 4):
         quant("E", 128 * b, 128, T.te, ["te", "tez"], "qE%d" % b, 3 - b)
     for b in range(4):
         mm(PA[b], 128, "Z", 128 * b, "G", 112, ["qZ", "sZ", "qG", "qGr"])
@@ -599,12 +669,12 @@ def rank_program(g, core, T, topo):
     def xn(b):
         tt(T.wn[:, 896 * b + 768:896 * b + 896], T.txg[:, 128 * b:128 * b + 128], T.thn[:, 128 * b:128 * b + 128], A.add, ["txg%d" % b, "thn%d" % b], "xn%d" % b)
 
-    def back(h, t, eng):
-        gather(T.xf[:, 1024 * h + t:1024 * h + 1024:4], T.wn[:, 896 * t:896 * t + 896], T.oM[:, 16 * h:16 * h + 16],
-               ["oM", "xp%d" % t, "xh%d" % t, "xn%d" % t], eng, "xf%d%d" % (h, t))
+    def back(c, n, t, eng):
+        gather(T.xf[:, 512 * c + t:512 * (c + n):4], T.wn[:, 896 * t:896 * t + 896], T.oM[:, 8 * c:8 * (c + n)],
+               ["oM", "xp%d" % t, "xh%d" % t, "xn%d" % t], eng, "xf%d%d" % (c, t))
 
-    def result(c):
-        quant("N", 128 * c, 128, T.xf, four("xf%d" % (c // 2)), "qN%d" % c)
+    def result(c, r):
+        quant("N", 128 * c, 128, T.xf, r, "qN%d" % c)
         mm(PB[c], 128, "v", 0, "N", 128 * c, ["qvv", "qN%d" % c])
 
     def out(c, eng):
@@ -613,29 +683,26 @@ def rank_program(g, core, T, topo):
             act(o, i, AF.Copy, [PB[c]], ["y%d" % c])
         else:
             cp(o, i, [PB[c]], "y%d" % c)
-
-    def scales(q, j):
-        dma(q, T.osc[4 * j:4 * j + 4, :], T.sN[32 * j:32 * j + 4, :], r=four("qN"), w=["osc%d" % j])
-    for f, b in ((hn, 0), (hn, 1), (xn, 0), (hn, 2), (xn, 1), (hn, 3), (xn, 2), (xn, 3)):
+    for f, b in ((hn, 0), (hn, 1), (hn, 2), (xn, 0), (hn, 3), (xn, 1), (xn, 2), (xn, 3)):
         f(b)
-    for h, t, eng in ((0, 0, "a"), (0, 1, "a"), (0, 2, "v"), (0, 3, "v"), (1, 0, "a"), (1, 1, "a"), (1, 2, "a")):
-        back(h, t, eng)
-    result(0)
-    result(1)
+    for c, n, t, eng in ((0, 2, 0, "a"), (0, 2, 1, "v"), (0, 2, 2, "a"), (0, 2, 3, "v"), (2, 2, 0, "a"), (2, 2, 2, "a"), (3, 1, 1, "a"), (2, 1, 3, "v")):
+        back(c, n, t, eng)
+    result(0, four("xf0"))
+    result(1, four("xf0"))
     dma("s", T.oc[:, 0:1024], codes(T.qN[:, 0:256]), r=["qN0", "qN1"], w=["oc0"])
-    back(1, 3, "v")
-    out(0, "v")
-    result(2)
-    result(3)
+    back(2, 1, 1, "v")
+    back(3, 1, 3, "v")
+    out(0, "a")
     out(1, "a")
     dma("a", T.y[:, 0:256], T.ysb[:, 0:256], r=["y0", "y1"], w=["yo0"])
+    result(2, four("xf2"))
+    result(3, ["xf20", "xf31", "xf22", "xf33"])
     dma("s", T.oc[:, 1024:2048], codes(T.qN[:, 256:512]), r=["qN2", "qN3"], w=["oc1"])
-    for j in range(3):
-        scales("s", j)
+    for j in range(4):
+        dma("s", T.osc[4 * j:4 * j + 4, :], T.sN[32 * j:32 * j + 4, :], r=four("qN"), w=["osc%d" % j])
     out(2, "a")
     out(3, "v")
     dma("a", T.y[:, 256:512], T.ysb[:, 256:512], r=["y2", "y3"], w=["yo1"])
-    scales("a", 3)
-    for s in sorted(total):
+    for s in sorted(total, key=lambda s: int(s[1:]) if s[1:].isdigit() else -1):
         if seen.get(s, 0) < total[s]:
             g.wait_ge(T.sem[s], total[s])

@@ -4,23 +4,24 @@ from concourse.mybir import dt, AluOpType as A, AxisListType, ActivationFunction
 F8, U8, BF, F32, I32, U16 = "float8_e4m3fn_x4", "uint8", "bfloat16", "float32", "int32", "uint16"
 SCRATCH = {}
 for _d, _l in (
-    (BF, "tu1 512 tu2 512 tv 512 tx 2048 xf 2048 wn 3584 tf 1024 th 1024 hp 1024 tg 512 tt 512 thn 512 txg 512 ones 128 te 528 "
-         "val1 256 RS 592 upd 544 val2 256 sj 512 sk 512 sjv 7424 R1 4896 R2 2464 Tr1 512 Tr2 256 mul 448 br 296"),
-    (F32, "tbr 128 tbt 128 kr 128 kt 128 ks 48 ku 32 arow 8 ar 8 X1 32 C1 32 W2 96 X2 96 crow 8 ft 16 cb 8 ir 1280 tr1 16 P0 128 P1 272 PO 128 tr2 16 c 40 gj 64 l64 32 "
-          "sm 64 srow 1024 ch1 32 ch2 16 GE 72 MK 72 sg 32 es2 32 D0 48 D1 104 DO 48 E0 72 E1 72 EO 104 "
-          "L1r 256 olr 128 M1 256 v3 128 Mr 528 TrM 1024 ysb 512"),
-    (I32, "ipick 24"),
-    (U16, "opick 24 off 2 og 4 osc1 16 osc2 16 o1 64 o2 80 oM 32 sel1 2 sel2 2 sel3 2")):
+    (BF, "tu1 512 tu2 512 tv 512 tx 2048 xf 2048 wn 5120 tf 1024 th 1024 hp 2048 tg 512 tt 832 xi 1024 alt 512 uk 256 cut 256 kk 8 sb 8 rep 256 krow 256 "
+         "af 256 ltf 256 ltr 256 cum 256 cf 576 cs 288 ones 128 te 528 "
+         "val1 256 RS 592 upd 544 sj 512 sk 512 sjv 7424 R1 4896 Tr1 512 mul 448 br 296"),
+    (F32, "tbr 128 tbt 128 kr 128 kt 128 arow 8 ar 8 X1 32 C1 32 W2 96 X2 96 crow 8 ft 16 cb 8 ir 1280 tr1 16 P0 128 P1 272 PO 128 c 40 gj 64 l64 32 "
+          "sm 64 srow 1024 ch1 32 GE 72 MK 72 sg 32 es2 32 E0 72 E1 72 EO 72 "
+          "L1r 256 olr 128 M1 256 v3 128 Mr 512 oMf 32 pa 16 pb 16 pc 16 ysb 512"),
+    (I32, "ipick 24 ph 16"),
+    (U16, "opick 24 off 2 og 4 osc1 16 o1 64 o2 80 oM 32 sel1 2")):
     _l = _l.split()
     for _i in range(0, len(_l), 2):
         SCRATCH[_l[_i]] = ("sbuf", [128, int(_l[_i + 1])], _d)
 for _n, _w in (("W", 512), ("Z", 512), ("x", 512), ("N", 512), ("E", 512), ("F", 256), ("H", 256), ("u1", 128), ("u2", 128), ("r1", 128), ("r2", 384), ("v", 128),
-               ("G", 240), ("T", 240)):
+               ("G", 240), ("T", 240), ("B", 128)):
     SCRATCH["q" + _n] = ("sbuf", [128, _w], F8)
     SCRATCH["s" + _n] = ("sbuf", [128, _w], U8)
 for _i in range(8):
     SCRATCH["p%d" % _i] = ("psum", [128, 512], F32)
-SEMAPHORES = ["qv", "qa", "qt", "qg", "down", "up", "sent"] + ["d%d" % i for i in range(44)]
+SEMAPHORES = ["qv", "qa", "qt", "qg", "down0", "down1", "up0", "up1", "sent"] + ["d%d" % i for i in range(44)]
 
 
 def rank_program(g, core, T, topo):
@@ -151,8 +152,6 @@ def rank_program(g, core, T, topo):
     iota("ipick", [[16, 2], [32, 4], [0, 2]], 0, at=8, w="ipick2")
     iota("kr", [[0, 2], [32, 4], [128, 2]], 0, at=64, w="kr2")
     iota("kr", [[0, 2], [32, 4], [128, 2]], 16, at=80, w="kr2b")
-    iota("kr", [[16, 2], [32, 8], [512, 2]], 0, at=96, w="kr3")
-    iota("ks", [[0, 5], [32, 4], [128, 2]], 0, at=8 - (rank + 1) % N)
     iota("tr1", [[1, 16]], 544, 16)
     iota("P1", [[0, 272]], 0, w="P1z")
     iota("ir", [[1, 1280]], 0)
@@ -160,14 +159,12 @@ def rank_program(g, core, T, topo):
     iota("MK", [[0, 72]], 1, w="MK1")
     iota("val1", [[2, 16], [32, 16]], -255)
     for t in range(4):
-        plane(T.wn[:, 896 * t:896 * t + 512], T.tx[:, t:2048:4], 512, X, "xp%d" % t)
+        plane(T.wn[:, 1280 * t:1280 * t + 512], T.tx[:, t:2048:4], 512, X, "xp%d" % t)
     iota("E0", [[0, 72]], 0)
+    iota("uk", [[0, 256]], 0)
     iota("E1", [[0, 72]], -5000)
-    iota("tr2", [[1, 16]], 256, 16)
-    iota("R2", [[0, 144]], 0)
-    iota("val2", [[1, 16], [16, 16]], 0)
-    iota("M1", [[1, 256]], 512)
-    iota("v3", [[1, 128]], 768)
+    iota("ones", [[0, 128]], 1)
+    iota("Mr", [[1, 16], [16, 32]], 0)
 
     br = T.br
     fill(T.mul[:, 0:146], 0.5, "mul0")
@@ -190,8 +187,7 @@ def rank_program(g, core, T, topo):
     turn(T.tbt[:, :], T.tbr[:, :], ["tb%s%d" % (x, h) for x in "abcd" for h in range(2)], "tbt")
     B1, T8, QL, PL = (T.tbt[:, 32 * j:32 * j + 1] for j in range(4))
     LANE, ODD = T.kt[:, 0:1], T.kt[:, 32:33]
-    (NB1, LP1, CN, CP, L33, O16, EVEN, NODD, L2, Z12, M8, D6, CB, CB6, L16, Z14, NO16, SQ, S0, SH, L64, BA, BE, BR1, BR2, BA2,
-     O4, BE2, L8, O8, SG, CC, LX, LZ) = range(34)
+    (NB1, LP1, CN, CP, LH, L2, Z12, M8, D6, CB, CB6, L16, Z14, SQ, S0, L64, BE, BR1, BA2, L8, O8, SG, CC, LX, LZ) = range(25)
     W2 = T.W2
     WT = ["W2z"]
     for k, (o, i, s) in enumerate(((W2[:, 0:30:2], br[:, 61:76], -1.0), (W2[:, 30:32], br[:, 75:77], -1.0), (W2[:, 32:48:2], br[:, 69:77], -1.0),
@@ -279,10 +275,10 @@ def rank_program(g, core, T, topo):
     mm("p2", 256, "r1", 0, "x", 0, QX[0:2] + R)
     mm("p3", 128, "r1", 0, "x", 256, QX[2:3] + R)
     mm("p4", 128, "r1", 0, "x", 384, QX[3:4] + R)
-    mm("p0", 400, "r1", 0, "x", 0, QX + R)
+    mm("p0", 384, "r1", 0, "x", 0, QX + R)
     mm("p1", 384, "r1", 0, "x", 128, QX[1:4] + R)
     cp(T.opick[:, 8:24], T.ipick[:, 8:24], ["ipick2"], "opick2")
-    turn(T.kt[:, 64:128], T.kr[:, 64:128], ["kr2", "kr2b", "kr3"], "kt2")
+    turn(T.kt[:, 64:96], T.kr[:, 64:96], ["kr2", "kr2b"], "kt2")
     fill(T.R1[:, 0:272], -1000.0, "R1")
 
     learn("s", [d for t in X for d in wr[t]])
@@ -299,11 +295,10 @@ def rank_program(g, core, T, topo):
             cp(T.srow[:, 0:256], T.p2[:, 0:256], ["p2", "sm1"], "srow0")
         elif k == 2:
             ts(cc(D6), cc(LP1), 0.125, A.mult, ["lp1", "m8"], "d6", cc(M8), A.max)
-            fill(T.D0[:, 0:48:3], 0.0, "D0a")
-            fill(T.D0[:, 2:48:3], 1.0, "D0c")
+            fill(T.alt[:, 0:512:2], 0.0, "alt0")
+            fill(T.upd[:, 0:544:2], 2.0, "up0")
         elif k == 3:
             ts(T.cb[:, 4:6], T.cb[:, 2:4], cc(D6), A.add, ["cb1", "d6", "l16"], "cb2", cc(L16), A.subtract)
-            fill(T.upd[:, 0:544:2], 2.0, "up0")
             quant("u2", 0, 128, T.tu2, ["tu2"], "qu2")
         elif k < 7:
             pick_q(k - 4)
@@ -337,12 +332,12 @@ def rank_program(g, core, T, topo):
         gather_sum(T.X1, 32, X1T, 4)
         cp(T.l64[:, 16:32], T.C1[:, :].indirect(T.off[:, 0:1]), ["off", "C1a", "C1b", "C1c"], "c16")
         job(0)
-        count(sm(4), 5, "sm4", "p0", 400)
-        flags(sm(4), "sm4", "p4", 16, 112, w=["p4s"])
+        count(sm(4), 5, "sm4", "p0", 384)
+        flags(sm(4), "sm4", "p4", 0, 128, w=["p4s"])
         red(sm(9), T.l64[:, 16:32], A.add, ["c16"], "sm9")
         gap(1)
         ts(sm(8), sm(4), QL, A.mult, ["sm4", "tbt"], "sm8", 2.0 ** -69, A.max)
-        v = total_of(112, -112.0)
+        v = total_of(128, -128.0)
         ts(sm(10), sm(4), PL, A.mult, ["sm4", "sm8", "tbt"], "sm10", sm(8), A.max)
         answer(v, "cv", 5, sm(9), "sm9")
         gather_sum(T.X2, 96, X2T + ["sm10"], 11, scale=sm(10))
@@ -350,7 +345,7 @@ def rank_program(g, core, T, topo):
         fill(T.R1[:, 272:544], -1000.0, "R1z")
         red(sm(12), T.l64[:, 0:16], A.add, ["w16"], "sm12")
         t, tk = sm(11), "sm11"
-        b = 112
+        b = 152
         for r in range(6):
             def start():
                 if r == 0:
@@ -405,7 +400,6 @@ def rank_program(g, core, T, topo):
             p = "p6" if a else "p4"
             act(flags(i, a, a + 128), T[p][:, 0:128], AF.Sign, [p, tk], ["fl%d_%d" % (i, a)], scale=-1.0, bias=t)
         turn(w[:, 512:640], T.p2[:, 0:128], ["p2"], "tra")
-        ts(T.sel2[:, 0:1], T.ku[:, 0:1], cc(O16), A.add, ["ku", "o16"], "sel2")
         for i in range(4):
             over(i, "p3", 0, 128)
         over(0, "p5", 128, 256)
@@ -440,36 +434,27 @@ def rank_program(g, core, T, topo):
         both = ((rawe, re_, 0), (rawo, ro, 1))
         act(w[:, 792:800], rawo, AF.Sign, ro, ["mk1"], scale=-1.0, bias=127.5)
         ts(w[:, 784:792], rawe, 128.0, A.is_lt, re_, "mk0")
-        for raw, rr, h in both:
-            ts(T.EO[:, 72 + 16 * h:88 + 16 * h:2], raw, cc(EVEN), A.mult, rr + ["even"], "gin0%d" % h, -500.0, A.add)
-        for raw, rr, h in both[::-1]:
-            act(T.EO[:, 73 + 16 * h:88 + 16 * h:2], raw, AF.Identity, rr + ["nodd"], ["gin1%d" % h], scale=cc(NODD), bias=-500.0)
+        cp(T.uk[:, 0:256:32], rawe, re_ + ["uk"], "uk0")
+        act(T.uk[:, 16:256:32], rawo, AF.Identity, ro + ["uk"], ["uk1"])
+        act(T.te[:, :], T.ir[:, 0:528], AF.Identity, ["ir"], ["tez"], scale=0.0)
         for raw, rr, h in both[::-1]:
             tt(T.E1[:, 48 * h:48 * h + 8], raw, w[:, 784 + 8 * h:792 + 8 * h], A.mult, rr + ["mk%d" % h, "E1"], "gm%d" % h)
+        scan(T.rep[:, :], T.cut[:, :], T.uk[:, :], ["uk0", "uk1", "cut"], "rep", 0.0, A.min, A.add)
         scan(T.EO[:, 0:72], T.E0[:, :], T.E1[:, :], ["gm0", "gm1", "E0a", "E0b", "E1"], "EO", -5000.0, A.add, A.max)
-        turn(w[:, 992:1024], T.EO[:, 72:104], ["gin00", "gin01", "gin10", "gin11"], "gout")
+        turn(T.krow[:, :], T.rep[:, :], ["rep"], "krow")
         turn(w[:, 928:992], T.EO[:, 8:72], ["EO"], "bmt")
-        tt(T.ch2[:, :], w[:, 992:1008], w[:, 1008:1024], A.add, ["gout"], "ch2")
-        red(sm(42), w[:, 928:992], A.max, ["bmt"], "sm42", negate=True)
-        return sm(42), "sm42"
-
-    def flags_of(n, ch, ck, t, tk):
-        q = n // 16
-        ts(T.GE[:, 32 - q:32], ch[:, :], t, A.is_gt, [ck, tk], "gt", U, A.mult)
-        ts(T.GE[:, 33:33 + q], ch[:, :], t, A.is_equal, [ck, tk], "eq", U, A.mult)
-
-    def running(n, D1, k, a, first, ch, ck, t, tk, r):
-        q = n // 16
-        act(T.sg[:, 0:q], ch[:, :], AF.Sign, [ck, tk], ["sg"], scale=-1.0, bias=t)
-        scan(D1[:, a:a + 2 * k * q + 1:k], T.MK[:, 32 - q:33 + q], T.GE[:, 32 - q:33 + q], ["gt", "eq", "MK", "GEz", "sh%d" % n] + r, "gs", first, A.mult, A.add)
+        ts(T.af[:, :], T.krow[:, :], 128.0, A.is_lt, ["krow"], "af")
+        red(T.sb[:, 0:1], w[:, 928:992], A.max, ["bmt"], "sm42")
 
     def others(out, off, r, j, k, add):
         act(out, T.ir[:, :].indirect(off), AF.Relu, ["ir"] + r, ["gk%d" % j, "sm%d" % j], scale=k, bias=add, accum_out=sm(j))
 
     def list1(ch, ck, t, tk):
         D1 = T.P1
-        flags_of(512, ch, ck, t, tk)
-        running(512, D1, 4, 11, cc(SG), ch, ck, t, tk, ["P1z"])
+        ts(T.GE[:, 0:32], ch[:, :], t, A.is_gt, [ck, tk], "gt", U, A.mult)
+        ts(T.GE[:, 33:65], ch[:, :], t, A.is_equal, [ck, tk], "eq", U, A.mult)
+        act(T.sg[:, 0:32], ch[:, :], AF.Sign, [ck, tk], ["sg"], scale=-1.0, bias=t)
+        scan(D1[:, 11:268:4], T.MK[:, 0:65], T.GE[:, 0:65], ["gt", "eq", "MK", "GEz", "sh512", "P1z"], "gs", cc(SG), A.mult, A.add)
         ts(T.og[:, 0:2], D1[:, 135:268:132], 1024.0, A.mult, ["gs", "lx"], "og", cc(LX), A.add)
         ts(T.og[:, 2:3], D1[:, 135:136], 1024.0, A.mult, ["gs", "lz"], "og2", cc(LZ), A.add)
         others(T.gj[:, 16:48], T.og[:, 0:2], ["og", "be512"], 32, U, cc(BE))
@@ -477,7 +462,6 @@ def rank_program(g, core, T, topo):
         tt(T.es2[:, :], D1[:, 139:267:4], T.sg[:, :], A.add, ["gs", "sg"], "es2")
         SM = ["sm32", "cc"]
         fill(T.P0[:, 7:128:8], 1.0, "P0c", ["P0z"])
-        turn(T.ku[:, :], T.ks[:, 8:40], ["ks"], "ku")
         ts(T.P0[:, 5:128:8], T.es2[:, 1:32:2], sm(32), A.add, ["es2", "P0z"] + SM, "yo", cc(CC), A.is_ge)
         ts(T.P0[:, 6:128:8], T.es2[:, 0:32:2], sm(32), A.add, ["es2", "P0z"] + SM, "ye", cc(CC), A.is_ge)
         ts(D1[:, 6:128:8], D1[:, 139:267:8], sm(32), A.add, ["gs", "P1z"] + SM, "me", cc(CC), A.min)
@@ -491,33 +475,26 @@ def rank_program(g, core, T, topo):
                 a = 304 * h + 32 * j + 1
                 turn(T.Tr1[:, 256 * h + 128 * j:256 * h + 128 * j + 128], T.RS[:, a:a + 255:2], ["RS%d" % h], "R1%d%d" % (h, j))
 
-    def list2(ch, ck, t, tk):
-        D1 = T.D1
-        es = D1[:, 53:101:3]
-        flags_of(256, ch, ck, t, tk)
-        ts(sm(31), t, U, A.mult, [tk, "br256"], "sm31", cc(BR2), A.add)
-        for j, e in ((34, 1.0), (35, -1.0)):
-            act(T.l64[:, 16 * j - 544:16 * j - 528], ch[:, :], AF.Sign, [ck, tk], ["gm%d" % j, "sm%d" % j], scale=-1.0 - e * 2.0 ** -12, bias=t, accum_out=sm(j))
-        running(256, D1, 3, 5, cc(SH), ch, ck, t, tk, [])
-        ts(T.og[:, 2:3], sm(34), sm(35), A.subtract, ["sm34", "sm35", "l33"], "og2", cc(L33), A.add)
-        ts(T.og[:, 0:1], sm(34), -0.5, A.mult, ["sm34", "l8"], "og", cc(L8), A.add)
-        others(T.gj[:, 16:32], T.og[:, 2:3], ["og2", "be256"], 32, U / 2, cc(BE2))
-        others(T.gj[:, 48:64], T.og[:, 0:1], ["og", "ba256"], 33, 1.0, cc(BA))
-        tt(T.es2[:, 0:16], es, T.sg[:, 0:16], A.add, ["gs", "sg"], "es2")
-        SM = ["sm32", "sm31"]
-        quant("v", 0, 128, T.tv, ["tv"], "qvv")
-        ts(D1[:, 1:48:3], es, sm(32), A.add, ["gs"] + SM, "me", sm(31), A.min)
-        ts(T.D0[:, 1:48:3], T.es2[:, 0:16], sm(32), A.add, ["es2"] + SM, "y1", sm(31), A.is_ge)
-        scan(T.DO[:, :], T.D0[:, :], D1[:, 0:48], ["me", "y1", "trn", "gs", "D0a", "D0c", "D1z"], "dd", 0.0, A.mult, A.add)
-        ts(T.osc2[:, :], T.DO[:, 2:48:3], 1024.0, A.mult, ["dd", "sm33"], "so", sm(33), A.add)
-        cp(T.R2[:, :].indirect(T.osc2[:, :]), T.val2[:, :], ["so", "val2"], "R2")
-        turn(T.Tr2[:, 0:128], T.R2[:, 0:128], ["R2"], "R2a")
-        turn(T.Tr2[:, 128:256], T.R2[:, 16:144], ["R2"], "R2b")
+    def list2():
+        ts(T.ltf[:, :], T.krow[:, :], 128.0, A.add, ["krow", "sm42"], "ltf", T.sb[:, 0:1], A.is_lt)
+        act(T.sb[:, 2:3], T.sb[:, 0:1], AF.Identity, ["sm42"], ["sm31"], scale=-1.0, bias=256.0)
+        act(T.M1[:, :], T.ir[:, 0:256], AF.Identity, ["ir"], ["M1"], scale=2.0, bias=513.0)
+        act(T.v3[:, :], T.ir[:, 0:128], AF.Identity, ["ir"], ["v3"], scale=2.0, bias=1025.0)
+        scan(T.ltr[:, :], T.ltf[:, :], T.ltf[:, :], ["ltf", "sm31"], "ltr", T.sb[:, 2:3], A.add, A.max)
+        scan(T.cum[:, :], T.af[:, :], T.ltr[:, :], ["af", "ltr"], "cum", 0.0, A.add, A.min)
+        at = [16 * ((m + rank + 1) % N) for m in range(N)]
+        for j in range(4):
+            act(T.sjv[:, 144 * j:144 * j + 144], T.cum[:, at[j]:at[j] + 144], AF.Sign, ["cum"] + KK, ["cj%d" % j, "sm%d" % (44 + j)],
+                scale=-1.0, bias=T.kk[:, j:j + 1], accum_out=sm(44 + j))
+            ts(T.cf[:, 144 * j:144 * j + 144], T.cum[:, at[4 + j]:at[4 + j] + 144], T.kk[:, 4 + j:5 + j], A.is_lt, ["cum"] + KK, "cf%d" % j)
+        for j in range(4):
+            scan(T.cs[:, 72 * j:72 * j + 72], T.cf[:, 144 * j:144 * j + 72], T.cf[:, 144 * j + 72:144 * j + 144], ["cf%d" % j], "cs%d" % j, float(at[4 + j]))
+        for j in range(4):
+            if j == 3:
+                ts(T.o2[:, 68:72], T.cs[:, 71:288:72], 2.0, A.mult, four("cs"), "o2v", 1.0, A.add)
+            ts(T.o2[:, 64 + j:65 + j], sm(44 + j), 2.0 * at[j] + 145.0, A.add, ["sm%d" % (44 + j)], "o2a%d" % j)
 
-    L2T = ["R2a", "R2b", "sel2"]
-
-    def pick(c, tr, sel, n, k, add, r, o, w):
-        ts(T[o][:, c:c + 16], T[tr][:, 0:n].indirect(T[sel][:, 0:1]), k, A.mult, r, w, add, A.add)
+    O2 = four("o2a") + ["o2v"]
 
     def gather(out, win, off, rs, eng, w):
         if eng == "a":
@@ -525,8 +502,7 @@ def rank_program(g, core, T, topo):
         else:
             cp(out, win.indirect(off), rs, w)
 
-    def relu(dst, h, b, p, eng, w):
-        o, i = T[dst][:, 512 * h + b:512 * h + 512:4], T[p][:, 0:128]
+    def relu(o, i, p, eng, w):
         if eng == "a":
             act(o, i, AF.Relu, [p], [w], scale=0.03125)
         else:
@@ -534,27 +510,16 @@ def rank_program(g, core, T, topo):
 
     t1, k1 = search()
     list1(T.ch1, "ch", t1, k1)
-    lin(cc(L33), "l33", LANE, -40.0, 600.0)
-    act(cc(SQ), LANE, AF.Square, ["lane"], ["sq"], bias=-0.5)
-    lin(cc(O16), "o16", ODD, 16.0, 0.0)
-    lin(cc(EVEN), "even", ODD, 1.0, -1.0)
-    lin(cc(NODD), "nodd", ODD, -1.0, 0.0)
-    lin(cc(NO16), "no16", ODD, -16.0, 0.0)
-    lin(cc(BR2), "br256", ODD, 8 * U, 1128 * U)
-    act(cc(S0), cc(SQ), AF.Identity, ["sq"], ["s0"], scale=-20 * U, bias=5 * U)
+    lin(cc(LH), "lh", LANE, 1.0, 0.5)
     pick_s(0)
-    act(cc(SH), ODD, AF.Identity, ["lane", "s0"], ["sh256"], scale=8 * U, bias=cc(S0))
-    lin(cc(BA), "ba256", LANE, 40.0, -640.0)
-    lin(cc(O4), "o4", ODD, 4 * U, 0.0)
-    lin(cc(BE2), "be256", LANE, 20.0 * U, -320 * U)
-    lin(cc(L8), "l8", LANE, -40.0, 608.0)
+    KK = ["kk1"]
+    if rank < N - 1:
+        act(T.kk[:, 0:N - 1 - rank], T.ir[:, 16 * rank + 16:128:16], AF.Identity, ["ir", "lh"], ["kk0"], bias=cc(LH))
+        KK.append("kk0")
+    act(T.kk[:, N - 1 - rank:N], T.ir[:, 0:16 * rank + 16:16], AF.Identity, ["ir", "lh"], ["kk1"], bias=cc(LH))
     pick_s(1)
-    act(T.D1[:, 0:48:3], T.tr2[:, :], AF.Identity, ["tr2"], ["trn"], scale=U)
-    act(T.D1[:, 2:3], cc(SH), AF.Identity, ["sh256"], ["D1z"])
-    act(T.E0[:, 8:57:48], T.arow[:, 0:2], AF.Identity, ["E0", "arow"], ["E0a"], scale=0.0, bias=1000.0)
-    act(T.E0[:, 24:25], ODD, AF.Identity, ["E0", "lane"], ["E0b"], scale=0.0, bias=-3000.0)
-    act(T.GE[:, 32:33], cc(SH), AF.Identity, ["sh256", "o4"], ["GEz"], scale=0.5, bias=cc(O4))
     pick_s(2)
+    act(T.alt[:, 1:512:2], T.ir[:, 0:256], AF.Identity, ["ir"], ["alt1"], scale=0.0, bias=1.0)
     dma("s", T.tv[:, :], T.v[:, :], w=["tv"])
     dma("s", codes(T.qZ[:, :]), T.zc[:, :], w=["qZ"])
     dma("s", T.sZ[:, :], T.zs[:, :], w=["sZ"])
@@ -563,7 +528,7 @@ def rank_program(g, core, T, topo):
     FA, FB, HA, HB = four("tfa"), four("tfb"), four("tha"), four("thb")
 
     def gather_f(h, t, eng):
-        gather(T.tf[:, 512 * h + t:512 * h + 512:4], T.wn[:, 896 * t:896 * t + 512], T.o1[:, 16 * h:16 * h + 8], ["xp%d" % t, "o1%d" % h], eng, (FA, FB)[h][t])
+        gather(T.tf[:, 512 * h + t:512 * h + 512:4], T.wn[:, 1280 * t:1280 * t + 512], T.o1[:, 16 * h:16 * h + 8], ["xp%d" % t, "o1%d" % h], eng, (FA, FB)[h][t])
     for t in range(4):
         gather_f(0, t, "avav"[t])
     for t in range(3):
@@ -577,100 +542,122 @@ def rank_program(g, core, T, topo):
            r=["qW", "sW", "qFa"], w=[PA[b], PA[b] + "s"])
     for b in range(4):
         mm(PB[b], 128, "W", 128 * b, "F", 128, ["qW", "sW", "qFb"])
+
+    def relu_h(h, b, eng):
+        p = (PA, PB)[h][b]
+        relu(T.th[:, 512 * h + b:512 * h + 512:4], T[p][:, 0:128], p, eng, (HA, HB)[h][b])
     for b in range(4):
-        relu("th", 0, b, PA[b], "avav"[b], HA[b])
-    relu("th", 1, 0, PB[0], "a", HB[0])
+        relu_h(0, b, "avav"[b])
+    relu_h(1, 0, "a")
     quant("H", 0, 128, T.th, HA, "qHa")
-    relu("th", 1, 1, PB[1], "v", HB[1])
+    relu_h(1, 1, "v")
     for p, k in (("p2", 0), ("p3", 1), ("p4", 2)):
         mm(p, 128, "r2", 128 * k, "H", 0, ["qHa", "qr2%d" % k, "sr2%d" % k])
-    relu("th", 1, 2, PB[2], "a", HB[2])
-    relu("th", 1, 3, PB[3], "v", HB[3])
+    relu_h(1, 2, "a")
+    relu_h(1, 3, "v")
     quant("H", 128, 128, T.th, HB, "qHb")
     for p, k, c in (("p5", 1, 128), ("p6", 2, 128), ("p7", 0, 128), ("p0", 2, 0)):
         mm(p, 256 - c, "r2", 128 * k, "H", c, ["qHa", "qHb", "qr2%d" % k, "sr2%d" % k])
     for t in range(4):
-        plane(T.hp[:, 256 * t:256 * t + 256], T.th[:, t:1024:4], 256, [HA[t], HB[t]], "hp%d" % t)
-    iota("te", [[0, 528]], 0, w="tez")
-    iota("ones", [[0, 128]], 1)
-    select(T.te[:, 3:515:4], T.ones[:, :], [[1, 128]], A.is_equal, 0, -1, ["ones", "tez"], "te")
-    t2, k2 = ranks()
-    list2(T.ch2, "ch2", t2, k2)
-    act(T.Mr[:, :], T.ir[:, 0:528], AF.Identity, ["ir", "no16"], ["Mr"], bias=cc(NO16))
-    pick(64, "Tr2", "sel2", 256, 1.0, 0.0, L2T, "o2", "o2")
+        plane(T.hp[:, 512 * t:512 * t + 512:2], T.tf[:, t:1024:4], 256, [FA[t], FB[t]], "fp%d" % t)
     for t in range(4):
-        gather(T.tg[:, t:512:4], T.hp[:, 256 * t:256 * t + 256], T.o2[:, 64:72], ["hp%d" % t, "o2"], "avav"[t], "tg%d" % t)
+        plane(T.hp[:, 512 * t + 1:512 * t + 512:2], T.th[:, t:1024:4], 256, [HA[t], HB[t]], "hp%d" % t)
+    act(T.cut[:, :], T.ir[:, 0:256], AF.Identity, ["ir"], ["cut1"], scale=0.0, bias=256.0)
+    act(T.E0[:, 8:57:48], T.arow[:, 0:2], AF.Identity, ["E0", "arow"], ["E0a"], scale=0.0, bias=128.0)
+    act(T.E0[:, 24:25], ODD, AF.Identity, ["E0", "lane"], ["E0b"], scale=0.0, bias=-3000.0)
+    act(T.cut[:, 0:256:16], T.ir[:, 0:16], AF.Identity, ["ir", "cut1"], ["cut"], scale=0.0)
+    ranks()
+    list2()
+    select(T.te[:, 3:515:4], T.ones[:, :], [[1, 128]], A.is_equal, 0, -1, ["ones", "tez"], "te")
+    for t in range(4):
+        gather(T.tg[:, t:512:4], T.hp[:, 512 * t:512 * t + 512], T.o2[:, 64:72], ["hp%d" % t, "fp%d" % t] + O2, "avav"[t], "tg%d" % t)
     quant("G", 0, 128, T.tg, four("tg"), "qG")
 
-    far = [d for d in range(N) if d != rank and topo.die(T.cores[d]) != topo.die(core)]
-    near = [d for d in range(N) if d != rank and topo.die(T.cores[d]) == topo.die(core)]
-    masks = {}
-    for lst, o in ((far, 0), (near, 1)):
-        for j, d in enumerate(lst):
-            e = topo.engines(core, T.cores[d])
-            masks[d] = sum(1 << x for x in (e[4 * j + o], e[4 * j + o + 2]))
-    order = sorted(masks, key=lambda d: (d - rank) % N)
+    QUADS = (((0,), (1,), (2,), (3,)), ((0,), (1,), (2,), (3,))), (((0,), (1,), (2, 3)), ((0, 1), (2,), (3,)))
 
-    def swap(a, src0, dst0, sem):
-        tok = "q" + a
-        learn("g", wr[tok])
-        for x in "qs":
+    def send(a, ks, src0, b, dst0, sem, late, r):
+        learn("g", wr[r])
+        n = 0
+        for x, parts in zip("qs", QUADS[late]):
             tr = []
-            for d in order:
-                rid, pid, _ = topo.addr(T.cores[d])
-                i, o = src0 + 16 * ((d - rank - 1) % N), dst0 + 16 * ((rank - d - 1) % N)
-                src, dst = T[x + a][:, i:i + 16], T[x + a][:, o:o + 16]
+            for k, part in zip(ks, parts):
+                d = T.cores[(rank + k + 1) % N]
+                rid, pid, _ = topo.addr(d)
+                e = [z for j in part for z in topo.engines(core, d)[j::4]]
+                n += len(e)
+                i, o = src0 + 16 * k, dst0 + 16 * (N - 2 - k)
+                src, dst = T[x + a][:, i:i + 16], T[x + b][:, o:o + 16]
                 if x == "q":
                     src, dst = codes(src), codes(dst)
-                tr.append(RemoteDMATransfer(dst_ids=[DstId(rid=rid, pnc=pid)], dma_engine_mask=masks[d], remote_sem=T.sem[sem], src=src, dst=dst))
+                tr.append(RemoteDMATransfer(dst_ids=[DstId(rid=rid, pnc=pid)], dma_engine_mask=sum(1 << z for z in e), remote_sem=T.sem[sem], src=src, dst=dst))
             g.remote_dma_fused(tr, local_sem=T.sem.sent)
-        total[sem] = 4 * (N - 1)
-        wr[tok + "r"] = [("far", sem, total[sem], {})]
-        total["sent"] = total.get("sent", 0) + 4 * (N - 1)
-    swap("G", 0, 128, "down")
+        total[sem] = n
+        wr[sem] = [("far", sem, n, {})]
+        total["sent"] = total.get("sent", 0) + n
+    send("G", (3, 4, 5, 6), 0, "G", 128, "down0", 0, "qG")
+    send("G", (0, 1, 2), 0, "G", 128, "down1", 1, "qG")
+    ts(T.o2[:, 72:80], T.o2[:, 64:72], 0.5, A.mult, O2, "o2k", -0.5, A.add)
     for h in range(2):
         cp(T.o1[:, 32 + 8 * h:40 + 8 * h], T.o1[:, 16 * h:16 * h + 8], ["o1%d" % h], "o1c%d" % h)
+    OC = ["o1c0", "o1c1"]
+
+    def times4(t):
+        ts(T.o2[:, 16 * t:16 * t + 8], T.o2[:, 64:72], 2.0, A.mult, O2, "o2_%d" % t, t - 2.0, A.add)
+
+    def unit(b):
+        quant("E", 128 * b, 128, T.te, ["te", "tez"], "qE%d" % b, 3 - b)
+    times4(0)
+    times4(1)
+    ts(T.ph[:, :], T.o1[:, 32:48], 0.0625, A.mult, OC, "ph", -0.46875, A.add)
+    ts(T.pa[:, :], T.o1[:, 32:48], 32.0, A.mult, OC, "pa")
+    times4(2)
+    times4(3)
+    act(T.tt[:, 320:640], T.ir[:, 0:320], AF.Identity, ["ir"], ["ttz"], scale=0.0)
+    act(T.L1r[:, :], T.ir[:, 0:512].indirect(T.o1[:, 32:48]), AF.Identity, ["ir"] + OC, ["L1r"])
     for t in range(4):
-        pick(16 * t, "Tr2", "sel2", 256, 4.0, float(t), L2T, "o2", "o2_%d" % t)
-    act(T.L1r[:, :], T.ir[:, 0:512].indirect(T.o1[:, 32:48]), AF.Identity, ["ir", "o1c0", "o1c1"], ["L1r"])
-    for t in range(4):
-        gather(T.txg[:, 128 * t:128 * t + 128], T.tf[:, :], T.o2[:, 16 * t:16 * t + 8], FA + FB + ["o2_%d" % t], "a", "txg%d" % t)
-    act(T.olr[:, :], T.L1r[:, :].indirect(T.o2[:, 64:72]), AF.Identity, ["L1r", "o2"], ["olr"])
+        gather(T.xi[:, 256 * t:256 * t + 256:2], T.tf[:, :], T.o2[:, 16 * t:16 * t + 8], FA + FB + ["o2_%d" % t], "a", "txg%d" % t)
+    act(T.olr[:, :], T.L1r[:, :].indirect(T.o2[:, 72:80]), AF.Identity, ["L1r", "o2k"], ["olr"])
     turned = 16 * (N - 1 - rank)
+    ts(T.pb[:, :], T.ph[:, :], -511.0, A.mult, ["ph"], "pb")
+    cp(T.M1[:, :].indirect(T.o2[:, 72:80]), T.v3[:, :], ["o2k", "v3"], "M1")
+    tt(T.pc[:, :], T.pa[:, :], T.pb[:, :], A.add, ["pa", "pb"], "pc")
+    unit(0)
+    cp(T.o1[:, 48:64], T.pc[:, :], ["pc"], "o1s")
+    unit(1)
+    cp(T.Mr[:, :].indirect(T.o1[:, 48:64]), T.M1[:, :], ["o1s", "M1"], "Mr")
+    dma("s", T.oMf[:, :], T.Mr[0:128:16, :], r=["Mr"], w=["oMf"])
     dma("s", T.ol[:, 0:128 - turned], T.olr[0:128:16, turned:128], r=["olr"], w=["ol"])
     if turned:
         dma("s", T.ol[:, 128 - turned:128], T.olr[0:128:16, 0:turned], r=["olr"], w=["ol2"])
-    ts(T.o1[:, 48:64], T.o1[:, 32:48], cc(O16), A.add, ["o1c0", "o1c1", "o16"], "o1s")
-    cp(T.M1[:, :].indirect(T.o2[:, 64:72]), T.v3[:, :], ["o2", "v3"], "M1")
-    cp(T.sel3[:, 0:1], T.kt[:, 96:97], ["kt2"], "sel3a")
-    ts(T.sel3[:, 1:2], T.kt[:, 96:97], 256.0, A.add, ["kt2"], "sel3b")
-    quant("E", 0, 128, T.te, ["te", "tez"], "qE0", 3)
-    cp(T.Mr[:, :].indirect(T.o1[:, 48:64]), T.M1[:, :], ["o1s", "M1"], "Mr")
-    for b in range(1, 4):
-        quant("E", 128 * b, 128, T.te, ["te", "tez"], "qE%d" % b, 3 - b)
     for b in range(4):
-        mm(PA[b], 128, "Z", 128 * b, "G", 112, ["qZ", "sZ", "qG", "qGr"])
+        mm(PB[b], 128, "Z", 128 * b, "G", 64, ["qZ", "sZ", "qG", "down0"])
     for b in range(4):
-        relu("tt", 0, b, PA[b], "avav"[b], "tt%d" % b)
-    quant("T", 112, 128, T.tt, four("tt"), "qT", 0)
-    swap("T", 128, 0, "up")
-    turn(T.TrM[:, 0:512], T.Mr[:, 0:512], ["Mr"], "TrMa")
-    turn(T.TrM[:, 512:1024], T.Mr[:, 16:528], ["Mr"], "TrMb")
+        mm(PA[b], 128, "Z", 128 * b, "G", 112, ["qZ", "sZ", "qG", "down0", "down1"])
+    for b in range(4):
+        relu(T.tt[:, b:320:4], T[PB[b]][:, 48:128], PB[b], "avav"[b], "tt%d" % b)
+    quant("T", 112, 128, T.tt, four("tt") + ["ttz"], "qT", 0)
+    send("T", (0, 1, 2, 3), 128, "T", 0, "up0", 0, "qT")
+    for b in range(4):
+        relu(T.tt[:, 640 + b:832:4], T[PA[b]][:, 80:128], PA[b], "aava"[b], "tb%d" % b)
+    quant("B", 0, 128, T.tt, four("tb") + ["ttz"], "qB", 320)
+    send("B", (4, 5, 6), 16, "T", 0, "up1", 1, "qB")
+    unit(2)
+    unit(3)
+    quant("v", 0, 128, T.tv, ["tv"], "qvv")
     for t in range(4):
-        tt(T.wn[:, 896 * t + 512:896 * t + 768], T.tf[:, t:1024:4], T.hp[:, 256 * t:256 * t + 256], A.add, [FA[t], FB[t], "hp%d" % t], "xh%d" % t)
-        if t == 0:
-            cp(T.oM[:, :], T.TrM[:, :].indirect(T.sel3[:, 0:2]), ["TrMa", "TrMb", "sel3a", "sel3b"], "oM")
+        scan(T.wn[:, 1280 * t + 512:1280 * t + 1024], T.alt[:, :], T.hp[:, 512 * t:512 * t + 512], ["alt0", "alt1", "fp%d" % t, "hp%d" % t], "xh%d" % t, 0.0, A.mult, A.add)
+    cp(T.oM[:, :], T.oMf[:, :], ["oMf"], "oM")
     for b in range(4):
-        mm(PA[b], 128, "E", 128 * b, "T", 0, ["qE%d" % b, "qT", "qTr"])
+        mm(PA[b], 128, "E", 128 * b, "T", 0, ["qE%d" % b, "qT", "up0", "up1"])
 
     def hn(b):
-        tt(T.thn[:, 128 * b:128 * b + 128], T[PA[b]][:, 0:128], T.tg[:, b:512:4], A.add, [PA[b], "tg%d" % b], "thn%d" % b)
+        tt(T.xi[:, 256 * b + 1:256 * b + 256:2], T[PA[b]][:, 0:128], T.tg[:, b:512:4], A.add, [PA[b], "tg%d" % b], "thn%d" % b)
 
     def xn(b):
-        tt(T.wn[:, 896 * b + 768:896 * b + 896], T.txg[:, 128 * b:128 * b + 128], T.thn[:, 128 * b:128 * b + 128], A.add, ["txg%d" % b, "thn%d" % b], "xn%d" % b)
+        scan(T.wn[:, 1280 * b + 1024:1280 * b + 1280], T.alt[:, 0:256], T.xi[:, 256 * b:256 * b + 256], ["alt0", "alt1", "txg%d" % b, "thn%d" % b], "xn%d" % b, 0.0, A.mult, A.add)
 
     def back(c, n, t, eng):
-        gather(T.xf[:, 512 * c + t:512 * (c + n):4], T.wn[:, 896 * t:896 * t + 896], T.oM[:, 8 * c:8 * (c + n)],
+        gather(T.xf[:, 512 * c + t:512 * (c + n):4], T.wn[:, 1280 * t:1280 * t + 1280], T.oM[:, 8 * c:8 * (c + n)],
                ["oM", "xp%d" % t, "xh%d" % t, "xn%d" % t], eng, "xf%d%d" % (c, t))
 
     def result(c, r):

from concourse.bass import DstId, RemoteDMATransfer
from concourse.mybir import dt, AluOpType as A, AxisListType, ActivationFunctionType as AF

F8, U8, BF, F32, I32, U16 = "float8_e4m3fn_x4", "uint8", "bfloat16", "float32", "int32", "uint16"
SCRATCH = {}
for _d, _l in (
    (BF, "tu1 512 tu2 512 tv 512 tx 2048 xf 2048 wn 5120 tf 1024 th 1024 hp 2048 tg 512 tt 832 xi 1024 alt 512 uk 256 cut 256 kk 8 sb 8 rep 256 krow 256 "
         "af 256 ltf 256 ltr 256 cum 256 cf 576 cs 288 ones 128 te 528 "
         "val1 256 RS 592 upd 544 sj 512 sk 512 sjv 7424 R1 4896 Tr1 512 mul 448 br 296"),
    (F32, "tbr 128 tbt 128 kr 128 kt 128 arow 8 ar 8 X1 32 C1 32 W2 96 X2 96 crow 8 ft 16 cb 8 ir 1280 tr1 16 P0 128 P1 272 PO 128 c 40 gj 64 l64 32 "
          "sm 64 srow 1024 ch1 32 GE 72 MK 72 sg 32 es2 32 E0 72 E1 72 EO 72 "
          "L1r 256 olr 128 M1 256 v3 128 Mr 512 oMf 32 pa 16 pb 16 pc 16 ysb 512"),
    (I32, "ipick 24 ph 16"),
    (U16, "opick 24 off 2 og 4 osc1 16 o1 64 o2 80 oM 32 sel1 2")):
    _l = _l.split()
    for _i in range(0, len(_l), 2):
        SCRATCH[_l[_i]] = ("sbuf", [128, int(_l[_i + 1])], _d)
for _n, _w in (("W", 512), ("Z", 512), ("x", 512), ("N", 512), ("E", 512), ("F", 256), ("H", 256), ("u1", 128), ("u2", 128), ("r1", 128), ("r2", 384), ("v", 128),
               ("G", 240), ("T", 240), ("B", 128)):
    SCRATCH["q" + _n] = ("sbuf", [128, _w], F8)
    SCRATCH["s" + _n] = ("sbuf", [128, _w], U8)
for _i in range(8):
    SCRATCH["p%d" % _i] = ("psum", [128, 512], F32)
SEMAPHORES = ["qv", "qa", "qt", "qg", "down0", "down1", "up0", "up1", "sent"] + ["d%d" % i for i in range(44)]


def rank_program(g, core, T, topo):
    rank = T.rank_of(core)
    if rank is None:
        return
    N = len(T.cores)
    V, S, P = g.vector, g.scalar, g.tensor
    ENG = {"v": V, "a": S, "t": P, "g": g, "s": g.sync}
    clock = {q: {} for q in ENG}
    total, seen, wr, rd, nd = {}, {}, {}, {}, [0]

    def learn(q, deps):
        want = {}
        for _, s, n, _c in deps:
            want[s] = max(want.get(s, 0), n)
        for s in sorted(want):
            n = want[s]
            if clock[q].get(s, 0) >= n:
                continue
            if any(d[1] != s and want[d[1]] == d[2] and d[3].get(s, 0) >= n for d in deps if clock[q].get(d[1], 0) < d[2]):
                continue
            ENG[q].wait_ge(T.sem[s], n)
            seen[s] = max(seen.get(s, 0), n)
        for d in deps:
            for s, n in list(d[3].items()) + [(d[1], d[2])]:
                clock[q][s] = max(clock[q].get(s, 0), n)

    def deps_of(r, w):
        deps = []
        for t in r:
            deps += wr[t]
        for t in w:
            deps += wr.get(t, []) + rd.get(t, [])
        return deps

    def note(q, s, n, r, w, base):
        e = (q, s, n, dict(base))
        for t in w:
            wr[t], rd[t] = [e], []
        for t in r:
            if t not in w:
                rd.setdefault(t, []).append(e)

    def do(q, fn, *a, r=(), w=(), **k):
        learn(q, deps_of(r, w))
        s = "q" + q
        total[s] = total.get(s, 0) + 1
        fn(*a, **k).then_inc(T.sem[s], 1)
        note(q, s, total[s], r, w, clock[q])

    def dma(q, out, in_, r=(), w=(), **k):
        learn(q, deps_of(r, w))
        s = "d%d" % nd[0]
        nd[0] += 1
        total[s] = 16
        ENG[q].dma_start(out, in_, **k).then_inc(T.sem[s], 16)
        note(q, s, 16, r, w, clock[q])

    def mm(p, n, a, ac, b, bc, r):
        do("t", P.matmul_mx, T[p][:, 0:n], T["q" + a][:, ac:ac + 128], T["s" + a][:, ac:ac + 128], T["q" + b][:, bc:bc + n], T["s" + b][:, bc:bc + n], True, True, r=r, w=[p])

    def quant(q, c, n, t, r, w, tc=None):
        tc = 4 * c if tc is None else tc
        do("v", V.quantize_mx, T["q" + q][:, c:c + n], T["s" + q][:, c:c + n], t[:, tc:tc + 4 * n], r=r, w=[w])

    def ts(out, in0, s1, op0, r, w, s2=None, op1=None):
        do("v", V.tensor_scalar, out, in0, s1, s2, op0, *([] if op1 is None else [op1]), r=r, w=[w])

    def tt(out, a, b, op, r, w):
        do("v", V.tensor_tensor, out, a, b, op, r=r, w=[w])

    def red(out, in_, op, r, w, **k):
        do("v", V.tensor_reduce, out, in_, AxisListType.X, op, r=r, w=[w], **k)

    def scan(out, a, z, r, w, first=0.0, op0=A.add, op1=A.add):
        do("v", V.tensor_tensor_scan, out, a, z, first, op0, op1, r=r, w=[w])

    def turn(out, in_, r, w):
        do("v", V.transpose, out, in_, r=r, w=[w])

    def fill(ap, x, w, r=()):
        do("v", V.memset, ap, x, r=r, w=[w])

    def cp(out, in_, r, w):
        do("v", V.tensor_copy, out, in_, r=r, w=[w])

    def act(out, in_, f, r, w, **k):
        do("a", S.activation, out, in_, f, r=r, w=w, **k)

    def codes(v):
        return v.bitcast(dt.uint8)

    def words(v):
        return v.bitcast(dt.uint32)

    def cc(j):
        return T.c[:, j:j + 1]

    def sm(j):
        return T.sm[:, j:j + 1]

    def four(n):
        return ["%s%d" % (n, t) for t in range(4)]

    dma("s", T.tu1[:, :], T.u1[:, :], w=["tu1"])
    dma("s", T.tx[:, 0:1024], T.x[:, 0:1024], w=["tx0", "tx1"])
    dma("s", T.tx[:, 1024:1536], T.x[:, 1024:1536], w=["tx2"])
    dma("s", T.tx[:, 1536:2048], T.x[:, 1536:2048], w=["tx3"])
    X = four("tx")

    def iota(n, pattern, base, cm=0, at=0, w=None):
        k = 1
        for _s, m in pattern:
            k *= m
        f = {} if SCRATCH[n][2] == I32 else {"allow_small_or_imprecise_dtypes": True}
        do("g", g.iota, T[n][:, at:at + k], pattern, base, cm, w=[w or n], **f)

    def select(out, src, pattern, op, base, cm, r, w):
        do("g", g.affine_select, out, src, pattern, op, 0.0, base, cm, r=r, w=[w])

    def plane(out, src, n, r, w):
        select(out, src, [[0, n]], A.is_ge, 0, 0, r, w)
    iota("ipick", [[16, 8]], 0)
    iota("kr", [[0, 2], [1, 16]], 0, w="kr0")
    iota("kr", [[1, 2], [0, 16]], 0, at=32, w="kr1")
    iota("arow", [[2, 8]], 0)
    iota("ipick", [[16, 2], [32, 4], [0, 2]], 0, at=8, w="ipick2")
    iota("kr", [[0, 2], [32, 4], [128, 2]], 0, at=64, w="kr2")
    iota("kr", [[0, 2], [32, 4], [128, 2]], 16, at=80, w="kr2b")
    iota("tr1", [[1, 16]], 544, 16)
    iota("P1", [[0, 272]], 0, w="P1z")
    iota("ir", [[1, 1280]], 0)
    iota("P0", [[0, 128]], 0, w="P0z")
    iota("MK", [[0, 72]], 1, w="MK1")
    iota("val1", [[2, 16], [32, 16]], -255)
    for t in range(4):
        plane(T.wn[:, 1280 * t:1280 * t + 512], T.tx[:, t:2048:4], 512, X, "xp%d" % t)
    iota("E0", [[0, 72]], 0)
    iota("uk", [[0, 256]], 0)
    iota("E1", [[0, 72]], -5000)
    iota("ones", [[0, 128]], 1)
    iota("Mr", [[1, 16], [16, 32]], 0)

    br = T.br
    fill(T.mul[:, 0:146], 0.5, "mul0")
    fill(T.mul[:, 146:290], 2.0, "mul1")
    fill(T.mul[:, 290:434], 1.0, "mul2")
    fill(T.X1[:, :], 0.0, "X1z")
    scan(br[:, 0:146], T.mul[:, 0:146], T.mul[:, 0:146], ["mul0"], "bn", -2.0 ** 76, A.mult, A.min)
    scan(br[:, 146:290], T.mul[:, 146:290], T.mul[:, 290:434], ["mul1", "mul2"], "bp", 2.0 ** -71, A.mult, A.mult)
    fill(T.C1[:, :], 0.0, "C1z")
    fill(T.W2[:, :], 0.0, "W2z")
    fill(T.ft[:, :], 0.0, "ftz")
    B = ["bn", "bp"]
    for h in range(2):
        cp(T.tbr[:, 16 * h:16 * h + 16], br[:, 17:289:17], B, "tba%d" % h)
        cp(T.tbr[:, 32 + 16 * h:48 + 16 * h], br[:, 137:153], B, "tbb%d" % h)
        act(T.tbr[:, 64 + 16 * h:80 + 16 * h], br[:, 75:91], AF.Identity, B, ["tbc%d" % h], scale=-1.0)
        act(T.tbr[:, 96 + 16 * h:112 + 16 * h], br[:, 201:217], AF.Identity, B, ["tbd%d" % h], scale=-1.0)
    cp(T.opick[:, 0:8], T.ipick[:, 0:8], ["ipick"], "opick")
    turn(T.kt[:, 0:64], T.kr[:, 0:64], ["kr0", "kr1"], "lane")
    turn(T.tbt[:, :], T.tbr[:, :], ["tb%s%d" % (x, h) for x in "abcd" for h in range(2)], "tbt")
    B1, T8, QL, PL = (T.tbt[:, 32 * j:32 * j + 1] for j in range(4))
    LANE, ODD = T.kt[:, 0:1], T.kt[:, 32:33]
    (NB1, LP1, CN, CP, LH, L2, Z12, M8, D6, CB, CB6, L16, Z14, SQ, S0, L64, BE, BR1, BA2, L8, O8, SG, CC, LX, LZ) = range(25)
    W2 = T.W2
    WT = ["W2z"]
    for k, (o, i, s) in enumerate(((W2[:, 0:30:2], br[:, 61:76], -1.0), (W2[:, 30:32], br[:, 75:77], -1.0), (W2[:, 32:48:2], br[:, 69:77], -1.0),
                                   (W2[:, 48:50], br[:, 215:217], 1.0), (W2[:, 51:52], br[:, 76:77], 1.0), (W2[:, 53:64:2], br[:, 215:221], 1.0),
                                   (W2[:, 64:66], br[:, 215:217], 1.0), (W2[:, 67:96:2], br[:, 216:231], 1.0))):
        act(o, i, AF.Identity, B + ["W2z"], ["W2%d" % k], scale=s)
        WT.append("W2%d" % k)
    K17 = 2.0 ** 17 - 1
    ts(cc(Z12), LANE, 0.0, A.is_equal, ["lane"], "z12", 12.0, A.mult)
    ts(cc(Z14), LANE, 15.0, A.is_equal, ["lane"], "z14", 14.0, A.mult)
    ts(cc(NB1), B1, -1.0, A.mult, ["tbt"], "nb1")
    X1T = ["X1" + x for x in "zabcde"]
    quant("u1", 0, 128, T.tu1, ["tu1"], "qu1")
    ts(T.ar[:, :], T.arow[:, :], cc(Z12), A.max, ["arow", "z12", "z14"], "ar", cc(Z14), A.max)
    ts(cc(M8), LANE, 8.0, A.is_ge, ["lane"], "m8", 4.0, A.mult)
    cp(words(T.qr1[:, :]), words(T.qu1[:, :]).indirect(T.opick[:, 0:8]), ["qu1", "opick"], "qr1")

    def lin(out, w, src, k, add, r=()):
        act(out, src, AF.Identity, ["lane"] + list(r), [w], scale=k, bias=add)
    lin(cc(L2), "l2", LANE, 2.0, 0.0)
    lin(T.C1[:, 14:15], "C1a", LANE, 2.0, 0.0, ["C1z"])
    lin(T.C1[:, 15:16], "C1b", LANE, 2.0, 32.0, ["C1z"])
    lin(T.C1[:, 17:18], "C1c", LANE, 0.0, 32.0, ["C1z"])
    lin(cc(CN), "cn", LANE, 0.0625, -1.9375)
    lin(cc(CP), "cp", LANE, 0.0625, 1.0625)
    lin(cc(CB), "cbl", LANE, -0.9375, -0.9375)
    lin(cc(LP1), "lp1", LANE, 1.0, 1.0)
    lin(cc(L16), "l16", LANE, 0.0625, 0.0625)
    lin(T.X2[:, 49:50], "X2c", LANE, 0.0625, -0.4375)
    lin(T.X2[:, 50:51], "X2d", LANE, 0.0, 0.0)
    lin(T.X2[:, 51:52], "X2e", LANE, -0.03125, 0.96875)
    act(T.sr1[:, :], T.su1[:, :].indirect(T.opick[:, 0:8]), AF.Copy, ["qu1", "opick"], ["sr1"])
    act(T.X2[:, 0:49], W2[:, 0:49], AF.Identity, WT + ["cn"], ["X2a"], scale=cc(CN))
    act(T.X2[:, 52:96], W2[:, 52:96], AF.Identity, WT + ["cp"], ["X2b"], scale=cc(CP))
    X2T = ["X2" + x for x in "abcde"]
    act(T.cb[:, 2:4], T.arow[:, 0:2], AF.Identity, ["arow", "cbl"], ["cb1"], scale=0.5, bias=cc(CB))
    act(T.crow[:, 0:5], br[:, 79:96:4], AF.Identity, B, ["crow0"], scale=-1.0)
    act(T.crow[:, 5:6], br[:, 98:99], AF.Identity, B, ["crow1"], scale=-1.0)
    act(T.cb[:, 0:2], T.cb[:, 2:4], AF.Identity, ["cb1"], ["cb0"], scale=0.0625)
    U = 2.0 ** -10

    def gap(k):
        if k < 2:
            p = ("p3", "p4")[k]
            act(T.srow[:, 256 + 128 * k:384 + 128 * k], T[p][:, 0:128], AF.Copy, [p], ["srow%d" % (k + 1), p + "s"])
            if k == 1:
                dma("s", T.ch1[:, :], T.srow[0:128:16, 0:512], r=["srow0", "srow1", "srow2"], w=["ch"])
                dma("s", codes(T.qW[:, :]), T.wc[:, :], w=["qW"])
                dma("s", T.sW[:, :], T.ws[:, :], w=["sW"])
        elif k == 2:
            act(cc(SQ), LANE, AF.Square, ["lane"], ["sq"])
            lin(cc(O8), "o8", ODD, 8.0, 0.0)
            lin(cc(S0), "s0", LANE, -620 * U, 320 * U)
            lin(cc(BE), "be512", LANE, 40.0 * U, -640 * U)
        elif k == 3:
            act(cc(SG), ODD, AF.Identity, ["lane", "s0"], ["sh512"], scale=8 * U, bias=cc(S0))
            act(cc(BR1), cc(SQ), AF.Identity, ["sq", "o8"], ["br512"], scale=20.0, bias=cc(O8))
            lin(cc(L64), "l64", LANE, -40.0, 1240.0)
            lin(cc(BA2), "ba512", LANE, -80.0, 0.0)
        elif k == 4:
            act(cc(CB6), cc(D6), AF.Identity, ["d6"], ["cb6"], scale=-8.0)
            act(cc(CC), cc(BR1), AF.Identity, ["br512"], ["cc"], scale=U, bias=4736 * U)
            act(cc(LX), cc(SG), AF.Identity, ["sh512", "l64"], ["lx"], scale=-1024.0, bias=cc(L64))
            act(T.P1[:, 4:128:8], T.tr1[:, :], AF.Identity, ["tr1", "P1z"], ["P1b"], scale=U / 2)
        elif k == 5:
            act(T.cb[:, 6:8], T.arow[:, 0:2], AF.Identity, ["arow", "cb6"], ["cb3"], scale=0.5, bias=cc(CB6))
            act(T.GE[:, 32:33], cc(SG), AF.Identity, ["sh512"], ["GEz"], bias=-640 * U)
            lin(cc(L8), "l8", LANE, 660.0, -320.0)
        elif k == 6:
            act(T.P1[:, 7:8], cc(SG), AF.Identity, ["sh512", "P1z"], ["P1a"])
            act(T.P1[:, 5:128:8], T.tr1[:, :], AF.Identity, ["tr1", "P1z"], ["P1c"], scale=0.0, bias=U / 2)
            act(cc(LZ), ODD, AF.Identity, ["lane", "l8"], ["lz"], scale=-8.0, bias=cc(L8))

    R = ["qr1", "sr1"]
    for j in range(2):
        quant("x", 128 * j, 128, T.tx, ["tx%d" % j], "qx%d" % j)
    ts(T.X1[:, 19:32:2], br[:, 153:256:17], PL, A.mult, B + ["tbt", "X1z"], "X1a", -2.0 ** 16 * K17, A.mult)
    ts(T.X1[:, 0:14:2], br[:, 34:137:17], QL, A.mult, B + ["tbt", "X1z"], "X1b", 2.0 ** 16 * K17, A.mult)
    for j in range(2, 4):
        quant("x", 128 * j, 128, T.tx, ["tx%d" % j], "qx%d" % j)
    ts(T.X1[:, 17:18], PL, -2.0 ** -47, A.mult, ["tbt", "X1z"], "X1c", T8, A.subtract)
    ts(T.X1[:, 14:15], QL, -2.0 ** -45, A.mult, ["tbt", "X1z"], "X1d")
    cp(T.X1[:, 15:16], T8, ["tbt", "X1z"], "X1e")
    QX = four("qx")
    mm("p2", 256, "r1", 0, "x", 0, QX[0:2] + R)
    mm("p3", 128, "r1", 0, "x", 256, QX[2:3] + R)
    mm("p4", 128, "r1", 0, "x", 384, QX[3:4] + R)
    mm("p0", 384, "r1", 0, "x", 0, QX + R)
    mm("p1", 384, "r1", 0, "x", 128, QX[1:4] + R)
    cp(T.opick[:, 8:24], T.ipick[:, 8:24], ["ipick2"], "opick2")
    turn(T.kt[:, 64:96], T.kr[:, 64:96], ["kr2", "kr2b"], "kt2")
    fill(T.R1[:, 0:272], -1000.0, "R1")

    learn("s", [d for t in X for d in wr[t]])
    dma("s", T.tu2[:, :], T.u2[:, :], w=["tu2"])

    def pick_q(k):
        cp(words(T.qr2[:, 128 * k:128 * k + 128]), words(T.qu2[:, :]).indirect(T.opick[:, 8 * k:8 * k + 8]), ["qu2", "opick", "opick2"], "qr2%d" % k)

    def pick_s(k):
        act(T.sr2[:, 128 * k:128 * k + 128], T.su2[:, :].indirect(T.opick[:, 8 * k:8 * k + 8]), AF.Copy, ["qu2", "opick", "opick2"], ["sr2%d" % k])

    def job(k):
        if k == 0:
            cp(T.srow[:, 0:256], T.p2[:, 0:256], ["p2", "sm1"], "srow0")
        elif k == 2:
            ts(cc(D6), cc(LP1), 0.125, A.mult, ["lp1", "m8"], "d6", cc(M8), A.max)
            fill(T.alt[:, 0:512:2], 0.0, "alt0")
            fill(T.upd[:, 0:544:2], 2.0, "up0")
        elif k == 3:
            ts(T.cb[:, 4:6], T.cb[:, 2:4], cc(D6), A.add, ["cb1", "d6", "l16"], "cb2", cc(L16), A.subtract)
            quant("u2", 0, 128, T.tu2, ["tu2"], "qu2")
        elif k < 7:
            pick_q(k - 4)
        else:
            fill(T.MK[:, 32:33], 0.0, "MK", ["MK1"])
            cp(T.sel1[:, 0:1], T.kt[:, 64:65], ["kt2"], "sel1")
            fill(T.upd[:, 1:544:2], -1.0, "up1")

    def search():
        def count(t, j, tk, p, w, sign=-1.0, buf="sj"):
            act(T[buf][:, 0:w], T[p][:, 0:w], AF.Sign, [p, tk], [buf, "sm%d" % j], scale=sign, bias=t, accum_out=sm(j))

        def flags(t, tk, p, a, b, op=A.is_ge, k=2.0, w=()):
            do("v", V.tensor_scalar, T.sjv[:, 0:b], T[p][:, a:a + b], t, k, op, A.mult, r=[p, tk], w=["fl"] + list(w))

        def total_of(b, first):
            scan(T.sjv[:, 512:512 + b // 2], T.sjv[:, 0:b // 2], T.sjv[:, b // 2:b], ["fl"], "cv", first)
            return T.sjv[:, 511 + b // 2:512 + b // 2]

        def answer(v, vk, j, at, ak, op=A.is_ge):
            ts(T.off[:, 0:1], v, sm(j), op, [vk, "sm%d" % j, ak], "off", at, A.add)

        def gather_sum(tab, n, r, j, **k):
            act(T.gj[:, 0:16], tab[:, 0:n].indirect(T.off[:, 0:1]), AF.Identity, ["off"] + r, ["gj", "sm%d" % j], accum_out=sm(j), **k)
        count(cc(NB1), 0, "nb1", "p2", 256, 1.0, "sk")
        count(cc(NB1), 1, "nb1", "p3", 128, 1.0, "sj")
        count(B1, 2, "tbt", "p4", 128, -1.0, "sk")
        gap(0)
        ts(sm(3), sm(0), sm(1), A.add, ["sm0", "sm1"], "sm3")
        answer(sm(2), "sm2", 3, cc(L2), "l2", A.is_le)
        gather_sum(T.X1, 32, X1T, 4)
        cp(T.l64[:, 16:32], T.C1[:, :].indirect(T.off[:, 0:1]), ["off", "C1a", "C1b", "C1c"], "c16")
        job(0)
        count(sm(4), 5, "sm4", "p0", 384)
        flags(sm(4), "sm4", "p4", 0, 128, w=["p4s"])
        red(sm(9), T.l64[:, 16:32], A.add, ["c16"], "sm9")
        gap(1)
        ts(sm(8), sm(4), QL, A.mult, ["sm4", "tbt"], "sm8", 2.0 ** -69, A.max)
        v = total_of(128, -128.0)
        ts(sm(10), sm(4), PL, A.mult, ["sm4", "sm8", "tbt"], "sm10", sm(8), A.max)
        answer(v, "cv", 5, sm(9), "sm9")
        gather_sum(T.X2, 96, X2T + ["sm10"], 11, scale=sm(10))
        ts(T.l64[:, 0:16], W2[:, :].indirect(T.off[:, 0:1]), sm(10), A.mult, ["off", "sm10"] + WT, "w16")
        fill(T.R1[:, 272:544], -1000.0, "R1z")
        red(sm(12), T.l64[:, 0:16], A.add, ["w16"], "sm12")
        t, tk = sm(11), "sm11"
        b = 152
        for r in range(6):
            def start():
                if r == 0:
                    ts(T.ft[:, 1:12:2], T.crow[:, 0:6], sm(12), A.mult, ["sm12", "crow0", "crow1", "ftz"], "steps")
                    ts(T.ft[:, 12:14], T.cb[:, 0:2], sm(12), A.mult, ["sm12", "cb0", "ftz", tk], "base", t, A.add)
                else:
                    k = max(r - 2, 1)
                    ts(T.ft[:, 12:14], T.cb[:, 2 * k:2 * k + 2], T.ft[:, 2 * r + 1:2 * r + 2], A.mult, ["steps", "cb%d" % k, tk], "base", t, A.add)
            if r < 5:
                count(t, 16 + r, tk, "p0", 512 - b)
                gap(2 + r)
                flags(t, tk, "p1", 384 - b, b)
                start()
                v = total_of(b, -float(b))
            else:
                act(T.sj[:, 0:192], T.p0[:, 0:192], AF.Sign, ["p0", tk], ["sj"], scale=-1.0, bias=t)
                flags(t, tk, "p1", 64, 320, A.is_lt, -1.0)
                act(T.sk[:, 0:192], T.sj[:, 0:192], AF.Relu, ["sj"], ["sk", "sm21"], accum_out=sm(21))
                start()
                v = total_of(320, 256.0)
            answer(v, "cv", 16 + r, T.ar[:, r:r + 1], "ar")
            gather_sum(T.ft, 16, ["steps", "base", "ftz"], 24 + r)
            t, tk = sm(24 + r), "sm%d" % (24 + r)
            job(2 + r)
        return t, tk

    def ranks():
        w = T.srow
        rawe, rawo = T.sjv[:, 4608 + 127:4608 + 1024:128], w[:, 776:784]

        def bound(i):
            k = 512 + 32 * (i % 8) + 16 * (i // 8)
            return w[:, k:k + 1], "tr" + "ab"[i % 8 // 4]

        def flags(i, a=0, b=256):
            return T.sjv[:, 512 + 256 * i + a:512 + 256 * i + b]

        def over(i, p, a, b):
            t, tk = bound(i)
            do("v", V.tensor_scalar, flags(i, a, b), T[p][:, 0:b - a], t, None, A.is_gt, r=[p, tk], w=["fl%d_%d" % (i, a)] + (["cv"] if i == 0 else []))

        def total_v(i):
            k = 4608 + 128 * (i if i < 8 else i - 6)
            scan(T.sjv[:, k:k + 128], flags(i, 0, 128), flags(i, 128, 256), ["fl%d_0" % i] + (["fl%d_128" % i] if i < 8 else []), "sc%d" % i)

        def total_a(i):
            k = 5888 + 256 * (i - 8)
            act(T.sjv[:, k:k + 256], flags(i), AF.Relu, ["fl%d_0" % i, "fl%d_128" % i], ["sc%d" % i], scale=-1.0, accum_out=w[:, 768 + i:769 + i])

        def sign(i, a):
            t, tk = bound(i)
            p = "p6" if a else "p4"
            act(flags(i, a, a + 128), T[p][:, 0:128], AF.Sign, [p, tk], ["fl%d_%d" % (i, a)], scale=-1.0, bias=t)
        turn(w[:, 512:640], T.p2[:, 0:128], ["p2"], "tra")
        for i in range(4):
            over(i, "p3", 0, 128)
        over(0, "p5", 128, 256)
        turn(w[:, 640:768], T.p7[:, 0:128], ["p7"], "trb")
        for i in range(8, 12):
            sign(i, 0)
        for i in range(8, 14):
            if i > 11:
                sign(i, 0)
            sign(i, 128)
            if i > 9:
                total_a(i - 2)
        total_a(12)
        for i in range(1, 4):
            over(i, "p5", 128, 256)
        over(14, "p0", 0, 256)
        over(15, "p0", 0, 256)
        for i in range(4, 8):
            over(i, "p3", 0, 128)
            if i == 5:
                total_v(14)
                total_v(15)
            over(i, "p5", 128, 256)
            if i < 6:
                total_v(2 * i - 8)
                total_v(2 * i - 7)
        act(w[:, 782:784], T.sjv[:, 4608 + 1024 + 127:4608 + 1280:128], AF.Identity, ["sc14", "sc15"], ["rawv"])
        total_a(13)
        for i in range(4, 8):
            total_v(i)
        re_, ro = ["sc%d" % i for i in range(8)], ["rawv"] + ["sc%d" % i for i in range(8, 14)]
        both = ((rawe, re_, 0), (rawo, ro, 1))
        act(w[:, 792:800], rawo, AF.Sign, ro, ["mk1"], scale=-1.0, bias=127.5)
        ts(w[:, 784:792], rawe, 128.0, A.is_lt, re_, "mk0")
        cp(T.uk[:, 0:256:32], rawe, re_ + ["uk"], "uk0")
        act(T.uk[:, 16:256:32], rawo, AF.Identity, ro + ["uk"], ["uk1"])
        act(T.te[:, :], T.ir[:, 0:528], AF.Identity, ["ir"], ["tez"], scale=0.0)
        for raw, rr, h in both[::-1]:
            tt(T.E1[:, 48 * h:48 * h + 8], raw, w[:, 784 + 8 * h:792 + 8 * h], A.mult, rr + ["mk%d" % h, "E1"], "gm%d" % h)
        scan(T.rep[:, :], T.cut[:, :], T.uk[:, :], ["uk0", "uk1", "cut"], "rep", 0.0, A.min, A.add)
        scan(T.EO[:, 0:72], T.E0[:, :], T.E1[:, :], ["gm0", "gm1", "E0a", "E0b", "E1"], "EO", -5000.0, A.add, A.max)
        turn(T.krow[:, :], T.rep[:, :], ["rep"], "krow")
        turn(w[:, 928:992], T.EO[:, 8:72], ["EO"], "bmt")
        ts(T.af[:, :], T.krow[:, :], 128.0, A.is_lt, ["krow"], "af")
        red(T.sb[:, 0:1], w[:, 928:992], A.max, ["bmt"], "sm42")

    def others(out, off, r, j, k, add):
        act(out, T.ir[:, :].indirect(off), AF.Relu, ["ir"] + r, ["gk%d" % j, "sm%d" % j], scale=k, bias=add, accum_out=sm(j))

    def list1(ch, ck, t, tk):
        D1 = T.P1
        ts(T.GE[:, 0:32], ch[:, :], t, A.is_gt, [ck, tk], "gt", U, A.mult)
        ts(T.GE[:, 33:65], ch[:, :], t, A.is_equal, [ck, tk], "eq", U, A.mult)
        act(T.sg[:, 0:32], ch[:, :], AF.Sign, [ck, tk], ["sg"], scale=-1.0, bias=t)
        scan(D1[:, 11:268:4], T.MK[:, 0:65], T.GE[:, 0:65], ["gt", "eq", "MK", "GEz", "sh512", "P1z"], "gs", cc(SG), A.mult, A.add)
        ts(T.og[:, 0:2], D1[:, 135:268:132], 1024.0, A.mult, ["gs", "lx"], "og", cc(LX), A.add)
        ts(T.og[:, 2:3], D1[:, 135:136], 1024.0, A.mult, ["gs", "lz"], "og2", cc(LZ), A.add)
        others(T.gj[:, 16:48], T.og[:, 0:2], ["og", "be512"], 32, U, cc(BE))
        others(T.gj[:, 48:64], T.og[:, 2:3], ["og2", "ba512"], 33, 2.0, cc(BA2))
        tt(T.es2[:, :], D1[:, 139:267:4], T.sg[:, :], A.add, ["gs", "sg"], "es2")
        SM = ["sm32", "cc"]
        fill(T.P0[:, 7:128:8], 1.0, "P0c", ["P0z"])
        ts(T.P0[:, 5:128:8], T.es2[:, 1:32:2], sm(32), A.add, ["es2", "P0z"] + SM, "yo", cc(CC), A.is_ge)
        ts(T.P0[:, 6:128:8], T.es2[:, 0:32:2], sm(32), A.add, ["es2", "P0z"] + SM, "ye", cc(CC), A.is_ge)
        ts(D1[:, 6:128:8], D1[:, 139:267:8], sm(32), A.add, ["gs", "P1z"] + SM, "me", cc(CC), A.min)
        scan(T.PO[:, :], T.P0[:, :], D1[:, 0:128], ["me", "yo", "ye", "gs", "P0c", "P1a", "P1b", "P1c"], "dd", 0.0, A.mult, A.add)
        ts(T.osc1[:, :], T.PO[:, 7:128:8], 2048.0, A.mult, ["dd", "sm33"], "so", sm(33), A.subtract)
        cp(T.R1[:, :].indirect(T.osc1[:, :]), T.val1[:, :], ["so", "val1", "R1z"], "R1")
        scan(T.RS[:, 0:288], T.upd[:, 0:288], T.R1[:, 0:288], ["R1", "up0", "up1"], "RS0", -2000.0, A.add, A.max)
        scan(T.RS[:, 302:592], T.upd[:, 0:290], T.R1[:, 254:544], ["R1", "up0", "up1"], "RS1", -2000.0, A.add, A.max)
        for h in range(2):
            for j in range(2):
                a = 304 * h + 32 * j + 1
                turn(T.Tr1[:, 256 * h + 128 * j:256 * h + 128 * j + 128], T.RS[:, a:a + 255:2], ["RS%d" % h], "R1%d%d" % (h, j))

    def list2():
        ts(T.ltf[:, :], T.krow[:, :], 128.0, A.add, ["krow", "sm42"], "ltf", T.sb[:, 0:1], A.is_lt)
        act(T.sb[:, 2:3], T.sb[:, 0:1], AF.Identity, ["sm42"], ["sm31"], scale=-1.0, bias=256.0)
        act(T.M1[:, :], T.ir[:, 0:256], AF.Identity, ["ir"], ["M1"], scale=2.0, bias=513.0)
        act(T.v3[:, :], T.ir[:, 0:128], AF.Identity, ["ir"], ["v3"], scale=2.0, bias=1025.0)
        scan(T.ltr[:, :], T.ltf[:, :], T.ltf[:, :], ["ltf", "sm31"], "ltr", T.sb[:, 2:3], A.add, A.max)
        scan(T.cum[:, :], T.af[:, :], T.ltr[:, :], ["af", "ltr"], "cum", 0.0, A.add, A.min)
        at = [16 * ((m + rank + 1) % N) for m in range(N)]
        for j in range(4):
            act(T.sjv[:, 144 * j:144 * j + 144], T.cum[:, at[j]:at[j] + 144], AF.Sign, ["cum"] + KK, ["cj%d" % j, "sm%d" % (44 + j)],
                scale=-1.0, bias=T.kk[:, j:j + 1], accum_out=sm(44 + j))
            ts(T.cf[:, 144 * j:144 * j + 144], T.cum[:, at[4 + j]:at[4 + j] + 144], T.kk[:, 4 + j:5 + j], A.is_lt, ["cum"] + KK, "cf%d" % j)
        for j in range(4):
            scan(T.cs[:, 72 * j:72 * j + 72], T.cf[:, 144 * j:144 * j + 72], T.cf[:, 144 * j + 72:144 * j + 144], ["cf%d" % j], "cs%d" % j, float(at[4 + j]))
        for j in range(4):
            if j == 3:
                ts(T.o2[:, 68:72], T.cs[:, 71:288:72], 2.0, A.mult, four("cs"), "o2v", 1.0, A.add)
            ts(T.o2[:, 64 + j:65 + j], sm(44 + j), 2.0 * at[j] + 145.0, A.add, ["sm%d" % (44 + j)], "o2a%d" % j)

    O2 = four("o2a") + ["o2v"]

    def gather(out, win, off, rs, eng, w):
        if eng == "a":
            act(out, win.indirect(off), AF.Copy, rs, [w])
        else:
            cp(out, win.indirect(off), rs, w)

    def relu(o, i, p, eng, w):
        if eng == "a":
            act(o, i, AF.Relu, [p], [w], scale=0.03125)
        else:
            ts(o, i, 0.0, A.max, [p], w, 0.03125, A.mult)

    t1, k1 = search()
    list1(T.ch1, "ch", t1, k1)
    lin(cc(LH), "lh", LANE, 1.0, 0.5)
    pick_s(0)
    KK = ["kk1"]
    if rank < N - 1:
        act(T.kk[:, 0:N - 1 - rank], T.ir[:, 16 * rank + 16:128:16], AF.Identity, ["ir", "lh"], ["kk0"], bias=cc(LH))
        KK.append("kk0")
    act(T.kk[:, N - 1 - rank:N], T.ir[:, 0:16 * rank + 16:16], AF.Identity, ["ir", "lh"], ["kk1"], bias=cc(LH))
    pick_s(1)
    pick_s(2)
    act(T.alt[:, 1:512:2], T.ir[:, 0:256], AF.Identity, ["ir"], ["alt1"], scale=0.0, bias=1.0)
    dma("s", T.tv[:, :], T.v[:, :], w=["tv"])
    dma("s", codes(T.qZ[:, :]), T.zc[:, :], w=["qZ"])
    dma("s", T.sZ[:, :], T.zs[:, :], w=["sZ"])
    for h in range(2):
        ts(T.o1[:, 16 * h:16 * h + 16], T.Tr1[:, 256 * h:256 * h + 256].indirect(T.sel1[:, 0:1]), 256.0, A.add, ["R1%d0" % h, "R1%d1" % h, "sel1"], "o1%d" % h)
    FA, FB, HA, HB = four("tfa"), four("tfb"), four("tha"), four("thb")

    def gather_f(h, t, eng):
        gather(T.tf[:, 512 * h + t:512 * h + 512:4], T.wn[:, 1280 * t:1280 * t + 512], T.o1[:, 16 * h:16 * h + 8], ["xp%d" % t, "o1%d" % h], eng, (FA, FB)[h][t])
    for t in range(4):
        gather_f(0, t, "avav"[t])
    for t in range(3):
        gather_f(1, t, "ava"[t])
    quant("F", 0, 128, T.tf, FA, "qFa")
    gather_f(1, 3, "v")
    quant("F", 128, 128, T.tf, FB, "qFb")
    PA, PB = ["p2", "p3", "p4", "p5"], ["p6", "p7", "p0", "p1"]
    for b in range(4):
        do("t", P.matmul_mx, T[PA[b]][:, 0:128], T.qW[:, 128 * b:128 * b + 128], T.sW[:, 128 * b:128 * b + 128], T.qF[:, 0:128], T.sF[:, 0:128], True, True,
           r=["qW", "sW", "qFa"], w=[PA[b], PA[b] + "s"])
    for b in range(4):
        mm(PB[b], 128, "W", 128 * b, "F", 128, ["qW", "sW", "qFb"])

    def relu_h(h, b, eng):
        p = (PA, PB)[h][b]
        relu(T.th[:, 512 * h + b:512 * h + 512:4], T[p][:, 0:128], p, eng, (HA, HB)[h][b])
    for b in range(4):
        relu_h(0, b, "avav"[b])
    relu_h(1, 0, "a")
    quant("H", 0, 128, T.th, HA, "qHa")
    relu_h(1, 1, "v")
    for p, k in (("p2", 0), ("p3", 1), ("p4", 2)):
        mm(p, 128, "r2", 128 * k, "H", 0, ["qHa", "qr2%d" % k, "sr2%d" % k])
    relu_h(1, 2, "a")
    relu_h(1, 3, "v")
    quant("H", 128, 128, T.th, HB, "qHb")
    for p, k, c in (("p5", 1, 128), ("p6", 2, 128), ("p7", 0, 128), ("p0", 2, 0)):
        mm(p, 256 - c, "r2", 128 * k, "H", c, ["qHa", "qHb", "qr2%d" % k, "sr2%d" % k])
    for t in range(4):
        plane(T.hp[:, 512 * t:512 * t + 512:2], T.tf[:, t:1024:4], 256, [FA[t], FB[t]], "fp%d" % t)
    for t in range(4):
        plane(T.hp[:, 512 * t + 1:512 * t + 512:2], T.th[:, t:1024:4], 256, [HA[t], HB[t]], "hp%d" % t)
    act(T.cut[:, :], T.ir[:, 0:256], AF.Identity, ["ir"], ["cut1"], scale=0.0, bias=256.0)
    act(T.E0[:, 8:57:48], T.arow[:, 0:2], AF.Identity, ["E0", "arow"], ["E0a"], scale=0.0, bias=128.0)
    act(T.E0[:, 24:25], ODD, AF.Identity, ["E0", "lane"], ["E0b"], scale=0.0, bias=-3000.0)
    act(T.cut[:, 0:256:16], T.ir[:, 0:16], AF.Identity, ["ir", "cut1"], ["cut"], scale=0.0)
    ranks()
    list2()
    select(T.te[:, 3:515:4], T.ones[:, :], [[1, 128]], A.is_equal, 0, -1, ["ones", "tez"], "te")
    for t in range(4):
        gather(T.tg[:, t:512:4], T.hp[:, 512 * t:512 * t + 512], T.o2[:, 64:72], ["hp%d" % t, "fp%d" % t] + O2, "avav"[t], "tg%d" % t)
    quant("G", 0, 128, T.tg, four("tg"), "qG")

    QUADS = (((0,), (1,), (2,), (3,)), ((0,), (1,), (2,), (3,))), (((0,), (1,), (2, 3)), ((0, 1), (2,), (3,)))

    def send(a, ks, src0, b, dst0, sem, late, r):
        learn("g", wr[r])
        n = 0
        for x, parts in zip("qs", QUADS[late]):
            tr = []
            for k, part in zip(ks, parts):
                d = T.cores[(rank + k + 1) % N]
                rid, pid, _ = topo.addr(d)
                e = [z for j in part for z in topo.engines(core, d)[j::4]]
                n += len(e)
                i, o = src0 + 16 * k, dst0 + 16 * (N - 2 - k)
                src, dst = T[x + a][:, i:i + 16], T[x + b][:, o:o + 16]
                if x == "q":
                    src, dst = codes(src), codes(dst)
                tr.append(RemoteDMATransfer(dst_ids=[DstId(rid=rid, pnc=pid)], dma_engine_mask=sum(1 << z for z in e), remote_sem=T.sem[sem], src=src, dst=dst))
            g.remote_dma_fused(tr, local_sem=T.sem.sent)
        total[sem] = n
        wr[sem] = [("far", sem, n, {})]
        total["sent"] = total.get("sent", 0) + n
    send("G", (3, 4, 5, 6), 0, "G", 128, "down0", 0, "qG")
    send("G", (0, 1, 2), 0, "G", 128, "down1", 1, "qG")
    ts(T.o2[:, 72:80], T.o2[:, 64:72], 0.5, A.mult, O2, "o2k", -0.5, A.add)
    for h in range(2):
        cp(T.o1[:, 32 + 8 * h:40 + 8 * h], T.o1[:, 16 * h:16 * h + 8], ["o1%d" % h], "o1c%d" % h)
    OC = ["o1c0", "o1c1"]

    def times4(t):
        ts(T.o2[:, 16 * t:16 * t + 8], T.o2[:, 64:72], 2.0, A.mult, O2, "o2_%d" % t, t - 2.0, A.add)

    def unit(b):
        quant("E", 128 * b, 128, T.te, ["te", "tez"], "qE%d" % b, 3 - b)
    times4(0)
    times4(1)
    ts(T.ph[:, :], T.o1[:, 32:48], 0.0625, A.mult, OC, "ph", -0.46875, A.add)
    ts(T.pa[:, :], T.o1[:, 32:48], 32.0, A.mult, OC, "pa")
    times4(2)
    times4(3)
    act(T.tt[:, 320:640], T.ir[:, 0:320], AF.Identity, ["ir"], ["ttz"], scale=0.0)
    act(T.L1r[:, :], T.ir[:, 0:512].indirect(T.o1[:, 32:48]), AF.Identity, ["ir"] + OC, ["L1r"])
    for t in range(4):
        gather(T.xi[:, 256 * t:256 * t + 256:2], T.tf[:, :], T.o2[:, 16 * t:16 * t + 8], FA + FB + ["o2_%d" % t], "a", "txg%d" % t)
    act(T.olr[:, :], T.L1r[:, :].indirect(T.o2[:, 72:80]), AF.Identity, ["L1r", "o2k"], ["olr"])
    turned = 16 * (N - 1 - rank)
    ts(T.pb[:, :], T.ph[:, :], -511.0, A.mult, ["ph"], "pb")
    cp(T.M1[:, :].indirect(T.o2[:, 72:80]), T.v3[:, :], ["o2k", "v3"], "M1")
    tt(T.pc[:, :], T.pa[:, :], T.pb[:, :], A.add, ["pa", "pb"], "pc")
    unit(0)
    cp(T.o1[:, 48:64], T.pc[:, :], ["pc"], "o1s")
    unit(1)
    cp(T.Mr[:, :].indirect(T.o1[:, 48:64]), T.M1[:, :], ["o1s", "M1"], "Mr")
    dma("s", T.oMf[:, :], T.Mr[0:128:16, :], r=["Mr"], w=["oMf"])
    dma("s", T.ol[:, 0:128 - turned], T.olr[0:128:16, turned:128], r=["olr"], w=["ol"])
    if turned:
        dma("s", T.ol[:, 128 - turned:128], T.olr[0:128:16, 0:turned], r=["olr"], w=["ol2"])
    for b in range(4):
        mm(PB[b], 128, "Z", 128 * b, "G", 64, ["qZ", "sZ", "qG", "down0"])
    for b in range(4):
        mm(PA[b], 128, "Z", 128 * b, "G", 112, ["qZ", "sZ", "qG", "down0", "down1"])
    for b in range(4):
        relu(T.tt[:, b:320:4], T[PB[b]][:, 48:128], PB[b], "avav"[b], "tt%d" % b)
    quant("T", 112, 128, T.tt, four("tt") + ["ttz"], "qT", 0)
    send("T", (0, 1, 2, 3), 128, "T", 0, "up0", 0, "qT")
    for b in range(4):
        relu(T.tt[:, 640 + b:832:4], T[PA[b]][:, 80:128], PA[b], "aava"[b], "tb%d" % b)
    quant("B", 0, 128, T.tt, four("tb") + ["ttz"], "qB", 320)
    send("B", (4, 5, 6), 16, "T", 0, "up1", 1, "qB")
    unit(2)
    unit(3)
    quant("v", 0, 128, T.tv, ["tv"], "qvv")
    for t in range(4):
        scan(T.wn[:, 1280 * t + 512:1280 * t + 1024], T.alt[:, :], T.hp[:, 512 * t:512 * t + 512], ["alt0", "alt1", "fp%d" % t, "hp%d" % t], "xh%d" % t, 0.0, A.mult, A.add)
    cp(T.oM[:, :], T.oMf[:, :], ["oMf"], "oM")
    for b in range(4):
        mm(PA[b], 128, "E", 128 * b, "T", 0, ["qE%d" % b, "qT", "up0", "up1"])

    def hn(b):
        tt(T.xi[:, 256 * b + 1:256 * b + 256:2], T[PA[b]][:, 0:128], T.tg[:, b:512:4], A.add, [PA[b], "tg%d" % b], "thn%d" % b)

    def xn(b):
        scan(T.wn[:, 1280 * b + 1024:1280 * b + 1280], T.alt[:, 0:256], T.xi[:, 256 * b:256 * b + 256], ["alt0", "alt1", "txg%d" % b, "thn%d" % b], "xn%d" % b, 0.0, A.mult, A.add)

    def back(c, n, t, eng):
        gather(T.xf[:, 512 * c + t:512 * (c + n):4], T.wn[:, 1280 * t:1280 * t + 1280], T.oM[:, 8 * c:8 * (c + n)],
               ["oM", "xp%d" % t, "xh%d" % t, "xn%d" % t], eng, "xf%d%d" % (c, t))

    def result(c, r):
        quant("N", 128 * c, 128, T.xf, r, "qN%d" % c)
        mm(PB[c], 128, "v", 0, "N", 128 * c, ["qvv", "qN%d" % c])

    def out(c, eng):
        o, i = T.ysb[:, 128 * c:128 * c + 128], T[PB[c]][:, 0:128]
        if eng == "a":
            act(o, i, AF.Copy, [PB[c]], ["y%d" % c])
        else:
            cp(o, i, [PB[c]], "y%d" % c)
    for f, b in ((hn, 0), (hn, 1), (hn, 2), (xn, 0), (hn, 3), (xn, 1), (xn, 2), (xn, 3)):
        f(b)
    for c, n, t, eng in ((0, 2, 0, "a"), (0, 2, 1, "v"), (0, 2, 2, "a"), (0, 2, 3, "v"), (2, 2, 0, "a"), (2, 2, 2, "a"), (3, 1, 1, "a"), (2, 1, 3, "v")):
        back(c, n, t, eng)
    result(0, four("xf0"))
    result(1, four("xf0"))
    dma("s", T.oc[:, 0:1024], codes(T.qN[:, 0:256]), r=["qN0", "qN1"], w=["oc0"])
    back(2, 1, 1, "v")
    back(3, 1, 3, "v")
    out(0, "a")
    out(1, "a")
    dma("a", T.y[:, 0:256], T.ysb[:, 0:256], r=["y0", "y1"], w=["yo0"])
    result(2, four("xf2"))
    result(3, ["xf20", "xf31", "xf22", "xf33"])
    dma("s", T.oc[:, 1024:2048], codes(T.qN[:, 256:512]), r=["qN2", "qN3"], w=["oc1"])
    for j in range(4):
        dma("s", T.osc[4 * j:4 * j + 4, :], T.sN[32 * j:32 * j + 4, :], r=four("qN"), w=["osc%d" % j])
    out(2, "a")
    out(3, "v")
    dma("a", T.y[:, 256:512], T.ysb[:, 256:512], r=["y2", "y3"], w=["yo1"])
    for s in sorted(total, key=lambda s: int(s[1:]) if s[1:].isdigit() else -1):
        if seen.get(s, 0) < total[s]:
            g.wait_ge(T.sem[s], total[s])
